import numpy as np
import ml_dtypes


def mxq(x, axis, fmt="e4m3"):
    dtype, down = {"e4m3": (ml_dtypes.float8_e4m3fn, 7), "e5m2": (ml_dtypes.float8_e5m2, 14)}[fmt]
    v = np.moveaxis(np.asarray(x, np.float32).astype(ml_dtypes.bfloat16).astype(np.float64), axis, -1)
    blocks = v.reshape(v.shape[:-1] + (-1, 32))
    amax = np.abs(blocks).max(-1, keepdims=True)
    byte = np.maximum(np.where(amax > 0, np.frexp(amax)[1] - 1 + 127, 0) - down, 1)
    scale = np.exp2(byte - 127.0)
    codes = (blocks / scale).astype(np.float32).astype(dtype).astype(np.float64)
    return np.moveaxis((codes * scale).reshape(v.shape), -1, axis)


WIDE = False


def mx_kscale(k):
    if not WIDE:
        return np.ones(k)
    levels = np.array([10, -10, 5, -5, 0])
    if k % 512:
        return np.exp2(np.random.permutation(np.resize(levels, k // 32))).repeat(32)
    a = np.empty((k // 512, 16))
    for p in range(k // 512):
        a[p, :8] = np.random.permutation(np.resize(levels, 8))
        for g in range(8):
            far = levels[np.abs(levels - a[p, g]) >= 10]
            a[p, g + 8] = far[np.random.randint(len(far))]
    return np.exp2(a.ravel()).repeat(32)


def f64(x):
    return np.asarray(x).astype(np.float64)


def striped(idx):
    return np.tile(idx.reshape(-1, 16).T, (8, 1)).astype(np.uint16)


def unstriped(offs):
    return offs[:16].T.reshape(-1).astype(np.int64)


def pack_weight(w):
    k, n = w.shape
    w = f64(np.asarray(w, np.float32).astype(ml_dtypes.bfloat16)).reshape(k // 32, 32, n)
    amax = np.abs(w).max(1)
    byte = np.clip(np.where(amax > 0, np.frexp(amax)[1] - 1 + 127 - 7, 1), 1, 254)
    scaled = (w * np.exp2(127.0 - byte)[:, None, :]).reshape(k, n).astype(np.float32)
    words = np.ascontiguousarray(scaled.reshape(k // 512, 128, 4, n).transpose(0, 1, 3, 2)).astype(ml_dtypes.float8_e4m3fn).view(np.uint8)
    return words, np.ascontiguousarray(byte.astype(np.uint8).reshape(k // 512, 16, n))


def unpack_weight(words, scales):
    g, p, n, _ = words.shape
    vals = np.ascontiguousarray(words).view(ml_dtypes.float8_e4m3fn).astype(np.float64) * np.repeat(np.exp2(scales.astype(np.float64) - 127.0), 8, axis=1)[..., None]
    return vals.transpose(0, 1, 3, 2).reshape(g * 512, n)


def relu2(v):
    return np.maximum(v, 0.0) ** 2


K, T, E, C, N = 1024, 512, 16, 128, 256
TOP = 4
M = 512


def by_expert(wq, xq):
    return np.concatenate([wq[e].T @ xq[:, e * C:(e + 1) * C] for e in range(E)], axis=1)


def setup_inputs():
    n = np.random.standard_normal
    s = mx_kscale(K)[:, None]
    deal = np.repeat(np.arange(E), C).reshape(TOP, T)[:, np.random.permutation(T)]
    deal = np.take_along_axis(deal, np.argsort(np.random.rand(TOP, T), axis=0), axis=0)
    for _ in range(8):
        s_, t_ = np.random.permutation(T).reshape(2, -1); r = np.random.randint(TOP, size=T // 2); x, y = deal[r, s_].copy(), deal[r, t_].copy()
        ok = ~((deal[:, s_] == y).any(0) | (deal[:, t_] == x).any(0)); deal[r[ok], s_[ok]] = y[ok]; deal[r[ok], t_[ok]] = x[ok]
    order = np.lexsort((np.random.rand(TOP * T), deal.reshape(-1)))
    slot_token = order % T; pos = np.empty(TOP * T, np.int64); pos[order] = np.arange(TOP * T); pos = pos.reshape(TOP, T)
    g = np.random.uniform(0.5, 1.5, (TOP, T)); g = g / g.sum(0)
    packed = [pack_weight(m) for m in n((E, K, N)) / np.sqrt(K) / s[None]]
    r = mx_kscale(M)[:, None]
    return {
        "uT": (n((M, T)) * r).astype(np.float32),
        "wu": (n((M, K)) / np.sqrt(M) / r * s.T).astype(np.float32),
        "w_words": np.stack([m[0] for m in packed]),
        "w_scales": np.stack([m[1] for m in packed]),
        "b": (0.3 * n((N, E))).astype(np.float32),
        "gate": np.stack([np.tile(r, (N, 1)) for r in g]).astype(np.float32),
        "offs": striped(slot_token),
        "pos1": striped(pos[0]),
        "pos2": striped(pos[1]),
        "pos3": striped(pos[2]),
        "pos4": striped(pos[3]),
    }


def reference(uT, wu, w_words, w_scales, b, gate, offs, pos1, pos2, pos3, pos4):
    idx = unstriped(offs)
    w = np.stack([unpack_weight(w_words[e], w_scales[e]) for e in range(E)])
    x = mxq(f64(wu), 0, "e4m3").T @ mxq(f64(uT), 0, "e4m3")
    xq = mxq(x[:, idx], 0, "e4m3")
    y = by_expert(w, xq)
    y = relu2(y + np.repeat(f64(b), C, axis=1))
    return sum(f64(gate[r]) * y[:, unstriped(p)] for r, p in enumerate((pos1, pos2, pos3, pos4)))

@@ -1,0 +1,236 @@
+from contextlib import ExitStack
+
+import concourse.mybir as mybir
+from concourse.masks import make_identity
+
+F32 = mybir.dt.float32
+BF16 = mybir.dt.bfloat16
+I32 = mybir.dt.int32
+U32 = mybir.dt.uint32
+U16 = mybir.dt.uint16
+U8 = mybir.dt.uint8
+FP8X4 = mybir.dt.float8_e4m3fn_x4
+ACT = mybir.ActivationFunctionType
+ALU = mybir.AluOpType
+
+P = 128
+K, T, E, C, N, M, TOP = 1024, 512, 16, 128, 256, 512, 4
+S = E * C
+PASSES = K // 512
+HALVES = N // P
+TH = T // 2
+WINDOW = 704
+CHUNKS = [(0, 4), (4, 4), (8, 4), (12, 2), (14, 1), (15, 1)]
+FLOPS = 2 * M * K * T + 2 * K * N * S
+
+
+def tile_moe_prv_lin_relu2_kernel(
+    tc, uT, wu, w_words, w_scales, b, gate, offs, pos1, pos2, pos3, pos4, out
+):
+    nc = tc.nc
+    with ExitStack() as ctx:
+        keep = ctx.enter_context(tc.tile_pool(name="keep", bufs=1))
+        ring = ctx.enter_context(tc.tile_pool(name="ring", bufs=3))
+        psum = ctx.enter_context(tc.psum_pool(name="psum", bufs=8))
+
+        offs_t = keep.tile([P, S // 16], U16, name="offs_t")
+        pos_t = [keep.tile([P, T // 16], U16, name="pos_t%d" % r) for r in range(TOP)]
+
+        windows = {}
+        for a in range(PASSES):
+            for u in range(2):
+                windows[a, u] = keep.tile([P, 2 * WINDOW], BF16, name="win%d%d" % (a, u), align_bytes=64)
+                nc.vector.memset(windows[a, u][:, 2 * T :].bitcast(U32), 0)
+        w_plane = keep.tile([P, E * PASSES * N], U8, name="w_plane", align_bytes=64)
+        nc.gpsimd.memset(w_plane[:].bitcast(I32), 0)
+        ident = keep.tile([P, P], F32, name="ident")
+        make_identity(nc, ident[:])
+
+        wu_rows = wu.rearrange("(p j) k -> p j k", j=4)
+        uT_rows = uT.rearrange("(p j) t -> p j t", j=4)
+        wu_raw, u_raw = {}, {}
+
+        def load_wu(a):
+            for s in range(2):
+                wu_raw[a, s] = keep.tile([P, 4, 256], F32, name="wu_raw%d%d" % (a, s))
+                nc.sync.dma_start(wu_raw[a, s][:], wu_rows[:, :, 512 * a + 256 * s : 512 * a + 256 * (s + 1)])
+
+        load_wu(0)
+        for s in range(2):
+            u_raw[s] = keep.tile([P, 4, TH], F32, name="u_raw%d" % s)
+            nc.sync.dma_start(u_raw[s][:], uT_rows[:, :, TH * s : TH * (s + 1)])
+        nc.sync.dma_start(offs_t[:], offs)
+        load_wu(1)
+        scale_rows = w_scales.rearrange("e a q n -> q (e a) n")
+        for q in range(4):
+            nc.sync.dma_start(
+                w_plane[32 * q : 32 * q + 4, :].bitcast(I32).rearrange("p (g n) -> p g n", g=E * PASSES),
+                scale_rows[4 * q : 4 * q + 4].bitcast(I32),
+            )
+        bias = keep.tile([P, HALVES, E], F32, name="bias")
+        nc.sync.dma_start(bias[:], b.rearrange("(h p) e -> p h e", p=P))
+        w_codes = []
+        for g in range(E // 2):
+            wt = keep.tile([P, 2 * PASSES * N * 4], U8, name="w_codes%d" % g, align_bytes=64)
+            nc.sync.dma_start(
+                wt[:].bitcast(I32).rearrange("p (g n) -> p g n", g=2 * PASSES),
+                w_words[2 * g : 2 * g + 2].rearrange("e a p n r -> p (e a) (n r)").bitcast(I32),
+            )
+            w_codes.append(wt)
+        for r, pos in enumerate((pos1, pos2, pos3, pos4)):
+            nc.sync.dma_start(pos_t[r][:], pos)
+        gate_t = []
+        for r in range(TOP):
+            gt = keep.tile([P, HALVES, T], F32, name="gate%d" % r)
+            nc.sync.dma_start(gt[:], gate[r].rearrange("(h p) t -> p h t", p=P))
+            gate_t.append(gt)
+
+        wu_codes, wu_plane, u_codes, u_plane = {}, {}, {}, {}
+
+        def quantize_wu(a, copy):
+            grouped = keep.tile([P, 4, P, 4], BF16, name="wu_bf%d" % a, align_bytes=64)
+            for s in range(2):
+                copy(
+                    grouped[:, :, 64 * s : 64 * (s + 1), :].rearrange("p t m j -> p m j t"),
+                    wu_raw[a, s][:].rearrange("p j (m t) -> p m j t", t=4),
+                )
+            wu_codes[a] = keep.tile([P, 512], U32, name="wu_codes%d" % a, align_bytes=64)
+            wu_plane[a] = keep.tile([P, 512], U8, name="wu_plane%d" % a, align_bytes=64)
+            nc.vector.quantize_mx(
+                wu_codes[a][:].bitcast(FP8X4), wu_plane[a][:], grouped[:].rearrange("p t m j -> p (t m j)")
+            )
+
+        def quantize_u(s, shares):
+            grouped = keep.tile([P, TH, 4], BF16, name="u_bf%d" % s, align_bytes=64)
+            for copy, cols in shares:
+                copy(
+                    grouped[:, cols, :].rearrange("p (c i) j -> p c j i", i=4),
+                    u_raw[s][:, :, cols].rearrange("p j (c i) -> p c j i", i=4),
+                )
+            u_codes[s] = keep.tile([P, TH], U32, name="u_codes%d" % s, align_bytes=64)
+            u_plane[s] = keep.tile([P, TH], U8, name="u_plane%d" % s, align_bytes=64)
+            nc.vector.quantize_mx(
+                u_codes[s][:].bitcast(FP8X4), u_plane[s][:], grouped[:].rearrange("p c j -> p (c j)")
+            )
+
+        def project(a, u, s, copy):
+            bank = psum.tile([P, 2, TH], F32, name="bank", tag="bank")
+            for i in range(2):
+                cols = slice(P * (2 * u + i), P * (2 * u + i + 1))
+                nc.tensor.matmul_mx(
+                    bank[:, i, :],
+                    lhsT=wu_codes[a][:, cols].bitcast(FP8X4),
+                    lhsT_scale=wu_plane[a][:, cols],
+                    rhs=u_codes[s][:].bitcast(FP8X4),
+                    rhs_scale=u_plane[s][:],
+                    start=True,
+                    stop=True,
+                )
+            copy(
+                windows[a, u][:, 2 * TH * s : 2 * TH * (s + 1)].rearrange("p (t i) -> p t i", i=2),
+                bank[:].rearrange("p i t -> p t i"),
+            )
+
+        quantize_wu(0, nc.vector.tensor_copy)
+        quantize_u(0, [(nc.vector.tensor_copy, slice(0, TH))])
+        project(0, 0, 0, nc.scalar.copy)
+        project(0, 1, 0, nc.scalar.copy)
+        quantize_u(1, [(nc.vector.tensor_copy, slice(0, 168)), (nc.scalar.copy, slice(168, TH))])
+        project(0, 0, 1, nc.vector.tensor_copy)
+        project(0, 1, 1, nc.scalar.copy)
+
+        x_codes, x_plane, paired = {}, {}, {}
+
+        def gather(c, a):
+            e0, ne = CHUNKS[c]
+            n = ne * C
+            picked = ring.tile([P, 2, n], U32, name="picked", tag="picked", align_bytes=64)
+            for u in range(2):
+                nc.vector.tensor_copy(
+                    picked[:, u, :], windows[a, u][:].bitcast(U32).indirect(offs_t[:, e0 * C // 16 : (e0 + ne) * C // 16])
+                )
+            paired[c, a] = ring.tile([P, 4 * n], BF16, name="paired", tag="paired", align_bytes=64)
+            copy = nc.vector.tensor_copy if ne == 1 else nc.scalar.copy
+            copy(paired[c, a][:].bitcast(U32).rearrange("p (c u) -> p c u", u=2), picked[:].rearrange("p u c -> p c u"))
+
+        def quantize_x(c, a):
+            n = CHUNKS[c][1] * C
+            x_codes[c, a] = keep.tile([P, n], U32, name="x_codes%d%d" % (c, a), align_bytes=64)
+            x_plane[c, a] = keep.tile([P, n], U8, name="x_plane%d%d" % (c, a), align_bytes=64)
+            nc.vector.quantize_mx(x_codes[c, a][:].bitcast(FP8X4), x_plane[c, a][:], paired[c, a][:])
+
+        y = [keep.tile([P, S], F32, name="y%d" % h) for h in range(HALVES)]
+
+        def experts(c, h):
+            e0, ne = CHUNKS[c]
+            bank = psum.tile([P, ne * C], F32, name="bank", tag="bank")
+            for i in range(ne):
+                e = e0 + i
+                slots = slice(C * i, C * (i + 1))
+                for a in range(PASSES):
+                    word0 = ((e % 2) * PASSES + a) * N + h * P
+                    byte0 = (e * PASSES + a) * N + h * P
+                    nc.tensor.matmul_mx(
+                        bank[:, slots],
+                        lhsT=w_codes[e // 2][:, 4 * word0 : 4 * (word0 + P)].bitcast(FP8X4),
+                        lhsT_scale=w_plane[:, byte0 : byte0 + P],
+                        rhs=x_codes[c, a][:, slots].bitcast(FP8X4),
+                        rhs_scale=x_plane[c, a][:, slots],
+                        start=(a == 0),
+                        stop=(a == PASSES - 1),
+                    )
+            positive = ring.tile([P, ne * C], F32, name="positive", tag="positive")
+            for i in range(ne):
+                slots = slice(C * i, C * (i + 1))
+                nc.scalar.activation(positive[:, slots], bank[:, slots], ACT.Relu, bias=bias[:, h, e0 + i : e0 + i + 1])
+            nc.scalar.activation(y[h][:, e0 * C : (e0 + ne) * C], positive[:], ACT.Square)
+
+        gather(0, 0)
+        quantize_wu(1, nc.scalar.copy)
+        for u in range(2):
+            for s in range(2):
+                project(1, u, s, nc.scalar.copy)
+        order = [(0, 0), (1, 0), (2, 0), (0, 1), (1, 1), (2, 1), (3, 0), (3, 1), (4, 0), (4, 1), (5, 0), (5, 1)]
+        for i, (c, a) in enumerate(order):
+            if i + 1 < len(order):
+                gather(*order[i + 1])
+            quantize_x(c, a)
+            if a == 1:
+                experts(c, 0)
+                if c < 3:
+                    experts(c, 1)
+        for c in range(3, len(CHUNKS)):
+            experts(c, 1)
+
+        prods = {}
+        partial = {}
+
+        def fetch(h, r):
+            prods[h, r] = keep.tile([P, T], F32, name="prod%d%d" % (h, r))
+            nc.vector.tensor_tensor(prods[h, r][:], y[h][:].indirect(pos_t[r][:]), gate_t[r][:, h, :], ALU.mult)
+
+        for h in range(HALVES):
+            turned = [psum.tile([P, P], F32, name="bank", tag="bank") for blk in range(T // P)]
+            for r in range(TOP - 1):
+                fetch(h, r)
+                for blk in range(T // P):
+                    nc.tensor.matmul(
+                        turned[blk][:],
+                        lhsT=prods[h, r][:, P * blk : P * (blk + 1)],
+                        rhs=ident[:],
+                        start=(r == 0),
+                        stop=(r == TOP - 2),
+                        is_transpose=True,
+                    )
+            summed = keep.tile([P, T], F32, name="summed%d" % h)
+            partial[h] = psum.tile([P, T], F32, name="bank", tag="bank")
+            for blk in range(T // P):
+                cols = slice(P * blk, P * (blk + 1))
+                nc.scalar.copy(summed[:, cols], turned[blk][:])
+                nc.tensor.transpose(partial[h][:, cols], summed[:, cols], ident[:])
+        for h in range(HALVES):
+            fetch(h, TOP - 1)
+        for h in range(HALVES):
+            result = keep.tile([P, T], F32, name="result%d" % h)
+            nc.vector.tensor_tensor(result[:], partial[h][:], prods[h, TOP - 1][:], ALU.add)
+            nc.sync.dma_start(out[P * h : P * (h + 1), :], result[:])

@@ -85,27 +85,28 @@ def tile_moe_prv_lin_relu2_kernel(
             nc.sync.dma_start(gt[:], gate[r].rearrange("(h p) t -> p h t", p=P))
             gate_t.append(gt)
 
-        wu_codes, wu_plane, u_codes, u_plane = {}, {}, {}, {}
+        wu_bf, wu_codes, wu_plane, u_codes, u_plane = {}, {}, {}, {}, {}
 
         def quantize_wu(a, copy):
-            grouped = keep.tile([P, 4, P, 4], BF16, name="wu_bf%d" % a, align_bytes=64)
+            wu_bf[a] = keep.tile([P, 4 * 512], BF16, name="wu_bf%d" % a, align_bytes=64)
+            grouped = wu_bf[a][:].rearrange("p (t m j) -> p t m j", t=4, j=4)
             for s in range(2):
                 copy(
-                    grouped[:, :, 64 * s : 64 * (s + 1), :].rearrange("p t m j -> p m j t"),
-                    wu_raw[a, s][:].rearrange("p j (m t) -> p m j t", t=4),
+                    grouped[:, :, 64 * s : 64 * (s + 1), :].rearrange("p t m j -> p m t j"),
+                    wu_raw[a, s][:].rearrange("p j (m t) -> p m t j", t=4),
                 )
             wu_codes[a] = keep.tile([P, 512], U32, name="wu_codes%d" % a, align_bytes=64)
             wu_plane[a] = keep.tile([P, 512], U8, name="wu_plane%d" % a, align_bytes=64)
             nc.vector.quantize_mx(
-                wu_codes[a][:].bitcast(FP8X4), wu_plane[a][:], grouped[:].rearrange("p t m j -> p (t m j)")
+                wu_codes[a][:].bitcast(FP8X4), wu_plane[a][:], wu_bf[a][:]
             )
 
         def quantize_u(s, shares):
             grouped = keep.tile([P, TH, 4], BF16, name="u_bf%d" % s, align_bytes=64)
             for copy, cols in shares:
                 copy(
-                    grouped[:, cols, :].rearrange("p (c i) j -> p c j i", i=4),
-                    u_raw[s][:, :, cols].rearrange("p j (c i) -> p c j i", i=4),
+                    grouped[:, cols, :],
+                    u_raw[s][:, :, cols].rearrange("p j c -> p c j"),
                 )
             u_codes[s] = keep.tile([P, TH], U32, name="u_codes%d" % s, align_bytes=64)
             u_plane[s] = keep.tile([P, TH], U8, name="u_plane%d" % s, align_bytes=64)
@@ -139,25 +140,37 @@ def tile_moe_prv_lin_relu2_kernel(
         project(0, 0, 1, nc.vector.tensor_copy)
         project(0, 1, 1, nc.scalar.copy)
 
-        x_codes, x_plane, paired = {}, {}, {}
+        order = [(0, 0), (1, 0), (0, 1), (1, 1), (2, 0), (2, 1), (3, 0), (3, 1), (4, 0), (4, 1), (5, 0), (5, 1)]
+        x_codes, x_plane, paired, picked = {}, {}, {}, {}
 
         def gather(c, a):
             e0, ne = CHUNKS[c]
             n = ne * C
-            picked = ring.tile([P, 2, n], U32, name="picked", tag="picked", align_bytes=64)
+            if ne == 1:
+                paired[c, a] = wu_bf[a][:, 4 * n * (e0 % 2) : 4 * n * (e0 % 2 + 1)]
+                picked[c, a] = paired[c, a].bitcast(U32).rearrange("p (c u) -> p u c", u=2)
+            else:
+                picked[c, a] = wu_bf[order.index((c, a)) % 2][:, : 4 * n].bitcast(U32).rearrange("p (u c) -> p u c", u=2)
             for u in range(2):
                 nc.vector.tensor_copy(
-                    picked[:, u, :], windows[a, u][:].bitcast(U32).indirect(offs_t[:, e0 * C // 16 : (e0 + ne) * C // 16])
+                    picked[c, a][:, u, :], windows[a, u][:].bitcast(U32).indirect(offs_t[:, e0 * C // 16 : (e0 + ne) * C // 16])
                 )
-            paired[c, a] = ring.tile([P, 4 * n], BF16, name="paired", tag="paired", align_bytes=64)
-            copy = nc.vector.tensor_copy if ne == 1 else nc.scalar.copy
-            copy(paired[c, a][:].bitcast(U32).rearrange("p (c u) -> p c u", u=2), picked[:].rearrange("p u c -> p c u"))
+
+        def pair(c, a):
+            ne = CHUNKS[c][1]
+            n = ne * C
+            if ne > 1:
+                both = ring.tile([P, 4 * n], BF16, name="paired", tag="paired", align_bytes=64)
+                paired[c, a] = both[:]
+                nc.scalar.copy(
+                    paired[c, a].bitcast(U32).rearrange("p (c u) -> p c u", u=2), picked[c, a].rearrange("p u c -> p c u")
+                )
 
         def quantize_x(c, a):
             n = CHUNKS[c][1] * C
             x_codes[c, a] = keep.tile([P, n], U32, name="x_codes%d%d" % (c, a), align_bytes=64)
             x_plane[c, a] = keep.tile([P, n], U8, name="x_plane%d%d" % (c, a), align_bytes=64)
-            nc.vector.quantize_mx(x_codes[c, a][:].bitcast(FP8X4), x_plane[c, a][:], paired[c, a][:])
+            nc.vector.quantize_mx(x_codes[c, a][:].bitcast(FP8X4), x_plane[c, a][:], paired[c, a])
 
         y = [keep.tile([P, S], F32, name="y%d" % h) for h in range(HALVES)]
 
@@ -179,7 +192,7 @@ def tile_moe_prv_lin_relu2_kernel(
                         start=(a == 0),
                         stop=(a == PASSES - 1),
                     )
-            positive = ring.tile([P, ne * C], F32, name="positive", tag="positive")
+            positive = ring.tile([P, ne * C], F32, name="positive", tag="positive%d" % h)
             for i in range(ne):
                 slots = slice(C * i, C * (i + 1))
                 nc.scalar.activation(positive[:, slots], bank[:, slots], ACT.Relu, bias=bias[:, h, e0 + i : e0 + i + 1])
@@ -190,8 +203,8 @@ def tile_moe_prv_lin_relu2_kernel(
         for u in range(2):
             for s in range(2):
                 project(1, u, s, nc.scalar.copy)
-        order = [(0, 0), (1, 0), (2, 0), (0, 1), (1, 1), (2, 1), (3, 0), (3, 1), (4, 0), (4, 1), (5, 0), (5, 1)]
         for i, (c, a) in enumerate(order):
+            pair(c, a)
             if i + 1 < len(order):
                 gather(*order[i + 1])
             quantize_x(c, a)
@@ -230,7 +243,7 @@ def tile_moe_prv_lin_relu2_kernel(
                 nc.tensor.transpose(partial[h][:, cols], summed[:, cols], ident[:])
         for h in range(HALVES):
             fetch(h, TOP - 1)
-        for h in range(HALVES):
-            result = keep.tile([P, T], F32, name="result%d" % h)
-            nc.vector.tensor_tensor(result[:], partial[h][:], prods[h, TOP - 1][:], ALU.add)
-            nc.sync.dma_start(out[P * h : P * (h + 1), :], result[:])
+        for h, cols in ((0, slice(0, T)), (1, slice(0, TH)), (1, slice(TH, T))):
+            result = keep.tile([P, cols.stop - cols.start], F32, name="result%d_%d" % (h, cols.start))
+            nc.vector.tensor_tensor(result[:], partial[h][:, cols], prods[h, TOP - 1][:, cols], ALU.add)
+            nc.sync.dma_start(out[P * h : P * (h + 1), cols], result[:])

@@ -20,6 +20,7 @@ PASSES = K // 512
 HALVES = N // P
 TH = T // 2
 WINDOW = 704
+PIECES = [(0, 256), (256, 128), (384, 128)]
 CHUNKS = [(0, 4), (4, 4), (8, 4), (12, 2), (14, 1), (15, 1)]
 FLOPS = 2 * M * K * T + 2 * K * N * S
 
@@ -56,9 +57,9 @@ def tile_moe_prv_lin_relu2_kernel(
                 nc.sync.dma_start(wu_raw[a, s][:], wu_rows[:, :, 512 * a + 256 * s : 512 * a + 256 * (s + 1)])
 
         load_wu(0)
-        for s in range(2):
-            u_raw[s] = keep.tile([P, 4, TH], F32, name="u_raw%d" % s)
-            nc.sync.dma_start(u_raw[s][:], uT_rows[:, :, TH * s : TH * (s + 1)])
+        for s, (t0, nt) in enumerate(PIECES):
+            u_raw[s] = keep.tile([P, 4, nt], F32, name="u_raw%d" % s)
+            nc.sync.dma_start(u_raw[s][:], uT_rows[:, :, t0 : t0 + nt])
         nc.sync.dma_start(offs_t[:], offs)
         load_wu(1)
         scale_rows = w_scales.rearrange("e a q n -> q (e a) n")
@@ -79,16 +80,16 @@ def tile_moe_prv_lin_relu2_kernel(
             w_codes.append(wt)
         for r, pos in enumerate((pos1, pos2, pos3, pos4)):
             nc.sync.dma_start(pos_t[r][:], pos)
-        gate_t = []
-        for r in range(TOP):
-            gt = keep.tile([P, HALVES, T], F32, name="gate%d" % r)
-            nc.sync.dma_start(gt[:], gate[r].rearrange("(h p) t -> p h t", p=P))
-            gate_t.append(gt)
+        gate_t = {}
+        for h in range(HALVES):
+            for r in range(TOP):
+                gate_t[h, r] = keep.tile([P, T], F32, name="gate%d%d" % (h, r))
+                nc.sync.dma_start(gate_t[h, r][:], gate[r, P * h : P * (h + 1), :])
 
-        wu_bf, wu_codes, wu_plane, u_codes, u_plane = {}, {}, {}, {}, {}
+        wu_codes, wu_plane = {}, {}
+        wu_bf = [keep.tile([P, 4 * 512], BF16, name="wu_bf%d" % a, align_bytes=64) for a in range(PASSES)]
 
         def quantize_wu(a, copy):
-            wu_bf[a] = keep.tile([P, 4 * 512], BF16, name="wu_bf%d" % a, align_bytes=64)
             grouped = wu_bf[a][:].rearrange("p (t m j) -> p t m j", t=4, j=4)
             for s in range(2):
                 copy(
@@ -101,47 +102,50 @@ def tile_moe_prv_lin_relu2_kernel(
                 wu_codes[a][:].bitcast(FP8X4), wu_plane[a][:], wu_bf[a][:]
             )
 
-        def quantize_u(s, shares):
-            grouped = keep.tile([P, TH, 4], BF16, name="u_bf%d" % s, align_bytes=64)
-            for copy, cols in shares:
-                copy(
-                    grouped[:, cols, :],
-                    u_raw[s][:, :, cols].rearrange("p j c -> p c j"),
-                )
-            u_codes[s] = keep.tile([P, TH], U32, name="u_codes%d" % s, align_bytes=64)
-            u_plane[s] = keep.tile([P, TH], U8, name="u_plane%d" % s, align_bytes=64)
+        u_codes = keep.tile([P, T], U32, name="u_codes", align_bytes=64)
+        u_plane = keep.tile([P, T], U8, name="u_plane", align_bytes=64)
+
+        def quantize_u(s):
+            t0, nt = PIECES[s]
+            grouped = wu_bf[1][:, 4 * t0 : 4 * (t0 + nt)]
+            nc.vector.tensor_copy(grouped.rearrange("p (c j) -> p c j", j=4), u_raw[s][:].rearrange("p j c -> p c j"))
             nc.vector.quantize_mx(
-                u_codes[s][:].bitcast(FP8X4), u_plane[s][:], grouped[:].rearrange("p c j -> p (c j)")
+                u_codes[:, t0 : t0 + nt].bitcast(FP8X4), u_plane[:, t0 : t0 + nt], grouped
             )
 
-        def project(a, u, s, copy):
-            bank = psum.tile([P, 2, TH], F32, name="bank", tag="bank")
+        def project(a, u, t0, nt, copy):
+            bank = psum.tile([P, 2, nt], F32, name="bank", tag="bank")
             for i in range(2):
                 cols = slice(P * (2 * u + i), P * (2 * u + i + 1))
                 nc.tensor.matmul_mx(
                     bank[:, i, :],
                     lhsT=wu_codes[a][:, cols].bitcast(FP8X4),
                     lhsT_scale=wu_plane[a][:, cols],
-                    rhs=u_codes[s][:].bitcast(FP8X4),
-                    rhs_scale=u_plane[s][:],
+                    rhs=u_codes[:, t0 : t0 + nt].bitcast(FP8X4),
+                    rhs_scale=u_plane[:, t0 : t0 + nt],
                     start=True,
                     stop=True,
                 )
             copy(
-                windows[a, u][:, 2 * TH * s : 2 * TH * (s + 1)].rearrange("p (t i) -> p t i", i=2),
+                windows[a, u][:, 2 * t0 : 2 * (t0 + nt)].rearrange("p (t i) -> p t i", i=2),
                 bank[:].rearrange("p i t -> p t i"),
             )
 
         quantize_wu(0, nc.vector.tensor_copy)
-        quantize_u(0, [(nc.vector.tensor_copy, slice(0, TH))])
-        project(0, 0, 0, nc.scalar.copy)
-        project(0, 1, 0, nc.scalar.copy)
-        quantize_u(1, [(nc.vector.tensor_copy, slice(0, 168)), (nc.scalar.copy, slice(168, TH))])
-        project(0, 0, 1, nc.vector.tensor_copy)
-        project(0, 1, 1, nc.scalar.copy)
+        quantize_u(0)
+        project(0, 0, 0, 256, nc.scalar.copy)
+        project(0, 1, 0, 256, nc.scalar.copy)
+        quantize_u(1)
+        quantize_u(2)
+        project(0, 0, 256, 128, nc.vector.tensor_copy)
+        project(0, 0, 384, 128, nc.vector.tensor_copy)
+        project(0, 1, 256, 256, nc.scalar.copy)
 
         order = [(0, 0), (1, 0), (0, 1), (1, 1), (2, 0), (2, 1), (3, 0), (3, 1), (4, 0), (4, 1), (5, 0), (5, 1)]
         x_codes, x_plane, paired, picked = {}, {}, {}, {}
+
+        spare = [keep.tile([P, 4 * 512], BF16, name="spare%d" % i, align_bytes=64) for i in range(2)]
+        positive = {}
 
         def gather(c, a):
             e0, ne = CHUNKS[c]
@@ -160,7 +164,10 @@ def tile_moe_prv_lin_relu2_kernel(
             ne = CHUNKS[c][1]
             n = ne * C
             if ne > 1:
-                both = ring.tile([P, 4 * n], BF16, name="paired", tag="paired", align_bytes=64)
+                if c == 2:
+                    both = spare[a]
+                else:
+                    both = ring.tile([P, 4 * n], BF16, name="paired", tag="paired", align_bytes=64)
                 paired[c, a] = both[:]
                 nc.scalar.copy(
                     paired[c, a].bitcast(U32).rearrange("p (c u) -> p c u", u=2), picked[c, a].rearrange("p u c -> p c u")
@@ -174,12 +181,17 @@ def tile_moe_prv_lin_relu2_kernel(
 
         y = [keep.tile([P, S], F32, name="y%d" % h) for h in range(HALVES)]
 
+        chunk_of = {e: c for c, (e0, ne) in enumerate(CHUNKS) for e in range(e0, e0 + ne)}
+        groups = CHUNKS + [(12, 4)]
+
         def experts(c, h):
-            e0, ne = CHUNKS[c]
+            e0, ne = groups[c]
             bank = psum.tile([P, ne * C], F32, name="bank", tag="bank")
             for i in range(ne):
                 e = e0 + i
                 slots = slice(C * i, C * (i + 1))
+                home = chunk_of[e]
+                own = slice(C * (e - CHUNKS[home][0]), C * (e - CHUNKS[home][0] + 1))
                 for a in range(PASSES):
                     word0 = ((e % 2) * PASSES + a) * N + h * P
                     byte0 = (e * PASSES + a) * N + h * P
@@ -187,63 +199,98 @@ def tile_moe_prv_lin_relu2_kernel(
                         bank[:, slots],
                         lhsT=w_codes[e // 2][:, 4 * word0 : 4 * (word0 + P)].bitcast(FP8X4),
                         lhsT_scale=w_plane[:, byte0 : byte0 + P],
-                        rhs=x_codes[c, a][:, slots].bitcast(FP8X4),
-                        rhs_scale=x_plane[c, a][:, slots],
+                        rhs=x_codes[home, a][:, own].bitcast(FP8X4),
+                        rhs_scale=x_plane[home, a][:, own],
                         start=(a == 0),
                         stop=(a == PASSES - 1),
                     )
-            positive = ring.tile([P, ne * C], F32, name="positive", tag="positive%d" % h)
+            if c == 0:
+                positive[c, h] = spare[h][:, : 2 * ne * C].bitcast(F32)
+            else:
+                fresh = ring.tile([P, ne * C], F32, name="fresh", tag="positive%d" % h)
+                positive[c, h] = fresh[:]
             for i in range(ne):
                 slots = slice(C * i, C * (i + 1))
-                nc.scalar.activation(positive[:, slots], bank[:, slots], ACT.Relu, bias=bias[:, h, e0 + i : e0 + i + 1])
-            nc.scalar.activation(y[h][:, e0 * C : (e0 + ne) * C], positive[:], ACT.Square)
+                nc.scalar.activation(
+                    positive[c, h][:, slots], bank[:, slots], ACT.Relu, bias=bias[:, h, e0 + i : e0 + i + 1]
+                )
+
+        def square(c, h):
+            e0, ne = groups[c]
+            nc.scalar.activation(y[h][:, e0 * C : (e0 + ne) * C], positive[c, h], ACT.Square)
 
         gather(0, 0)
         quantize_wu(1, nc.scalar.copy)
         for u in range(2):
             for s in range(2):
-                project(1, u, s, nc.scalar.copy)
-        for i, (c, a) in enumerate(order):
-            pair(c, a)
-            if i + 1 < len(order):
-                gather(*order[i + 1])
-            quantize_x(c, a)
-            if a == 1:
-                experts(c, 0)
-                if c < 3:
-                    experts(c, 1)
-        for c in range(3, len(CHUNKS)):
-            experts(c, 1)
+                project(1, u, TH * s, TH, nc.scalar.copy)
+        steps = [
+            (pair, 0, 0), (gather, 1, 0), (quantize_x, 0, 0),
+            (pair, 1, 0), (gather, 0, 1), (quantize_x, 1, 0),
+            (pair, 0, 1), (gather, 1, 1), (quantize_x, 0, 1),
+            (pair, 1, 1), (gather, 2, 0), (quantize_x, 1, 1),
+            (experts, 0, 0), (square, 0, 0), (experts, 0, 1),
+            (pair, 2, 0), (gather, 2, 1), (quantize_x, 2, 0),
+            (square, 0, 1), (experts, 1, 0),
+            (pair, 2, 1), (gather, 3, 0), (quantize_x, 2, 1),
+            (square, 1, 0),
+            (pair, 3, 0), (gather, 3, 1), (quantize_x, 3, 0),
+            (experts, 1, 1),
+            (pair, 3, 1), (gather, 4, 0), (quantize_x, 3, 1),
+            (gather, 4, 1), (quantize_x, 4, 0), (gather, 5, 0), (quantize_x, 4, 1),
+            (gather, 5, 1), (quantize_x, 5, 0), (quantize_x, 5, 1),
+            (experts, 2, 0), (square, 1, 1), (square, 2, 0),
+        ]
+        steps += [(step, c, 0) for c in (3, 4, 5) for step in (experts, square)]
+        steps += [(step, c, 1) for c in (2, 6) for step in (experts, square)]
+        for step, c, i in steps:
+            step(c, i)
 
-        prods = {}
-        partial = {}
+        def fetch(h, r, cols):
+            prod = keep.tile([P, cols.stop - cols.start], F32, name="prod%d%d_%d" % (h, r, cols.start))
+            nc.vector.tensor_tensor(
+                prod[:], y[h][:].indirect(pos_t[r][:, cols.start // 16 : cols.stop // 16]), gate_t[h, r][:, cols], ALU.mult
+            )
+            return prod
 
-        def fetch(h, r):
-            prods[h, r] = keep.tile([P, T], F32, name="prod%d%d" % (h, r))
-            nc.vector.tensor_tensor(prods[h, r][:], y[h][:].indirect(pos_t[r][:]), gate_t[r][:, h, :], ALU.mult)
+        def turn(turned, prod, blk0, start, stop):
+            for i in range(prod.shape[1] // P):
+                nc.tensor.matmul(
+                    turned[blk0 + i][:],
+                    lhsT=prod[:, P * i : P * (i + 1)],
+                    rhs=ident[:],
+                    start=start,
+                    stop=stop,
+                    is_transpose=True,
+                )
 
-        for h in range(HALVES):
-            turned = [psum.tile([P, P], F32, name="bank", tag="bank") for blk in range(T // P)]
-            for r in range(TOP - 1):
-                fetch(h, r)
-                for blk in range(T // P):
-                    nc.tensor.matmul(
-                        turned[blk][:],
-                        lhsT=prods[h, r][:, P * blk : P * (blk + 1)],
-                        rhs=ident[:],
-                        start=(r == 0),
-                        stop=(r == TOP - 2),
-                        is_transpose=True,
-                    )
-            summed = keep.tile([P, T], F32, name="summed%d" % h)
-            partial[h] = psum.tile([P, T], F32, name="bank", tag="bank")
-            for blk in range(T // P):
-                cols = slice(P * blk, P * (blk + 1))
-                nc.scalar.copy(summed[:, cols], turned[blk][:])
-                nc.tensor.transpose(partial[h][:, cols], summed[:, cols], ident[:])
-        for h in range(HALVES):
-            fetch(h, TOP - 1)
-        for h, cols in ((0, slice(0, T)), (1, slice(0, TH)), (1, slice(TH, T))):
-            result = keep.tile([P, cols.stop - cols.start], F32, name="result%d_%d" % (h, cols.start))
-            nc.vector.tensor_tensor(result[:], partial[h][:, cols], prods[h, TOP - 1][:, cols], ALU.add)
-            nc.sync.dma_start(out[P * h : P * (h + 1), cols], result[:])
+        def turn_back(turned, name):
+            summed = keep.tile([P, len(turned) * P], F32, name=name)
+            back = psum.tile([P, len(turned) * P], F32, name="bank", tag="bank")
+            for i, block in enumerate(turned):
+                cols = slice(P * i, P * (i + 1))
+                nc.scalar.copy(summed[:, cols], block[:])
+                nc.tensor.transpose(back[:, cols], summed[:, cols], ident[:])
+            return back
+
+        whole = slice(0, T)
+        halves = [slice(0, TH), slice(TH, T)]
+        turned = [psum.tile([P, P], F32, name="bank", tag="bank") for blk in range(T // P)]
+        for r in range(TOP):
+            turn(turned, fetch(0, r, whole), 0, r == 0, r == TOP - 1)
+        back = turn_back(turned, "summed0")
+        result = keep.tile([P, T], F32, name="result0")
+        nc.scalar.copy(result[:], back[:])
+        nc.sync.dma_start(out[:P, :], result[:])
+
+        for r in range(TOP - 2):
+            turn(turned, fetch(1, r, whole), 0, r == 0, False)
+        partial = []
+        for s, cols in enumerate(halves):
+            turn(turned, fetch(1, TOP - 2, cols), 2 * s, False, True)
+            partial.append(turn_back(turned[2 * s : 2 * s + 2], "summed1%d" % s))
+        last = [fetch(1, TOP - 1, cols) for cols in halves]
+        for s, cols in enumerate(halves):
+            result = keep.tile([P, TH], F32, name="result1%d" % s)
+            nc.vector.tensor_tensor(result[:], partial[s][:], last[s][:], ALU.add)
+            nc.sync.dma_start(out[P:, cols], result[:])

@@ -21,7 +21,7 @@ HALVES = N // P
 TH = T // 2
 WINDOW = 704
 PIECES = [(0, 256), (256, 128), (384, 128)]
-CHUNKS = [(0, 4), (4, 4), (8, 4), (12, 2), (14, 1), (15, 1)]
+UNITS = [(0, 0, 4), (0, 4, 4), (1, 0, 4), (1, 4, 4), (0, 8, 4), (1, 8, 4), (0, 12, 4), (1, 12, 2), (1, 14, 1), (1, 15, 1)]
 FLOPS = 2 * M * K * T + 2 * K * N * S
 
 
@@ -141,110 +141,91 @@ def tile_moe_prv_lin_relu2_kernel(
         project(0, 0, 384, 128, nc.vector.tensor_copy)
         project(0, 1, 256, 256, nc.scalar.copy)
 
-        order = [(0, 0), (1, 0), (0, 1), (1, 1), (2, 0), (2, 1), (3, 0), (3, 1), (4, 0), (4, 1), (5, 0), (5, 1)]
-        x_codes, x_plane, paired, picked = {}, {}, {}, {}
-
+        x_codes, x_plane, paired, picked, positive = {}, {}, {}, {}, {}
         spare = [keep.tile([P, 4 * 512], BF16, name="spare%d" % i, align_bytes=64) for i in range(2)]
-        positive = {}
+        last_unit = len(UNITS) - 1
 
-        def gather(c, a):
-            e0, ne = CHUNKS[c]
-            n = ne * C
-            if ne == 1:
-                paired[c, a] = wu_bf[a][:, 4 * n * (e0 % 2) : 4 * n * (e0 % 2 + 1)]
-                picked[c, a] = paired[c, a].bitcast(U32).rearrange("p (c u) -> p u c", u=2)
+        def gather(i):
+            a, e0, ne = UNITS[i]
+            words = wu_bf[i % 2][:, : 4 * ne * C].bitcast(U32)
+            if i == last_unit:
+                paired[i] = wu_bf[i % 2][:, : 4 * ne * C]
+                picked[i] = words.rearrange("p (c u) -> p u c", u=2)
             else:
-                picked[c, a] = wu_bf[order.index((c, a)) % 2][:, : 4 * n].bitcast(U32).rearrange("p (u c) -> p u c", u=2)
+                picked[i] = words.rearrange("p (u c) -> p u c", u=2)
             for u in range(2):
                 nc.vector.tensor_copy(
-                    picked[c, a][:, u, :], windows[a, u][:].bitcast(U32).indirect(offs_t[:, e0 * C // 16 : (e0 + ne) * C // 16])
+                    picked[i][:, u, :], windows[a, u][:].bitcast(U32).indirect(offs_t[:, e0 * C // 16 : (e0 + ne) * C // 16])
                 )
 
-        def pair(c, a):
-            ne = CHUNKS[c][1]
-            n = ne * C
-            if ne > 1:
-                if c == 2:
-                    both = spare[a]
-                else:
-                    both = ring.tile([P, 4 * n], BF16, name="paired", tag="paired", align_bytes=64)
-                paired[c, a] = both[:]
-                nc.scalar.copy(
-                    paired[c, a].bitcast(U32).rearrange("p (c u) -> p c u", u=2), picked[c, a].rearrange("p u c -> p c u")
-                )
+        def pair(i):
+            if i in (4, 5):
+                both = spare[i - 4]
+            else:
+                both = ring.tile([P, 4 * UNITS[i][2] * C], BF16, name="both", tag="paired", align_bytes=64)
+            paired[i] = both[:]
+            nc.scalar.copy(paired[i].bitcast(U32).rearrange("p (c u) -> p c u", u=2), picked[i].rearrange("p u c -> p c u"))
 
-        def quantize_x(c, a):
-            n = CHUNKS[c][1] * C
-            x_codes[c, a] = keep.tile([P, n], U32, name="x_codes%d%d" % (c, a), align_bytes=64)
-            x_plane[c, a] = keep.tile([P, n], U8, name="x_plane%d%d" % (c, a), align_bytes=64)
-            nc.vector.quantize_mx(x_codes[c, a][:].bitcast(FP8X4), x_plane[c, a][:], paired[c, a])
+        def quantize_x(i):
+            n = UNITS[i][2] * C
+            x_codes[i] = keep.tile([P, n], U32, name="x_codes%d" % i, align_bytes=64)
+            x_plane[i] = keep.tile([P, n], U8, name="x_plane%d" % i, align_bytes=64)
+            nc.vector.quantize_mx(x_codes[i][:].bitcast(FP8X4), x_plane[i][:], paired[i])
 
         y = [keep.tile([P, S], F32, name="y%d" % h) for h in range(HALVES)]
+        unit_of = {(a, e): i for i, (a, e0, ne) in enumerate(UNITS) for e in range(e0, e0 + ne)}
 
-        chunk_of = {e: c for c, (e0, ne) in enumerate(CHUNKS) for e in range(e0, e0 + ne)}
-        groups = CHUNKS + [(12, 4)]
-
-        def experts(c, h):
-            e0, ne = groups[c]
+        def experts(h, e0, ne):
             bank = psum.tile([P, ne * C], F32, name="bank", tag="bank")
-            for i in range(ne):
-                e = e0 + i
-                slots = slice(C * i, C * (i + 1))
-                home = chunk_of[e]
-                own = slice(C * (e - CHUNKS[home][0]), C * (e - CHUNKS[home][0] + 1))
+            for e in range(e0, e0 + ne):
                 for a in range(PASSES):
+                    i = unit_of[a, e]
+                    own = slice(C * (e - UNITS[i][1]), C * (e - UNITS[i][1] + 1))
                     word0 = ((e % 2) * PASSES + a) * N + h * P
                     byte0 = (e * PASSES + a) * N + h * P
                     nc.tensor.matmul_mx(
-                        bank[:, slots],
+                        bank[:, C * (e - e0) : C * (e - e0 + 1)],
                         lhsT=w_codes[e // 2][:, 4 * word0 : 4 * (word0 + P)].bitcast(FP8X4),
                         lhsT_scale=w_plane[:, byte0 : byte0 + P],
-                        rhs=x_codes[home, a][:, own].bitcast(FP8X4),
-                        rhs_scale=x_plane[home, a][:, own],
+                        rhs=x_codes[i][:, own].bitcast(FP8X4),
+                        rhs_scale=x_plane[i][:, own],
                         start=(a == 0),
                         stop=(a == PASSES - 1),
                     )
-            if c == 0:
-                positive[c, h] = spare[h][:, : 2 * ne * C].bitcast(F32)
+            if e0 == 0:
+                positive[h, e0] = spare[h][:, : 2 * ne * C].bitcast(F32)
             else:
                 fresh = ring.tile([P, ne * C], F32, name="fresh", tag="positive%d" % h)
-                positive[c, h] = fresh[:]
-            for i in range(ne):
-                slots = slice(C * i, C * (i + 1))
-                nc.scalar.activation(
-                    positive[c, h][:, slots], bank[:, slots], ACT.Relu, bias=bias[:, h, e0 + i : e0 + i + 1]
-                )
+                positive[h, e0] = fresh[:]
+            for e in range(e0, e0 + ne):
+                slots = slice(C * (e - e0), C * (e - e0 + 1))
+                nc.scalar.activation(positive[h, e0][:, slots], bank[:, slots], ACT.Relu, bias=bias[:, h, e : e + 1])
 
-        def square(c, h):
-            e0, ne = groups[c]
-            nc.scalar.activation(y[h][:, e0 * C : (e0 + ne) * C], positive[c, h], ACT.Square)
+        def square(h, e0, ne):
+            nc.scalar.activation(y[h][:, e0 * C : (e0 + ne) * C], positive[h, e0], ACT.Square)
 
-        gather(0, 0)
+        gather(0)
         quantize_wu(1, nc.scalar.copy)
         for u in range(2):
             for s in range(2):
                 project(1, u, TH * s, TH, nc.scalar.copy)
-        steps = [
-            (pair, 0, 0), (gather, 1, 0), (quantize_x, 0, 0),
-            (pair, 1, 0), (gather, 0, 1), (quantize_x, 1, 0),
-            (pair, 0, 1), (gather, 1, 1), (quantize_x, 0, 1),
-            (pair, 1, 1), (gather, 2, 0), (quantize_x, 1, 1),
-            (experts, 0, 0), (square, 0, 0), (experts, 0, 1),
-            (pair, 2, 0), (gather, 2, 1), (quantize_x, 2, 0),
-            (square, 0, 1), (experts, 1, 0),
-            (pair, 2, 1), (gather, 3, 0), (quantize_x, 2, 1),
-            (square, 1, 0),
-            (pair, 3, 0), (gather, 3, 1), (quantize_x, 3, 0),
-            (experts, 1, 1),
-            (pair, 3, 1), (gather, 4, 0), (quantize_x, 3, 1),
-            (gather, 4, 1), (quantize_x, 4, 0), (gather, 5, 0), (quantize_x, 4, 1),
-            (gather, 5, 1), (quantize_x, 5, 0), (quantize_x, 5, 1),
-            (experts, 2, 0), (square, 1, 1), (square, 2, 0),
-        ]
-        steps += [(step, c, 0) for c in (3, 4, 5) for step in (experts, square)]
-        steps += [(step, c, 1) for c in (2, 6) for step in (experts, square)]
-        for step, c, i in steps:
-            step(c, i)
+        between = {
+            3: [(experts, 0, 0, 4), (square, 0, 0, 4), (experts, 1, 0, 4)],
+            4: [(square, 1, 0, 4), (experts, 0, 4, 4)],
+            5: [(square, 0, 4, 4), (experts, 1, 4, 4), (square, 1, 4, 4)],
+            6: [(experts, 0, 8, 4)],
+            7: [(square, 0, 8, 4)],
+        }
+        for i in range(last_unit):
+            pair(i)
+            gather(i + 1)
+            quantize_x(i)
+            for step, h, e0, ne in between.get(i, []):
+                step(h, e0, ne)
+        quantize_x(last_unit)
+        for h, e0, ne in ((0, 12, 2), (0, 14, 1), (0, 15, 1), (1, 8, 4), (1, 12, 4)):
+            experts(h, e0, ne)
+            square(h, e0, ne)
 
         def fetch(h, r, cols):
             prod = keep.tile([P, cols.stop - cols.start], F32, name="prod%d%d_%d" % (h, r, cols.start))

@@ -87,10 +87,11 @@ def tile_moe_prv_lin_relu2_kernel(
                 nc.sync.dma_start(gate_t[h, r][:], gate[r, P * h : P * (h + 1), :])
 
         wu_codes, wu_plane = {}, {}
-        wu_bf = [keep.tile([P, 4 * 512], BF16, name="wu_bf%d" % a, align_bytes=64) for a in range(PASSES)]
+        stage = [keep.tile([P, (4 + 2 * a) * 512], BF16, name="stage%d" % a, align_bytes=64) for a in range(PASSES)]
+        wu_bf = [stage[a][:, 2 * a * 512 :] for a in range(PASSES)]
 
         def quantize_wu(a, copy):
-            grouped = wu_bf[a][:].rearrange("p (t m j) -> p t m j", t=4, j=4)
+            grouped = wu_bf[a].rearrange("p (t m j) -> p t m j", t=4, j=4)
             for s in range(2):
                 copy(
                     grouped[:, :, 64 * s : 64 * (s + 1), :].rearrange("p t m j -> p m t j"),
@@ -99,7 +100,7 @@ def tile_moe_prv_lin_relu2_kernel(
             wu_codes[a] = keep.tile([P, 512], U32, name="wu_codes%d" % a, align_bytes=64)
             wu_plane[a] = keep.tile([P, 512], U8, name="wu_plane%d" % a, align_bytes=64)
             nc.vector.quantize_mx(
-                wu_codes[a][:].bitcast(FP8X4), wu_plane[a][:], wu_bf[a][:]
+                wu_codes[a][:].bitcast(FP8X4), wu_plane[a][:], wu_bf[a]
             )
 
         u_codes = keep.tile([P, T], U32, name="u_codes", align_bytes=64)
@@ -147,9 +148,9 @@ def tile_moe_prv_lin_relu2_kernel(
 
         def gather(i):
             a, e0, ne = UNITS[i]
-            words = wu_bf[i % 2][:, : 4 * ne * C].bitcast(U32)
+            words = stage[i % 2][:, : 4 * ne * C].bitcast(U32)
             if i == last_unit:
-                paired[i] = wu_bf[i % 2][:, : 4 * ne * C]
+                paired[i] = stage[i % 2][:, : 4 * ne * C]
                 picked[i] = words.rearrange("p (c u) -> p u c", u=2)
             else:
                 picked[i] = words.rearrange("p (u c) -> p u c", u=2)
@@ -271,7 +272,7 @@ def tile_moe_prv_lin_relu2_kernel(
             turn(turned, fetch(1, TOP - 2, cols), 2 * s, False, True)
             partial.append(turn_back(turned[2 * s : 2 * s + 2], "summed1%d" % s))
         last = [fetch(1, TOP - 1, cols) for cols in halves]
-        for s, cols in enumerate(halves):
-            result = keep.tile([P, TH], F32, name="result1%d" % s)
-            nc.vector.tensor_tensor(result[:], partial[s][:], last[s][:], ALU.add)
-            nc.sync.dma_start(out[P:, cols], result[:])
+        for s, cols in ((0, slice(0, TH)), (1, slice(0, P)), (1, slice(P, TH))):
+            result = keep.tile([P, cols.stop - cols.start], F32, name="result1%d_%d" % (s, cols.start))
+            nc.vector.tensor_tensor(result[:], partial[s][:, cols], last[s][:, cols], ALU.add)
+            nc.sync.dma_start(out[P:, TH * s + cols.start : TH * s + cols.stop], result[:])

@@ -20,7 +20,8 @@ PASSES = K // 512
 HALVES = N // P
 TH = T // 2
 WINDOW = 704
-PIECES = [(0, 256), (256, 128), (384, 128)]
+LOADS = [(0, 256), (256, 128), (384, 128)]
+PIECES = [(0, 0, 128), (0, 128, 128), (1, 256, 128), (2, 384, 128)]
 UNITS = [(0, 0, 4), (0, 4, 4), (1, 0, 4), (1, 4, 4), (0, 8, 4), (1, 8, 4), (0, 12, 4), (1, 12, 2), (1, 14, 1), (1, 15, 1)]
 FLOPS = 2 * M * K * T + 2 * K * N * S
 
@@ -43,7 +44,7 @@ def tile_moe_prv_lin_relu2_kernel(
                 windows[a, u] = keep.tile([P, 2 * WINDOW], BF16, name="win%d%d" % (a, u), align_bytes=64)
                 nc.vector.memset(windows[a, u][:, 2 * T :].bitcast(U32), 0)
         w_plane = keep.tile([P, E * PASSES * N], U8, name="w_plane", align_bytes=64)
-        nc.gpsimd.memset(w_plane[:].bitcast(I32), 0)
+        nc.vector.memset(w_plane[:].bitcast(I32), 0)
         ident = keep.tile([P, P], F32, name="ident")
         make_identity(nc, ident[:])
 
@@ -52,12 +53,11 @@ def tile_moe_prv_lin_relu2_kernel(
         wu_raw, u_raw = {}, {}
 
         def load_wu(a):
-            for s in range(2):
-                wu_raw[a, s] = keep.tile([P, 4, 256], F32, name="wu_raw%d%d" % (a, s))
-                nc.sync.dma_start(wu_raw[a, s][:], wu_rows[:, :, 512 * a + 256 * s : 512 * a + 256 * (s + 1)])
+            wu_raw[a] = keep.tile([P, 4, 512], F32, name="wu_raw%d" % a)
+            nc.sync.dma_start(wu_raw[a][:], wu_rows[:, :, 512 * a : 512 * (a + 1)])
 
         load_wu(0)
-        for s, (t0, nt) in enumerate(PIECES):
+        for s, (t0, nt) in enumerate(LOADS):
             u_raw[s] = keep.tile([P, 4, nt], F32, name="u_raw%d" % s)
             nc.sync.dma_start(u_raw[s][:], uT_rows[:, :, t0 : t0 + nt])
         nc.sync.dma_start(offs_t[:], offs)
@@ -86,42 +86,45 @@ def tile_moe_prv_lin_relu2_kernel(
                 gate_t[h, r] = keep.tile([P, T], F32, name="gate%d%d" % (h, r))
                 nc.sync.dma_start(gate_t[h, r][:], gate[r, P * h : P * (h + 1), :])
 
-        wu_codes, wu_plane = {}, {}
-        stage = [keep.tile([P, (4 + 2 * a) * 512], BF16, name="stage%d" % a, align_bytes=64) for a in range(PASSES)]
-        wu_bf = [stage[a][:, 2 * a * 512 :] for a in range(PASSES)]
+        wu_codes, wu_plane, wu_bf = {}, {}, {}
+        stage = [keep.tile([P, 6 * 512], BF16, name="stage%d" % i, align_bytes=64) for i in range(2)]
+        wu_bf[0, 0] = stage[0][:, :1024]
+        wu_bf[0, 1] = stage[0][:, 1024:2048]
+        wu_bf[1, 0] = stage[1][:, 1024:2048]
+        wu_bf[1, 1] = stage[0][:, 2048:]
 
-        def quantize_wu(a, copy):
-            grouped = wu_bf[a].rearrange("p (t m j) -> p t m j", t=4, j=4)
-            for s in range(2):
-                copy(
-                    grouped[:, :, 64 * s : 64 * (s + 1), :].rearrange("p t m j -> p m t j"),
-                    wu_raw[a, s][:].rearrange("p j (m t) -> p m t j", t=4),
-                )
-            wu_codes[a] = keep.tile([P, 512], U32, name="wu_codes%d" % a, align_bytes=64)
-            wu_plane[a] = keep.tile([P, 512], U8, name="wu_plane%d" % a, align_bytes=64)
-            nc.vector.quantize_mx(
-                wu_codes[a][:].bitcast(FP8X4), wu_plane[a][:], wu_bf[a]
+        def cast_wu(a, u, copy):
+            copy(
+                wu_bf[a, u].rearrange("p (t m j) -> p m t j", t=2, j=4),
+                wu_raw[a][:].rearrange("p j (m t) -> p m t j", t=4)[:, :, 2 * u : 2 * u + 2, :],
             )
+
+        def quantize_wu(a, u):
+            wu_codes[a, u] = keep.tile([P, 256], U32, name="wu_codes%d%d" % (a, u), align_bytes=64)
+            wu_plane[a, u] = keep.tile([P, 256], U8, name="wu_plane%d%d" % (a, u), align_bytes=64)
+            nc.vector.quantize_mx(wu_codes[a, u][:].bitcast(FP8X4), wu_plane[a, u][:], wu_bf[a, u])
 
         u_codes = keep.tile([P, T], U32, name="u_codes", align_bytes=64)
         u_plane = keep.tile([P, T], U8, name="u_plane", align_bytes=64)
+        u_bf = [keep.tile([P, 4 * nt], BF16, name="u_bf%d" % t0, align_bytes=64) for load, t0, nt in PIECES]
+
+        def cast_u(s, copy):
+            load, t0, nt = PIECES[s]
+            c0 = t0 - LOADS[load][0]
+            copy(u_bf[s][:].rearrange("p (c j) -> p c j", j=4), u_raw[load][:, :, c0 : c0 + nt].rearrange("p j c -> p c j"))
 
         def quantize_u(s):
-            t0, nt = PIECES[s]
-            grouped = wu_bf[1][:, 4 * t0 : 4 * (t0 + nt)]
-            nc.vector.tensor_copy(grouped.rearrange("p (c j) -> p c j", j=4), u_raw[s][:].rearrange("p j c -> p c j"))
-            nc.vector.quantize_mx(
-                u_codes[:, t0 : t0 + nt].bitcast(FP8X4), u_plane[:, t0 : t0 + nt], grouped
-            )
+            load, t0, nt = PIECES[s]
+            nc.vector.quantize_mx(u_codes[:, t0 : t0 + nt].bitcast(FP8X4), u_plane[:, t0 : t0 + nt], u_bf[s][:])
 
         def project(a, u, t0, nt, copy):
             bank = psum.tile([P, 2, nt], F32, name="bank", tag="bank")
             for i in range(2):
-                cols = slice(P * (2 * u + i), P * (2 * u + i + 1))
+                cols = slice(P * i, P * (i + 1))
                 nc.tensor.matmul_mx(
                     bank[:, i, :],
-                    lhsT=wu_codes[a][:, cols].bitcast(FP8X4),
-                    lhsT_scale=wu_plane[a][:, cols],
+                    lhsT=wu_codes[a, u][:, cols].bitcast(FP8X4),
+                    lhsT_scale=wu_plane[a, u][:, cols],
                     rhs=u_codes[:, t0 : t0 + nt].bitcast(FP8X4),
                     rhs_scale=u_plane[:, t0 : t0 + nt],
                     start=True,
@@ -132,14 +135,23 @@ def tile_moe_prv_lin_relu2_kernel(
                 bank[:].rearrange("p i t -> p t i"),
             )
 
-        quantize_wu(0, nc.vector.tensor_copy)
+        cast_wu(0, 0, nc.vector.tensor_copy)
+        cast_wu(0, 1, nc.scalar.copy)
+        quantize_wu(0, 0)
+        cast_u(0, nc.scalar.copy)
+        cast_u(1, nc.vector.tensor_copy)
         quantize_u(0)
-        project(0, 0, 0, 256, nc.scalar.copy)
-        project(0, 1, 0, 256, nc.scalar.copy)
+        cast_u(2, nc.scalar.copy)
         quantize_u(1)
+        cast_u(3, nc.scalar.copy)
         quantize_u(2)
+        quantize_wu(0, 1)
+        quantize_u(3)
+        project(0, 0, 0, 128, nc.vector.tensor_copy)
+        project(0, 0, 128, 128, nc.scalar.copy)
         project(0, 0, 256, 128, nc.vector.tensor_copy)
-        project(0, 0, 384, 128, nc.vector.tensor_copy)
+        project(0, 0, 384, 128, nc.scalar.copy)
+        project(0, 1, 0, 256, nc.scalar.copy)
         project(0, 1, 256, 256, nc.scalar.copy)
 
         x_codes, x_plane, paired, picked, positive = {}, {}, {}, {}, {}
@@ -206,8 +218,10 @@ def tile_moe_prv_lin_relu2_kernel(
             nc.scalar.activation(y[h][:, e0 * C : (e0 + ne) * C], positive[h, e0], ACT.Square)
 
         gather(0)
-        quantize_wu(1, nc.scalar.copy)
         for u in range(2):
+            cast_wu(1, u, nc.scalar.copy)
+        for u in range(2):
+            quantize_wu(1, u)
             for s in range(2):
                 project(1, u, TH * s, TH, nc.scalar.copy)
         between = {

@@ -23,6 +23,8 @@ WINDOW = 704
 LOADS = [(0, 256), (256, 128), (384, 128)]
 PIECES = [(0, 0, 128), (0, 128, 128), (1, 256, 128), (2, 384, 128)]
 UNITS = [(0, 0, 4), (0, 4, 4), (1, 0, 4), (1, 4, 4), (0, 8, 4), (1, 8, 4), (0, 12, 4), (1, 12, 2), (1, 14, 1), (1, 15, 1)]
+SHARED = {3: 256, 5: 256}
+BANK_OF = {(0, 0): 2, (1, 0): 3, (0, 4): 4, (1, 4): 0, (0, 8): 5, (1, 8): 1, (0, 12): 6, (0, 14): 7, (0, 15): 4, (1, 12): 2}
 FLOPS = 2 * M * K * T + 2 * K * N * S
 
 
@@ -32,8 +34,8 @@ def tile_moe_prv_lin_relu2_kernel(
     nc = tc.nc
     with ExitStack() as ctx:
         keep = ctx.enter_context(tc.tile_pool(name="keep", bufs=1))
-        ring = ctx.enter_context(tc.tile_pool(name="ring", bufs=3))
-        psum = ctx.enter_context(tc.psum_pool(name="psum", bufs=8))
+        psum = ctx.enter_context(tc.psum_pool(name="psum", bufs=1))
+        banks = [psum.tile([P, 512], F32, name="bank%d" % i) for i in range(8)]
 
         offs_t = keep.tile([P, S // 16], U16, name="offs_t")
         pos_t = [keep.tile([P, T // 16], U16, name="pos_t%d" % r) for r in range(TOP)]
@@ -53,7 +55,7 @@ def tile_moe_prv_lin_relu2_kernel(
         wu_raw, u_raw = {}, {}
 
         def load_wu(a):
-            wu_raw[a] = keep.tile([P, 4, 512], F32, name="wu_raw%d" % a)
+            wu_raw[a] = keep.tile([P, 4, 512], F32, name="wu_raw%d" % a, align_bytes=64)
             nc.sync.dma_start(wu_raw[a][:], wu_rows[:, :, 512 * a : 512 * (a + 1)])
 
         load_wu(0)
@@ -90,8 +92,8 @@ def tile_moe_prv_lin_relu2_kernel(
         stage = [keep.tile([P, 6 * 512], BF16, name="stage%d" % i, align_bytes=64) for i in range(2)]
         wu_bf[0, 0] = stage[0][:, :1024]
         wu_bf[0, 1] = stage[0][:, 1024:2048]
-        wu_bf[1, 0] = stage[1][:, 1024:2048]
-        wu_bf[1, 1] = stage[0][:, 2048:]
+        wu_bf[1, 1] = stage[1][:, 1024:2048]
+        wu_bf[1, 0] = stage[1][:, :1024]
 
         def cast_wu(a, u, copy):
             copy(
@@ -117,8 +119,8 @@ def tile_moe_prv_lin_relu2_kernel(
             load, t0, nt = PIECES[s]
             nc.vector.quantize_mx(u_codes[:, t0 : t0 + nt].bitcast(FP8X4), u_plane[:, t0 : t0 + nt], u_bf[s][:])
 
-        def project(a, u, t0, nt, copy):
-            bank = psum.tile([P, 2, nt], F32, name="bank", tag="bank")
+        def project(a, u, t0, nt, copy, nb):
+            bank = banks[nb][:, : 2 * nt].rearrange("p (i t) -> p i t", i=2)
             for i in range(2):
                 cols = slice(P * i, P * (i + 1))
                 nc.tensor.matmul_mx(
@@ -132,7 +134,7 @@ def tile_moe_prv_lin_relu2_kernel(
                 )
             copy(
                 windows[a, u][:, 2 * t0 : 2 * (t0 + nt)].rearrange("p (t i) -> p t i", i=2),
-                bank[:].rearrange("p i t -> p t i"),
+                bank.rearrange("p i t -> p t i"),
             )
 
         cast_wu(0, 0, nc.vector.tensor_copy)
@@ -147,36 +149,53 @@ def tile_moe_prv_lin_relu2_kernel(
         quantize_u(2)
         quantize_wu(0, 1)
         quantize_u(3)
-        project(0, 0, 0, 128, nc.vector.tensor_copy)
-        project(0, 0, 128, 128, nc.scalar.copy)
-        project(0, 0, 256, 128, nc.vector.tensor_copy)
-        project(0, 0, 384, 128, nc.scalar.copy)
-        project(0, 1, 0, 256, nc.scalar.copy)
-        project(0, 1, 256, 256, nc.scalar.copy)
+        project(0, 0, 0, 128, nc.vector.tensor_copy, 0)
+        project(0, 0, 128, 128, nc.scalar.copy, 1)
+        project(0, 0, 256, 128, nc.vector.tensor_copy, 2)
+        project(0, 0, 384, 128, nc.scalar.copy, 3)
+        project(0, 1, 0, 256, nc.scalar.copy, 4)
+        project(0, 1, 256, 256, nc.scalar.copy, 5)
 
-        x_codes, x_plane, paired, picked, positive = {}, {}, {}, {}, {}
-        spare = [keep.tile([P, 4 * 512], BF16, name="spare%d" % i, align_bytes=64) for i in range(2)]
+        x_codes, x_plane, picked = {}, {}, {}
+        spare = [keep.tile([P, 4 * 512], BF16, name="spare%d" % i, align_bytes=64) for i in range(5)]
+        singles = spare[4][:, : 2 * T].rearrange("p (i t) -> p i t", i=2)
+        late = keep.tile([P, 12 * C], F32, name="late")
+        paired = [
+            wu_raw[1][:, :2, :].rearrange("p j c -> p (j c)").bitcast(BF16),
+            spare[2][:],
+            spare[3][:],
+            spare[0][:],
+            spare[4][:],
+            spare[0][:],
+            spare[1][:],
+            stage[0][:, 1536:2560],
+            stage[1][:, 512:1024],
+            stage[1][:, :512],
+        ]
         last_unit = len(UNITS) - 1
+
+        def slots_of(s0, ns):
+            return offs_t[:, s0 // 16 : (s0 + ns) // 16]
 
         def gather(i):
             a, e0, ne = UNITS[i]
             words = stage[i % 2][:, : 4 * ne * C].bitcast(U32)
             if i == last_unit:
-                paired[i] = stage[i % 2][:, : 4 * ne * C]
                 picked[i] = words.rearrange("p (c u) -> p u c", u=2)
             else:
                 picked[i] = words.rearrange("p (u c) -> p u c", u=2)
             for u in range(2):
-                nc.vector.tensor_copy(
-                    picked[i][:, u, :], windows[a, u][:].bitcast(U32).indirect(offs_t[:, e0 * C // 16 : (e0 + ne) * C // 16])
-                )
+                ns = ne * C - u * SHARED.get(i, 0)
+                nc.vector.tensor_copy(picked[i][:, u, :ns], windows[a, u][:].bitcast(U32).indirect(slots_of(e0 * C, ns)))
+
+        def gather_share(i):
+            a, e0, ne = UNITS[i]
+            ns = SHARED[i]
+            words = stage[i % 2][:, 4 * ne * C - 2 * ns : 4 * ne * C].rearrange("p (c i) -> p c i", i=2)
+            for k in range(2):
+                nc.scalar.activation(words[:, :, k], singles[:, k, :].indirect(slots_of((e0 + ne) * C - ns, ns)), ACT.Copy)
 
         def pair(i):
-            if i in (4, 5):
-                both = spare[i - 4]
-            else:
-                both = ring.tile([P, 4 * UNITS[i][2] * C], BF16, name="both", tag="paired", align_bytes=64)
-            paired[i] = both[:]
             nc.scalar.copy(paired[i].bitcast(U32).rearrange("p (c u) -> p c u", u=2), picked[i].rearrange("p u c -> p c u"))
 
         def quantize_x(i):
@@ -188,59 +207,109 @@ def tile_moe_prv_lin_relu2_kernel(
         y = [keep.tile([P, S], F32, name="y%d" % h) for h in range(HALVES)]
         unit_of = {(a, e): i for i, (a, e0, ne) in enumerate(UNITS) for e in range(e0, e0 + ne)}
 
-        def experts(h, e0, ne):
-            bank = psum.tile([P, ne * C], F32, name="bank", tag="bank")
+        def one_pass(h, e0, e, a):
+            i = unit_of[a, e]
+            own = slice(C * (e - UNITS[i][1]), C * (e - UNITS[i][1] + 1))
+            word0 = ((e % 2) * PASSES + a) * N + h * P
+            byte0 = (e * PASSES + a) * N + h * P
+            nc.tensor.matmul_mx(
+                banks[BANK_OF[h, e0]][:, C * (e - e0) : C * (e - e0 + 1)],
+                lhsT=w_codes[e // 2][:, 4 * word0 : 4 * (word0 + P)].bitcast(FP8X4),
+                lhsT_scale=w_plane[:, byte0 : byte0 + P],
+                rhs=x_codes[i][:, own].bitcast(FP8X4),
+                rhs_scale=x_plane[i][:, own],
+                start=(a == 0),
+                stop=(a == PASSES - 1),
+            )
+
+        def multiply(h, e0, ne):
             for e in range(e0, e0 + ne):
                 for a in range(PASSES):
-                    i = unit_of[a, e]
-                    own = slice(C * (e - UNITS[i][1]), C * (e - UNITS[i][1] + 1))
-                    word0 = ((e % 2) * PASSES + a) * N + h * P
-                    byte0 = (e * PASSES + a) * N + h * P
-                    nc.tensor.matmul_mx(
-                        bank[:, C * (e - e0) : C * (e - e0 + 1)],
-                        lhsT=w_codes[e // 2][:, 4 * word0 : 4 * (word0 + P)].bitcast(FP8X4),
-                        lhsT_scale=w_plane[:, byte0 : byte0 + P],
-                        rhs=x_codes[i][:, own].bitcast(FP8X4),
-                        rhs_scale=x_plane[i][:, own],
-                        start=(a == 0),
-                        stop=(a == PASSES - 1),
-                    )
-            if e0 == 0:
-                positive[h, e0] = spare[h][:, : 2 * ne * C].bitcast(F32)
-            else:
-                fresh = ring.tile([P, ne * C], F32, name="fresh", tag="positive%d" % h)
-                positive[h, e0] = fresh[:]
+                    one_pass(h, e0, e, a)
+
+        def rectify(h, e0, ne, positive):
             for e in range(e0, e0 + ne):
                 slots = slice(C * (e - e0), C * (e - e0 + 1))
-                nc.scalar.activation(positive[h, e0][:, slots], bank[:, slots], ACT.Relu, bias=bias[:, h, e : e + 1])
+                nc.scalar.activation(positive[:, slots], banks[BANK_OF[h, e0]][:, slots], ACT.Relu, bias=bias[:, h, e : e + 1])
 
-        def square(h, e0, ne):
-            nc.scalar.activation(y[h][:, e0 * C : (e0 + ne) * C], positive[h, e0], ACT.Square)
+        def square(h, e0, ne, positive):
+            nc.scalar.activation(y[h][:, e0 * C : (e0 + ne) * C], positive, ACT.Square)
+
+        def activate(h, e0, ne, positive):
+            rectify(h, e0, ne, positive)
+            square(h, e0, ne, positive)
 
         gather(0)
         for u in range(2):
             cast_wu(1, u, nc.scalar.copy)
+        pair(0)
         for u in range(2):
             quantize_wu(1, u)
             for s in range(2):
-                project(1, u, TH * s, TH, nc.scalar.copy)
-        between = {
-            3: [(experts, 0, 0, 4), (square, 0, 0, 4), (experts, 1, 0, 4)],
-            4: [(square, 1, 0, 4), (experts, 0, 4, 4)],
-            5: [(square, 0, 4, 4), (experts, 1, 4, 4), (square, 1, 4, 4)],
-            6: [(experts, 0, 8, 4)],
-            7: [(square, 0, 8, 4)],
-        }
-        for i in range(last_unit):
-            pair(i)
-            gather(i + 1)
-            quantize_x(i)
-            for step, h, e0, ne in between.get(i, []):
-                step(h, e0, ne)
-        quantize_x(last_unit)
-        for h, e0, ne in ((0, 12, 2), (0, 14, 1), (0, 15, 1), (1, 8, 4), (1, 12, 4)):
-            experts(h, e0, ne)
-            square(h, e0, ne)
+                project(1, u, TH * s, TH, nc.scalar.copy, (6 + 2 * u + s) % 8)
+        gather(1)
+        quantize_x(0)
+        pair(1)
+        for s in range(2):
+            nc.scalar.copy(singles[:, :, TH * s : TH * (s + 1)], banks[s][:].rearrange("p (i t) -> p i t", i=2))
+        gather(2)
+        quantize_x(1)
+        pair(2)
+        gather(3)
+        gather_share(3)
+        quantize_x(2)
+        pair(3)
+        gather(4)
+        quantize_x(3)
+        gather(5)
+        gather_share(5)
+        pair(4)
+        quantize_x(4)
+        multiply(0, 0, 4)
+        activate(0, 0, 4, spare[0][:, : 8 * C].bitcast(F32))
+        multiply(1, 0, 4)
+        multiply(0, 4, 4)
+        multiply(1, 4, 4)
+        pair(5)
+        gather(6)
+        quantize_x(5)
+        activate(0, 4, 4, spare[1][:, : 8 * C].bitcast(F32))
+        pair(6)
+        gather(7)
+        quantize_x(6)
+        multiply(0, 8, 4)
+        multiply(1, 8, 4)
+        pair(7)
+        gather(8)
+        quantize_x(7)
+        third = stage[0][:, 512:1536].bitcast(F32)
+        rectify(0, 8, 4, third)
+        pair(8)
+        square(0, 8, 4, third)
+        gather(9)
+        quantize_x(8)
+        quantize_x(9)
+        fresh = keep.tile([P, 3 * C], F32, name="fresh")
+        multiply(0, 12, 2)
+        activate(0, 12, 2, fresh[:, : 2 * C])
+        multiply(0, 14, 1)
+        activate(0, 14, 1, fresh[:, 2 * C :])
+        multiply(0, 15, 1)
+        multiply(1, 12, 4)
+        spread = late[:].rearrange("p (g c) -> p g c", g=16)[:, :, :8]
+        nc.scalar.activation(
+            spread, banks[BANK_OF[0, 15]][:, :C].rearrange("p (g c) -> p g c", g=16), ACT.Relu, bias=bias[:, 0, 15:16]
+        )
+        nc.scalar.activation(y[0][:, 15 * C :].rearrange("p (g c) -> p g c", g=16), spread, ACT.Square)
+        first = stage[1][:, : 8 * C].bitcast(F32)
+        for e in range(4):
+            slots = slice(C * e, C * (e + 1))
+            nc.vector.tensor_scalar(
+                first[:, slots], banks[BANK_OF[1, 0]][:, slots], bias[:, 1, e : e + 1], 0.0, ALU.add, ALU.max
+            )
+        nc.vector.tensor_tensor(y[1][:, : 4 * C], first, first, ALU.mult)
+        for e0 in (4, 8, 12):
+            activate(1, e0, 4, late[:, C * (e0 - 4) : C * e0])
 
         def fetch(h, r, cols):
             prod = keep.tile([P, cols.stop - cols.start], F32, name="prod%d%d_%d" % (h, r, cols.start))
@@ -252,7 +321,7 @@ def tile_moe_prv_lin_relu2_kernel(
         def turn(turned, prod, blk0, start, stop):
             for i in range(prod.shape[1] // P):
                 nc.tensor.matmul(
-                    turned[blk0 + i][:],
+                    turned[blk0 + i],
                     lhsT=prod[:, P * i : P * (i + 1)],
                     rhs=ident[:],
                     start=start,
@@ -260,23 +329,22 @@ def tile_moe_prv_lin_relu2_kernel(
                     is_transpose=True,
                 )
 
-        def turn_back(turned, name):
-            summed = keep.tile([P, len(turned) * P], F32, name=name)
-            back = psum.tile([P, len(turned) * P], F32, name="bank", tag="bank")
+        def turn_back(turned, summed, nb):
+            back = banks[nb][:, : len(turned) * P]
             for i, block in enumerate(turned):
                 cols = slice(P * i, P * (i + 1))
-                nc.scalar.copy(summed[:, cols], block[:])
+                nc.scalar.copy(summed[:, cols], block)
                 nc.tensor.transpose(back[:, cols], summed[:, cols], ident[:])
             return back
 
         whole = slice(0, T)
         halves = [slice(0, TH), slice(TH, T)]
-        turned = [psum.tile([P, P], F32, name="bank", tag="bank") for blk in range(T // P)]
+        turned = [banks[4 + blk][:, :P] for blk in range(T // P)]
         for r in range(TOP):
             turn(turned, fetch(0, r, whole), 0, r == 0, r == TOP - 1)
-        back = turn_back(turned, "summed0")
+        back = turn_back(turned, late[:, 8 * C :], 3)
         result = keep.tile([P, T], F32, name="result0")
-        nc.scalar.copy(result[:], back[:])
+        nc.scalar.copy(result[:], back)
         nc.sync.dma_start(out[:P, :], result[:])
 
         for r in range(TOP - 2):
@@ -284,7 +352,7 @@ def tile_moe_prv_lin_relu2_kernel(
         partial = []
         for s, cols in enumerate(halves):
             turn(turned, fetch(1, TOP - 2, cols), 2 * s, False, True)
-            partial.append(turn_back(turned[2 * s : 2 * s + 2], "summed1%d" % s))
+            partial.append(turn_back(turned[2 * s : 2 * s + 2], late[:, TH * s : TH * (s + 1)], s))
         last = [fetch(1, TOP - 1, cols) for cols in halves]
         for s, cols in ((0, slice(0, TH)), (1, slice(0, P)), (1, slice(P, TH))):
             result = keep.tile([P, cols.stop - cols.start], F32, name="result1%d_%d" % (s, cols.start))

@@ -23,7 +23,7 @@ WINDOW = 704
 LOADS = [(0, 256), (256, 128), (384, 128)]
 PIECES = [(0, 0, 128), (0, 128, 128), (1, 256, 128), (2, 384, 128)]
 UNITS = [(0, 0, 4), (0, 4, 4), (1, 0, 4), (1, 4, 4), (0, 8, 4), (1, 8, 4), (0, 12, 4), (1, 12, 2), (1, 14, 1), (1, 15, 1)]
-SHARED = {3: 256, 5: 256}
+SHARED = {3: 384, 5: 256}
 BANK_OF = {(0, 0): 2, (1, 0): 3, (0, 4): 4, (1, 4): 0, (0, 8): 5, (1, 8): 1, (0, 12): 6, (0, 14): 7, (0, 15): 4, (1, 12): 2}
 FLOPS = 2 * M * K * T + 2 * K * N * S
 
@@ -89,11 +89,13 @@ def tile_moe_prv_lin_relu2_kernel(
                 nc.sync.dma_start(gate_t[h, r][:], gate[r, P * h : P * (h + 1), :])
 
         wu_codes, wu_plane, wu_bf = {}, {}, {}
-        stage = [keep.tile([P, 6 * 512], BF16, name="stage%d" % i, align_bytes=64) for i in range(2)]
+        reused = wu_raw[1][:].rearrange("p j c -> p (j c)").bitcast(BF16)
+        stage = [keep.tile([P, 5 * 512], BF16, name="stage0", align_bytes=64), reused[:, 2048:]]
+        second_bf = keep.tile([P, 2048], BF16, name="second_bf", align_bytes=64)
         wu_bf[0, 0] = stage[0][:, :1024]
         wu_bf[0, 1] = stage[0][:, 1024:2048]
-        wu_bf[1, 1] = stage[1][:, 1024:2048]
-        wu_bf[1, 0] = stage[1][:, :1024]
+        wu_bf[1, 0] = second_bf[:, :1024]
+        wu_bf[1, 1] = second_bf[:, 1024:]
 
         def cast_wu(a, u, copy):
             copy(
@@ -161,13 +163,13 @@ def tile_moe_prv_lin_relu2_kernel(
         singles = spare[4][:, : 2 * T].rearrange("p (i t) -> p i t", i=2)
         late = keep.tile([P, 12 * C], F32, name="late")
         paired = [
-            wu_raw[1][:, :2, :].rearrange("p j c -> p (j c)").bitcast(BF16),
+            reused[:, :2048],
             spare[2][:],
             spare[3][:],
             spare[0][:],
+            spare[2][:],
+            spare[3][:],
             spare[4][:],
-            spare[0][:],
-            spare[1][:],
             stage[0][:, 1536:2560],
             stage[1][:, 512:1024],
             stage[1][:, :512],
@@ -227,24 +229,32 @@ def tile_moe_prv_lin_relu2_kernel(
                 for a in range(PASSES):
                     one_pass(h, e0, e, a)
 
-        def rectify(h, e0, ne, positive):
+        def rectify(h, group, e0, ne, positive):
             for e in range(e0, e0 + ne):
-                slots = slice(C * (e - e0), C * (e - e0 + 1))
-                nc.scalar.activation(positive[:, slots], banks[BANK_OF[h, e0]][:, slots], ACT.Relu, bias=bias[:, h, e : e + 1])
+                nc.scalar.activation(
+                    positive[:, C * (e - e0) : C * (e - e0 + 1)],
+                    banks[BANK_OF[h, group]][:, C * (e - group) : C * (e - group + 1)],
+                    ACT.Relu,
+                    bias=bias[:, h, e : e + 1],
+                )
 
         def square(h, e0, ne, positive):
             nc.scalar.activation(y[h][:, e0 * C : (e0 + ne) * C], positive, ACT.Square)
 
         def activate(h, e0, ne, positive):
-            rectify(h, e0, ne, positive)
+            rectify(h, e0, e0, ne, positive)
             square(h, e0, ne, positive)
 
         gather(0)
-        for u in range(2):
-            cast_wu(1, u, nc.scalar.copy)
+        cast_wu(1, 0, nc.scalar.copy)
+        cast_wu(1, 1, lambda dst, src: nc.gpsimd.tensor_scalar(dst, src, 1.0, 0.0, ALU.mult, ALU.add))
         pair(0)
+        second_codes = keep.tile([P, 512], U32, name="second_codes", align_bytes=64)
+        second_plane = keep.tile([P, 512], U8, name="second_plane", align_bytes=64)
+        nc.vector.quantize_mx(second_codes[:].bitcast(FP8X4), second_plane[:], second_bf[:])
         for u in range(2):
-            quantize_wu(1, u)
+            wu_codes[1, u] = second_codes[:, 256 * u : 256 * (u + 1)]
+            wu_plane[1, u] = second_plane[:, 256 * u : 256 * (u + 1)]
             for s in range(2):
                 project(1, u, TH * s, TH, nc.scalar.copy, (6 + 2 * u + s) % 8)
         gather(1)
@@ -258,23 +268,36 @@ def tile_moe_prv_lin_relu2_kernel(
         gather(3)
         gather_share(3)
         quantize_x(2)
+        ahead_of_share = stage[1][:, 12 * C : 14 * C].bitcast(F32)
+        ahead_of_pair = [spare[2][:, : 2 * C].bitcast(F32), spare[4][:, 2 * T : 2 * T + 2 * C].bitcast(F32)]
+        rest = spare[1][:].bitcast(F32)
         pair(3)
         gather(4)
+        multiply(0, 0, 4)
+        rectify(0, 0, 1, 1, ahead_of_pair[0])
+        rectify(0, 0, 0, 1, ahead_of_share)
+        square(0, 1, 1, ahead_of_pair[0])
+        rectify(0, 0, 2, 1, rest[:, :C])
+        square(0, 0, 1, ahead_of_share)
+        rectify(0, 0, 3, 1, rest[:, C : 2 * C])
         quantize_x(3)
         gather(5)
-        gather_share(5)
         pair(4)
+        square(0, 2, 2, rest[:, : 2 * C])
+        gather_share(5)
         quantize_x(4)
-        multiply(0, 0, 4)
-        activate(0, 0, 4, spare[0][:, : 8 * C].bitcast(F32))
         multiply(1, 0, 4)
         multiply(0, 4, 4)
         multiply(1, 4, 4)
         pair(5)
         gather(6)
         quantize_x(5)
-        activate(0, 4, 4, spare[1][:, : 8 * C].bitcast(F32))
+        rectify(0, 4, 4, 1, ahead_of_pair[1])
+        rectify(0, 4, 5, 1, rest[:, 2 * C : 3 * C])
+        square(0, 4, 1, ahead_of_pair[1])
+        rectify(0, 4, 6, 2, rest[:, 3 * C : 5 * C])
         pair(6)
+        square(0, 5, 3, rest[:, 2 * C : 5 * C])
         gather(7)
         quantize_x(6)
         multiply(0, 8, 4)
@@ -283,7 +306,7 @@ def tile_moe_prv_lin_relu2_kernel(
         gather(8)
         quantize_x(7)
         third = stage[0][:, 512:1536].bitcast(F32)
-        rectify(0, 8, 4, third)
+        rectify(0, 8, 8, 4, third)
         pair(8)
         square(0, 8, 4, third)
         gather(9)
@@ -291,15 +314,17 @@ def tile_moe_prv_lin_relu2_kernel(
         quantize_x(9)
         fresh = keep.tile([P, 3 * C], F32, name="fresh")
         multiply(0, 12, 2)
-        activate(0, 12, 2, fresh[:, : 2 * C])
+        rectify(0, 12, 12, 2, fresh[:, : 2 * C])
         multiply(0, 14, 1)
-        activate(0, 14, 1, fresh[:, 2 * C :])
+        rectify(0, 14, 14, 1, fresh[:, 2 * C :])
+        square(0, 12, 2, fresh[:, : 2 * C])
         multiply(0, 15, 1)
         multiply(1, 12, 4)
         spread = late[:].rearrange("p (g c) -> p g c", g=16)[:, :, :8]
         nc.scalar.activation(
             spread, banks[BANK_OF[0, 15]][:, :C].rearrange("p (g c) -> p g c", g=16), ACT.Relu, bias=bias[:, 0, 15:16]
         )
+        square(0, 14, 1, fresh[:, 2 * C :])
         nc.scalar.activation(y[0][:, 15 * C :].rearrange("p (g c) -> p g c", g=16), spread, ACT.Square)
         first = stage[1][:, : 8 * C].bitcast(F32)
         for e in range(4):

@@ -22,8 +22,9 @@ TH = T // 2
 WINDOW = 704
 LOADS = [(0, 256), (256, 128), (384, 128)]
 PIECES = [(0, 0, 128), (0, 128, 128), (1, 256, 128), (2, 384, 128)]
-UNITS = [(0, 0, 4), (0, 4, 4), (1, 0, 4), (1, 4, 4), (0, 8, 4), (1, 8, 4), (0, 12, 4), (1, 12, 2), (1, 14, 1), (1, 15, 1)]
-SHARED = {3: 384, 5: 256}
+UNITS = [(0, 0, 4), (0, 4, 4), (0, 8, 4), (1, 0, 4), (1, 4, 4), (1, 8, 4), (0, 12, 4), (1, 12, 2), (1, 14, 1), (1, 15, 1)]
+SHARED = (3, 4, 5)
+WOVEN = [512, 512, 320, 320, 320, 512, 320, 128, 128]
 BANK_OF = {(0, 0): 2, (1, 0): 3, (0, 4): 4, (1, 4): 0, (0, 8): 5, (1, 8): 1, (0, 12): 6, (0, 14): 7, (0, 15): 4, (1, 12): 2}
 FLOPS = 2 * M * K * T + 2 * K * N * S
 
@@ -40,11 +41,11 @@ def tile_moe_prv_lin_relu2_kernel(
         offs_t = keep.tile([P, S // 16], U16, name="offs_t")
         pos_t = [keep.tile([P, T // 16], U16, name="pos_t%d" % r) for r in range(TOP)]
 
-        windows = {}
-        for a in range(PASSES):
-            for u in range(2):
-                windows[a, u] = keep.tile([P, 2 * WINDOW], BF16, name="win%d%d" % (a, u), align_bytes=64)
-                nc.vector.memset(windows[a, u][:, 2 * T :].bitcast(U32), 0)
+        spare = [keep.tile([P, 4 * 512], BF16, name="spare%d" % i, align_bytes=64) for i in range(5)]
+        windows = {(1, 1): spare[0][:, : 2 * T]}
+        for a, u in ((0, 0), (0, 1), (1, 0)):
+            windows[a, u] = keep.tile([P, 2 * WINDOW], BF16, name="win%d%d" % (a, u), align_bytes=64)[:]
+            nc.vector.memset(windows[a, u][:, 2 * T :].bitcast(U32), 0)
         w_plane = keep.tile([P, E * PASSES * N], U8, name="w_plane", align_bytes=64)
         nc.vector.memset(w_plane[:].bitcast(I32), 0)
         ident = keep.tile([P, P], F32, name="ident")
@@ -52,11 +53,12 @@ def tile_moe_prv_lin_relu2_kernel(
 
         wu_rows = wu.rearrange("(p j) k -> p j k", j=4)
         uT_rows = uT.rearrange("(p j) t -> p j t", j=4)
-        wu_raw, u_raw = {}, {}
+        wu_room, wu_raw, u_raw = {}, {}, {}
 
         def load_wu(a):
-            wu_raw[a] = keep.tile([P, 4, 512], F32, name="wu_raw%d" % a, align_bytes=64)
-            nc.sync.dma_start(wu_raw[a][:], wu_rows[:, :, 512 * a : 512 * (a + 1)])
+            wu_room[a] = keep.tile([P, 4 + a, 512], F32, name="wu_raw%d" % a, align_bytes=64)
+            wu_raw[a] = wu_room[a][:, :4, :]
+            nc.sync.dma_start(wu_raw[a], wu_rows[:, :, 512 * a : 512 * (a + 1)])
 
         load_wu(0)
         for s, (t0, nt) in enumerate(LOADS):
@@ -82,15 +84,14 @@ def tile_moe_prv_lin_relu2_kernel(
             w_codes.append(wt)
         for r, pos in enumerate((pos1, pos2, pos3, pos4)):
             nc.sync.dma_start(pos_t[r][:], pos)
-        gate_t = {}
-        for h in range(HALVES):
-            for r in range(TOP):
-                gate_t[h, r] = keep.tile([P, T], F32, name="gate%d%d" % (h, r))
-                nc.sync.dma_start(gate_t[h, r][:], gate[r, P * h : P * (h + 1), :])
+        gate_t = [keep.tile([P, T], F32, name="gate%d" % r) for r in range(TOP)]
+        for r in range(TOP):
+            nc.sync.dma_start(gate_t[r][:], gate[r, :P, :])
 
         wu_codes, wu_plane, wu_bf = {}, {}, {}
-        reused = wu_raw[1][:].rearrange("p j c -> p (j c)").bitcast(BF16)
-        stage = [keep.tile([P, 5 * 512], BF16, name="stage0", align_bytes=64), reused[:, 2048:]]
+        odd = wu_room[1][:].rearrange("p j c -> p (j c)").bitcast(BF16)
+        even = keep.tile([P, 3 * 1024], BF16, name="even", align_bytes=64)
+        stage = [even[:, :2048], odd[:, 2048:4096], even[:, :2048]] + [odd[:, 3072:], even[:, 1024:]] * 4
         second_bf = keep.tile([P, 2048], BF16, name="second_bf", align_bytes=64)
         wu_bf[0, 0] = stage[0][:, :1024]
         wu_bf[0, 1] = stage[0][:, 1024:2048]
@@ -100,7 +101,7 @@ def tile_moe_prv_lin_relu2_kernel(
         def cast_wu(a, u, copy):
             copy(
                 wu_bf[a, u].rearrange("p (t m j) -> p m t j", t=2, j=4),
-                wu_raw[a][:].rearrange("p j (m t) -> p m t j", t=4)[:, :, 2 * u : 2 * u + 2, :],
+                wu_raw[a].rearrange("p j (m t) -> p m t j", t=4)[:, :, 2 * u : 2 * u + 2, :],
             )
 
         def quantize_wu(a, u):
@@ -121,7 +122,7 @@ def tile_moe_prv_lin_relu2_kernel(
             load, t0, nt = PIECES[s]
             nc.vector.quantize_mx(u_codes[:, t0 : t0 + nt].bitcast(FP8X4), u_plane[:, t0 : t0 + nt], u_bf[s][:])
 
-        def project(a, u, t0, nt, copy, nb):
+        def project(a, u, t0, nt, nb):
             bank = banks[nb][:, : 2 * nt].rearrange("p (i t) -> p i t", i=2)
             for i in range(2):
                 cols = slice(P * i, P * (i + 1))
@@ -134,9 +135,11 @@ def tile_moe_prv_lin_relu2_kernel(
                     start=True,
                     stop=True,
                 )
+
+        def fill(a, u, t0, nt, nb, copy):
             copy(
                 windows[a, u][:, 2 * t0 : 2 * (t0 + nt)].rearrange("p (t i) -> p t i", i=2),
-                bank.rearrange("p i t -> p t i"),
+                banks[nb][:, : 2 * nt].rearrange("p (i t) -> p t i", i=2),
             )
 
         cast_wu(0, 0, nc.vector.tensor_copy)
@@ -151,54 +154,66 @@ def tile_moe_prv_lin_relu2_kernel(
         quantize_u(2)
         quantize_wu(0, 1)
         quantize_u(3)
-        project(0, 0, 0, 128, nc.vector.tensor_copy, 0)
-        project(0, 0, 128, 128, nc.scalar.copy, 1)
-        project(0, 0, 256, 128, nc.vector.tensor_copy, 2)
-        project(0, 0, 384, 128, nc.scalar.copy, 3)
-        project(0, 1, 0, 256, nc.scalar.copy, 4)
-        project(0, 1, 256, 256, nc.scalar.copy, 5)
+        project(0, 0, 0, 128, 0)
+        fill(0, 0, 0, 128, 0, nc.vector.tensor_copy)
+        project(0, 0, 128, 128, 1)
+        fill(0, 0, 128, 128, 1, nc.scalar.copy)
+        project(0, 0, 256, 128, 2)
+        fill(0, 0, 256, 128, 2, nc.vector.tensor_copy)
+        project(0, 0, 384, 128, 3)
+        fill(0, 0, 384, 128, 3, nc.scalar.copy)
+        project(0, 1, 0, 256, 4)
+        fill(0, 1, 0, 256, 4, nc.scalar.copy)
+        project(0, 1, 256, 256, 5)
+        fill(0, 1, 256, 256, 5, nc.scalar.copy)
 
-        x_codes, x_plane, picked = {}, {}, {}
-        spare = [keep.tile([P, 4 * 512], BF16, name="spare%d" % i, align_bytes=64) for i in range(5)]
-        singles = spare[4][:, : 2 * T].rearrange("p (i t) -> p i t", i=2)
+        x_codes, x_plane = {}, {}
+        singles = keep.tile([P, 2, T], BF16, name="singles", align_bytes=64)
         late = keep.tile([P, 12 * C], F32, name="late")
         paired = [
-            reused[:, :2048],
+            odd[:, :2048],
             spare[2][:],
             spare[3][:],
             spare[0][:],
             spare[2][:],
             spare[3][:],
-            spare[4][:],
-            stage[0][:, 1536:2560],
-            stage[1][:, 512:1024],
-            stage[1][:, :512],
+            spare[1][:],
+            spare[4][:, :1024],
+            stage[7][:, 512:1024],
+            stage[9][:, :512],
         ]
         last_unit = len(UNITS) - 1
 
         def slots_of(s0, ns):
             return offs_t[:, s0 // 16 : (s0 + ns) // 16]
 
+        def picked(i):
+            words = stage[i][:, : 4 * UNITS[i][2] * C].bitcast(U32)
+            return words.rearrange("p (c u) -> p u c" if i == last_unit else "p (u c) -> p u c", u=2)
+
         def gather(i):
             a, e0, ne = UNITS[i]
-            words = stage[i % 2][:, : 4 * ne * C].bitcast(U32)
-            if i == last_unit:
-                picked[i] = words.rearrange("p (c u) -> p u c", u=2)
-            else:
-                picked[i] = words.rearrange("p (u c) -> p u c", u=2)
-            for u in range(2):
-                ns = ne * C - u * SHARED.get(i, 0)
-                nc.vector.tensor_copy(picked[i][:, u, :ns], windows[a, u][:].bitcast(U32).indirect(slots_of(e0 * C, ns)))
+            for u in range(1 if i in SHARED else 2):
+                nc.vector.tensor_copy(picked(i)[:, u, :], windows[a, u].bitcast(U32).indirect(slots_of(e0 * C, ne * C)))
 
-        def gather_share(i):
+        def gather_share(i, half):
             a, e0, ne = UNITS[i]
-            ns = SHARED[i]
-            words = stage[i % 2][:, 4 * ne * C - 2 * ns : 4 * ne * C].rearrange("p (c i) -> p c i", i=2)
+            ns = ne * C // 2
+            words = stage[i][:, 2 * ns * (2 + half) : 2 * ns * (3 + half)].rearrange("p (c i) -> p c i", i=2)
             for k in range(2):
-                nc.scalar.activation(words[:, :, k], singles[:, k, :].indirect(slots_of((e0 + ne) * C - ns, ns)), ACT.Copy)
+                nc.scalar.activation(words[:, :, k], singles[:, k, :].indirect(slots_of(e0 * C + ns * half, ns)), ACT.Copy)
+
+        def weave(i, copy, slots):
+            copy(
+                paired[i].bitcast(U32).rearrange("p (c u) -> p c u", u=2)[:, slots, :],
+                picked(i).rearrange("p u c -> p c u")[:, slots, :],
+            )
 
         def pair(i):
-            nc.scalar.copy(paired[i].bitcast(U32).rearrange("p (c u) -> p c u", u=2), picked[i].rearrange("p u c -> p c u"))
+            weave(i, nc.gpsimd.tensor_copy, slice(0, WOVEN[i]))
+
+        def pair_rest(i):
+            weave(i, nc.scalar.copy, slice(WOVEN[i], UNITS[i][2] * C))
 
         def quantize_x(i):
             n = UNITS[i][2] * C
@@ -255,66 +270,77 @@ def tile_moe_prv_lin_relu2_kernel(
         for u in range(2):
             wu_codes[1, u] = second_codes[:, 256 * u : 256 * (u + 1)]
             wu_plane[1, u] = second_plane[:, 256 * u : 256 * (u + 1)]
-            for s in range(2):
-                project(1, u, TH * s, TH, nc.scalar.copy, (6 + 2 * u + s) % 8)
+        for s in range(2):
+            project(1, 1, TH * s, TH, 6 + s)
+            nc.scalar.copy(singles[:, :, TH * s : TH * (s + 1)], banks[6 + s][:].rearrange("p (i t) -> p i t", i=2))
+        for s in range(2):
+            project(1, 0, TH * s, TH, s)
         gather(1)
         quantize_x(0)
         pair(1)
+        gather_share(3, 0)
+        gather_share(3, 1)
         for s in range(2):
-            nc.scalar.copy(singles[:, :, TH * s : TH * (s + 1)], banks[s][:].rearrange("p (i t) -> p i t", i=2))
+            fill(1, 0, TH * s, TH, s, nc.scalar.copy)
         gather(2)
         quantize_x(1)
         pair(2)
+        pair_rest(2)
+        gather_share(4, 0)
         gather(3)
-        gather_share(3)
         quantize_x(2)
-        ahead_of_share = stage[1][:, 12 * C : 14 * C].bitcast(F32)
-        ahead_of_pair = [spare[2][:, : 2 * C].bitcast(F32), spare[4][:, 2 * T : 2 * T + 2 * C].bitcast(F32)]
-        rest = spare[1][:].bitcast(F32)
         pair(3)
+        pair_rest(3)
+        gather_share(4, 1)
         gather(4)
-        multiply(0, 0, 4)
-        rectify(0, 0, 1, 1, ahead_of_pair[0])
-        rectify(0, 0, 0, 1, ahead_of_share)
-        square(0, 1, 1, ahead_of_pair[0])
-        rectify(0, 0, 2, 1, rest[:, :C])
-        square(0, 0, 1, ahead_of_share)
-        rectify(0, 0, 3, 1, rest[:, C : 2 * C])
         quantize_x(3)
-        gather(5)
         pair(4)
-        square(0, 2, 2, rest[:, : 2 * C])
-        gather_share(5)
+        pair_rest(4)
+        gather(5)
+        gather_share(5, 0)
+        gather_share(5, 1)
         quantize_x(4)
-        multiply(1, 0, 4)
-        multiply(0, 4, 4)
-        multiply(1, 4, 4)
         pair(5)
         gather(6)
         quantize_x(5)
-        rectify(0, 4, 4, 1, ahead_of_pair[1])
-        rectify(0, 4, 5, 1, rest[:, 2 * C : 3 * C])
-        square(0, 4, 1, ahead_of_pair[1])
-        rectify(0, 4, 6, 2, rest[:, 3 * C : 5 * C])
-        pair(6)
-        square(0, 5, 3, rest[:, 2 * C : 5 * C])
-        gather(7)
-        quantize_x(6)
+        ahead = [paired[i][:, 4 * WOVEN[i] : 4 * WOVEN[i] + 2 * C].bitcast(F32) for i in (6, 7)]
+        rest = keep.tile([P, 10 * C], F32, name="rest")
+        multiply(0, 0, 4)
+        rectify(0, 0, 0, 1, ahead[0])
+        rectify(0, 0, 1, 1, rest[:, :C])
+        square(0, 0, 1, ahead[0])
+        rectify(0, 0, 2, 2, rest[:, C : 3 * C])
+        fill(1, 1, 0, TH, 6, nc.scalar.copy)
+        square(0, 1, 3, rest[:, : 3 * C])
+        fill(1, 1, TH, TH, 7, nc.scalar.copy)
+        multiply(1, 0, 4)
+        multiply(0, 4, 4)
+        multiply(1, 4, 4)
         multiply(0, 8, 4)
         multiply(1, 8, 4)
+        pair(6)
+        pair_rest(6)
+        gather(7)
+        quantize_x(6)
+        rectify(0, 4, 4, 1, ahead[1])
+        rectify(0, 4, 5, 1, rest[:, 3 * C : 4 * C])
+        square(0, 4, 1, ahead[1])
+        rectify(0, 4, 6, 2, rest[:, 4 * C : 6 * C])
         pair(7)
+        pair_rest(7)
+        square(0, 5, 3, rest[:, 3 * C : 6 * C])
         gather(8)
         quantize_x(7)
-        third = stage[0][:, 512:1536].bitcast(F32)
+        third = rest[:, 6 * C :]
         rectify(0, 8, 8, 4, third)
         pair(8)
-        square(0, 8, 4, third)
         gather(9)
         quantize_x(8)
         quantize_x(9)
         fresh = keep.tile([P, 3 * C], F32, name="fresh")
         multiply(0, 12, 2)
         rectify(0, 12, 12, 2, fresh[:, : 2 * C])
+        square(0, 8, 4, third)
         multiply(0, 14, 1)
         rectify(0, 14, 14, 1, fresh[:, 2 * C :])
         square(0, 12, 2, fresh[:, : 2 * C])
@@ -326,7 +352,7 @@ def tile_moe_prv_lin_relu2_kernel(
         )
         square(0, 14, 1, fresh[:, 2 * C :])
         nc.scalar.activation(y[0][:, 15 * C :].rearrange("p (g c) -> p g c", g=16), spread, ACT.Square)
-        first = stage[1][:, : 8 * C].bitcast(F32)
+        first = stage[9][:, : 8 * C].bitcast(F32)
         for e in range(4):
             slots = slice(C * e, C * (e + 1))
             nc.vector.tensor_scalar(
@@ -339,7 +365,7 @@ def tile_moe_prv_lin_relu2_kernel(
         def fetch(h, r, cols):
             prod = keep.tile([P, cols.stop - cols.start], F32, name="prod%d%d_%d" % (h, r, cols.start))
             nc.vector.tensor_tensor(
-                prod[:], y[h][:].indirect(pos_t[r][:, cols.start // 16 : cols.stop // 16]), gate_t[h, r][:, cols], ALU.mult
+                prod[:], y[h][:].indirect(pos_t[r][:, cols.start // 16 : cols.stop // 16]), gate_t[r][:, cols], ALU.mult
             )
             return prod
 

@@ -24,7 +24,7 @@ LOADS = [(0, 256), (256, 128), (384, 128)]
 PIECES = [(0, 0, 128), (0, 128, 128), (1, 256, 128), (2, 384, 128)]
 UNITS = [(0, 0, 4), (0, 4, 4), (0, 8, 4), (1, 0, 4), (1, 4, 4), (1, 8, 4), (0, 12, 4), (1, 12, 2), (1, 14, 1), (1, 15, 1)]
 SHARED = (3, 4, 5)
-WOVEN = [512, 512, 320, 320, 320, 512, 320, 128, 128]
+WOVEN = [512, 512, 256, 256, 256, 384, 256, 128, 128]
 BANK_OF = {(0, 0): 2, (1, 0): 3, (0, 4): 4, (1, 4): 0, (0, 8): 5, (1, 8): 1, (0, 12): 6, (0, 14): 7, (0, 15): 4, (1, 12): 2}
 FLOPS = 2 * M * K * T + 2 * K * N * S
 
@@ -98,10 +98,10 @@ def tile_moe_prv_lin_relu2_kernel(
         wu_bf[1, 0] = second_bf[:, :1024]
         wu_bf[1, 1] = second_bf[:, 1024:]
 
-        def cast_wu(a, u, copy):
+        def cast_wu(a, u, copy, rows=slice(0, P)):
             copy(
-                wu_bf[a, u].rearrange("p (t m j) -> p m t j", t=2, j=4),
-                wu_raw[a].rearrange("p j (m t) -> p m t j", t=4)[:, :, 2 * u : 2 * u + 2, :],
+                wu_bf[a, u].rearrange("p (t m j) -> p m t j", t=2, j=4)[:, rows],
+                wu_raw[a].rearrange("p j (m t) -> p m t j", t=4)[:, rows, 2 * u : 2 * u + 2, :],
             )
 
         def quantize_wu(a, u):
@@ -191,9 +191,9 @@ def tile_moe_prv_lin_relu2_kernel(
             words = stage[i][:, : 4 * UNITS[i][2] * C].bitcast(U32)
             return words.rearrange("p (c u) -> p u c" if i == last_unit else "p (u c) -> p u c", u=2)
 
-        def gather(i):
+        def gather(i, pairs=(0, 1)):
             a, e0, ne = UNITS[i]
-            for u in range(1 if i in SHARED else 2):
+            for u in (0,) if i in SHARED else pairs:
                 nc.vector.tensor_copy(picked(i)[:, u, :], windows[a, u].bitcast(U32).indirect(slots_of(e0 * C, ne * C)))
 
         def gather_share(i, half):
@@ -261,21 +261,21 @@ def tile_moe_prv_lin_relu2_kernel(
             square(h, e0, ne, positive)
 
         gather(0)
-        cast_wu(1, 0, nc.scalar.copy)
-        cast_wu(1, 1, lambda dst, src: nc.gpsimd.tensor_scalar(dst, src, 1.0, 0.0, ALU.mult, ALU.add))
+        for u in (1, 0):
+            cast_wu(1, u, nc.scalar.copy, slice(0, P // 2))
+            cast_wu(
+                1, u, lambda dst, src: nc.gpsimd.tensor_scalar(dst, src, 1.0, 0.0, ALU.mult, ALU.add), slice(P // 2, P)
+            )
         pair(0)
-        second_codes = keep.tile([P, 512], U32, name="second_codes", align_bytes=64)
-        second_plane = keep.tile([P, 512], U8, name="second_plane", align_bytes=64)
-        nc.vector.quantize_mx(second_codes[:].bitcast(FP8X4), second_plane[:], second_bf[:])
-        for u in range(2):
-            wu_codes[1, u] = second_codes[:, 256 * u : 256 * (u + 1)]
-            wu_plane[1, u] = second_plane[:, 256 * u : 256 * (u + 1)]
+        quantize_wu(1, 1)
         for s in range(2):
             project(1, 1, TH * s, TH, 6 + s)
             nc.scalar.copy(singles[:, :, TH * s : TH * (s + 1)], banks[6 + s][:].rearrange("p (i t) -> p i t", i=2))
+        gather(1, (0,))
+        quantize_wu(1, 0)
         for s in range(2):
             project(1, 0, TH * s, TH, s)
-        gather(1)
+        gather(1, (1,))
         quantize_x(0)
         pair(1)
         gather_share(3, 0)
@@ -300,7 +300,9 @@ def tile_moe_prv_lin_relu2_kernel(
         gather_share(5, 0)
         gather_share(5, 1)
         quantize_x(4)
-        pair(5)
+        weave(5, nc.gpsimd.tensor_copy, slice(0, 2 * C))
+        weave(5, nc.gpsimd.tensor_copy, slice(2 * C, WOVEN[5]))
+        pair_rest(5)
         gather(6)
         quantize_x(5)
         ahead = [paired[i][:, 4 * WOVEN[i] : 4 * WOVEN[i] + 2 * C].bitcast(F32) for i in (6, 7)]

@@ -24,7 +24,7 @@ LOADS = [(0, 256), (256, 128), (384, 128)]
 PIECES = [(0, 0, 128), (0, 128, 128), (1, 256, 128), (2, 384, 128)]
 UNITS = [(0, 0, 4), (0, 4, 4), (0, 8, 4), (1, 0, 4), (1, 4, 4), (1, 8, 4), (0, 12, 4), (1, 12, 2), (1, 14, 1), (1, 15, 1)]
 SHARED = (3, 4, 5)
-WOVEN = [512, 512, 256, 256, 256, 384, 256, 128, 128]
+WOVEN = [256, 512, 320, 320, 320, 384, 320, 128, 128]
 BANK_OF = {(0, 0): 2, (1, 0): 3, (0, 4): 4, (1, 4): 0, (0, 8): 5, (1, 8): 1, (0, 12): 6, (0, 14): 7, (0, 15): 4, (1, 12): 2}
 FLOPS = 2 * M * K * T + 2 * K * N * S
 
@@ -267,6 +267,7 @@ def tile_moe_prv_lin_relu2_kernel(
                 1, u, lambda dst, src: nc.gpsimd.tensor_scalar(dst, src, 1.0, 0.0, ALU.mult, ALU.add), slice(P // 2, P)
             )
         pair(0)
+        pair_rest(0)
         quantize_wu(1, 1)
         for s in range(2):
             project(1, 1, TH * s, TH, 6 + s)

@@ -19,12 +19,15 @@ S = E * C
 PASSES = K // 512
 HALVES = N // P
 TH = T // 2
+RUN = 2 * 4 * C
 WINDOW = 704
-LOADS = [(0, 256), (256, 128), (384, 128)]
-PIECES = [(0, 0, 128), (0, 128, 128), (1, 256, 128), (2, 384, 128)]
+TOKEN_LOADS = [(0, 256), (256, 128), (384, 128)]
+TOKEN_PIECES = [(0, 0), (0, 128), (1, 256), (2, 384)]
 UNITS = [(0, 0, 4), (0, 4, 4), (0, 8, 4), (1, 0, 4), (1, 4, 4), (1, 8, 4), (0, 12, 4), (1, 12, 2), (1, 14, 1), (1, 15, 1)]
-SHARED = (3, 4, 5)
-WOVEN = [256, 512, 320, 320, 320, 384, 320, 128, 128]
+LAST_UNIT = len(UNITS) - 1
+SCALAR_GATHERS = (3, 4, 5)
+SHORT_SHARE = 320
+GPSIMD_WEAVES = [2 * C, 4 * C, SHORT_SHARE, SHORT_SHARE, SHORT_SHARE, 2 * C, SHORT_SHARE, C, C]
 BANK_OF = {(0, 0): 2, (1, 0): 3, (0, 4): 4, (1, 4): 0, (0, 8): 5, (1, 8): 1, (0, 12): 6, (0, 14): 7, (0, 15): 4, (1, 12): 2}
 FLOPS = 2 * M * K * T + 2 * K * N * S
 
@@ -41,8 +44,9 @@ def tile_moe_prv_lin_relu2_kernel(
         offs_t = keep.tile([P, S // 16], U16, name="offs_t")
         pos_t = [keep.tile([P, T // 16], U16, name="pos_t%d" % r) for r in range(TOP)]
 
-        spare = [keep.tile([P, 4 * 512], BF16, name="spare%d" % i, align_bytes=64) for i in range(5)]
-        windows = {(1, 1): spare[0][:, : 2 * T]}
+        spare = [keep.tile([P, 2 * RUN], BF16, name="spare%d" % i, align_bytes=64) for i in range(5)]
+        shifted = keep.tile([P, T + 2 * RUN], BF16, name="shifted", align_bytes=64)
+        windows = {(1, 1): shifted[:, : 2 * T]}
         for a, u in ((0, 0), (0, 1), (1, 0)):
             windows[a, u] = keep.tile([P, 2 * WINDOW], BF16, name="win%d%d" % (a, u), align_bytes=64)[:]
             nc.vector.memset(windows[a, u][:, 2 * T :].bitcast(U32), 0)
@@ -61,7 +65,7 @@ def tile_moe_prv_lin_relu2_kernel(
             nc.sync.dma_start(wu_raw[a], wu_rows[:, :, 512 * a : 512 * (a + 1)])
 
         load_wu(0)
-        for s, (t0, nt) in enumerate(LOADS):
+        for s, (t0, nt) in enumerate(TOKEN_LOADS):
             u_raw[s] = keep.tile([P, 4, nt], F32, name="u_raw%d" % s)
             nc.sync.dma_start(u_raw[s][:], uT_rows[:, :, t0 : t0 + nt])
         nc.sync.dma_start(offs_t[:], offs)
@@ -76,58 +80,59 @@ def tile_moe_prv_lin_relu2_kernel(
         nc.sync.dma_start(bias[:], b.rearrange("(h p) e -> p h e", p=P))
         w_codes = []
         for g in range(E // 2):
-            wt = keep.tile([P, 2 * PASSES * N * 4], U8, name="w_codes%d" % g, align_bytes=64)
+            two_experts = keep.tile([P, 2 * PASSES * N * 4], U8, name="w_codes%d" % g, align_bytes=64)
             nc.sync.dma_start(
-                wt[:].bitcast(I32).rearrange("p (g n) -> p g n", g=2 * PASSES),
+                two_experts[:].bitcast(I32).rearrange("p (g n) -> p g n", g=2 * PASSES),
                 w_words[2 * g : 2 * g + 2].rearrange("e a p n r -> p (e a) (n r)").bitcast(I32),
             )
-            w_codes.append(wt)
+            w_codes.append(two_experts)
         for r, pos in enumerate((pos1, pos2, pos3, pos4)):
             nc.sync.dma_start(pos_t[r][:], pos)
         gate_t = [keep.tile([P, T], F32, name="gate%d" % r) for r in range(TOP)]
         for r in range(TOP):
             nc.sync.dma_start(gate_t[r][:], gate[r, :P, :])
 
-        wu_codes, wu_plane, wu_bf = {}, {}, {}
         odd = wu_room[1][:].rearrange("p j c -> p (j c)").bitcast(BF16)
-        even = keep.tile([P, 3 * 1024], BF16, name="even", align_bytes=64)
-        stage = [even[:, :2048], odd[:, 2048:4096], even[:, :2048]] + [odd[:, 3072:], even[:, 1024:]] * 4
-        second_bf = keep.tile([P, 2048], BF16, name="second_bf", align_bytes=64)
-        wu_bf[0, 0] = stage[0][:, :1024]
-        wu_bf[0, 1] = stage[0][:, 1024:2048]
-        wu_bf[1, 0] = second_bf[:, :1024]
-        wu_bf[1, 1] = second_bf[:, 1024:]
+        even = keep.tile([P, 3 * RUN], BF16, name="even", align_bytes=64)
+        runs = [even[:, : 2 * RUN], odd[:, 2 * RUN : 4 * RUN], even[:, : 2 * RUN]] + [odd[:, 3 * RUN :], even[:, RUN:]] * 4
 
-        def cast_wu(a, u, copy, rows=slice(0, P)):
+        wu_codes, wu_plane = {}, {}
+        second_bf = keep.tile([P, 2 * RUN], BF16, name="second_bf", align_bytes=64)
+        wu_bf = {(0, 0): even[:, :RUN], (0, 1): even[:, RUN : 2 * RUN], (1, 0): second_bf[:, :RUN], (1, 1): second_bf[:, RUN:]}
+
+        def cast_wu(a, u, copy, words=slice(0, P)):
             copy(
-                wu_bf[a, u].rearrange("p (t m j) -> p m t j", t=2, j=4)[:, rows],
-                wu_raw[a].rearrange("p j (m t) -> p m t j", t=4)[:, rows, 2 * u : 2 * u + 2, :],
+                wu_bf[a, u].rearrange("p (i m j) -> p m i j", i=2, j=4)[:, words],
+                wu_raw[a].rearrange("p j (m t) -> p m t j", t=4)[:, words, 2 * u : 2 * u + 2, :],
             )
 
+        def gpsimd_cast(dst, src):
+            nc.gpsimd.tensor_scalar(dst, src, 1.0, 0.0, ALU.mult, ALU.add)
+
         def quantize_wu(a, u):
-            wu_codes[a, u] = keep.tile([P, 256], U32, name="wu_codes%d%d" % (a, u), align_bytes=64)
-            wu_plane[a, u] = keep.tile([P, 256], U8, name="wu_plane%d%d" % (a, u), align_bytes=64)
+            wu_codes[a, u] = keep.tile([P, 2 * P], U32, name="wu_codes%d%d" % (a, u), align_bytes=64)
+            wu_plane[a, u] = keep.tile([P, 2 * P], U8, name="wu_plane%d%d" % (a, u), align_bytes=64)
             nc.vector.quantize_mx(wu_codes[a, u][:].bitcast(FP8X4), wu_plane[a, u][:], wu_bf[a, u])
 
         u_codes = keep.tile([P, T], U32, name="u_codes", align_bytes=64)
         u_plane = keep.tile([P, T], U8, name="u_plane", align_bytes=64)
-        u_bf = [keep.tile([P, 4 * nt], BF16, name="u_bf%d" % t0, align_bytes=64) for load, t0, nt in PIECES]
+        u_bf = [keep.tile([P, 4 * P], BF16, name="u_bf%d" % t0, align_bytes=64) for load, t0 in TOKEN_PIECES]
 
         def cast_u(s, copy):
-            load, t0, nt = PIECES[s]
-            c0 = t0 - LOADS[load][0]
-            copy(u_bf[s][:].rearrange("p (c j) -> p c j", j=4), u_raw[load][:, :, c0 : c0 + nt].rearrange("p j c -> p c j"))
+            load, t0 = TOKEN_PIECES[s]
+            c0 = t0 - TOKEN_LOADS[load][0]
+            copy(u_bf[s][:].rearrange("p (c j) -> p c j", j=4), u_raw[load][:, :, c0 : c0 + P].rearrange("p j c -> p c j"))
 
         def quantize_u(s):
-            load, t0, nt = PIECES[s]
-            nc.vector.quantize_mx(u_codes[:, t0 : t0 + nt].bitcast(FP8X4), u_plane[:, t0 : t0 + nt], u_bf[s][:])
+            t0 = TOKEN_PIECES[s][1]
+            nc.vector.quantize_mx(u_codes[:, t0 : t0 + P].bitcast(FP8X4), u_plane[:, t0 : t0 + P], u_bf[s][:])
 
-        def project(a, u, t0, nt, nb):
-            bank = banks[nb][:, : 2 * nt].rearrange("p (i t) -> p i t", i=2)
+        def project(a, u, t0, nt, bank):
+            both = banks[bank][:, : 2 * nt].rearrange("p (i t) -> p i t", i=2)
             for i in range(2):
                 cols = slice(P * i, P * (i + 1))
                 nc.tensor.matmul_mx(
-                    bank[:, i, :],
+                    both[:, i, :],
                     lhsT=wu_codes[a, u][:, cols].bitcast(FP8X4),
                     lhsT_scale=wu_plane[a, u][:, cols],
                     rhs=u_codes[:, t0 : t0 + nt].bitcast(FP8X4),
@@ -136,10 +141,10 @@ def tile_moe_prv_lin_relu2_kernel(
                     stop=True,
                 )
 
-        def fill(a, u, t0, nt, nb, copy):
+        def fill_window(a, u, t0, nt, bank, copy):
             copy(
                 windows[a, u][:, 2 * t0 : 2 * (t0 + nt)].rearrange("p (t i) -> p t i", i=2),
-                banks[nb][:, : 2 * nt].rearrange("p (i t) -> p t i", i=2),
+                banks[bank][:, : 2 * nt].rearrange("p (i t) -> p t i", i=2),
             )
 
         cast_wu(0, 0, nc.vector.tensor_copy)
@@ -154,95 +159,92 @@ def tile_moe_prv_lin_relu2_kernel(
         quantize_u(2)
         quantize_wu(0, 1)
         quantize_u(3)
-        project(0, 0, 0, 128, 0)
-        fill(0, 0, 0, 128, 0, nc.vector.tensor_copy)
-        project(0, 0, 128, 128, 1)
-        fill(0, 0, 128, 128, 1, nc.scalar.copy)
-        project(0, 0, 256, 128, 2)
-        fill(0, 0, 256, 128, 2, nc.vector.tensor_copy)
-        project(0, 0, 384, 128, 3)
-        fill(0, 0, 384, 128, 3, nc.scalar.copy)
-        project(0, 1, 0, 256, 4)
-        fill(0, 1, 0, 256, 4, nc.scalar.copy)
-        project(0, 1, 256, 256, 5)
-        fill(0, 1, 256, 256, 5, nc.scalar.copy)
+        for s in range(T // P):
+            project(0, 0, P * s, P, s)
+            fill_window(0, 0, P * s, P, s, nc.scalar.copy if s % 2 else nc.vector.tensor_copy)
+        for s in range(2):
+            project(0, 1, TH * s, TH, 4 + s)
+            fill_window(0, 1, TH * s, TH, 4 + s, nc.scalar.copy)
 
         x_codes, x_plane = {}, {}
         singles = keep.tile([P, 2, T], BF16, name="singles", align_bytes=64)
         late = keep.tile([P, 12 * C], F32, name="late")
-        paired = [
-            odd[:, :2048],
+        woven = [
+            odd[:, : 2 * RUN],
             spare[2][:],
             spare[3][:],
             spare[0][:],
-            spare[2][:],
+            shifted[:, T:],
             spare[3][:],
             spare[1][:],
-            spare[4][:, :1024],
-            stage[7][:, 512:1024],
-            stage[9][:, :512],
+            spare[4][:, :RUN],
+            runs[7][:, 4 * C : 8 * C],
+            runs[9][:, : 4 * C],
         ]
-        last_unit = len(UNITS) - 1
 
         def slots_of(s0, ns):
             return offs_t[:, s0 // 16 : (s0 + ns) // 16]
 
         def picked(i):
-            words = stage[i][:, : 4 * UNITS[i][2] * C].bitcast(U32)
-            return words.rearrange("p (c u) -> p u c" if i == last_unit else "p (u c) -> p u c", u=2)
+            words = runs[i][:, : 4 * UNITS[i][2] * C].bitcast(U32)
+            return words.rearrange("p (c u) -> p u c" if i == LAST_UNIT else "p (u c) -> p u c", u=2)
 
         def gather(i, pairs=(0, 1)):
             a, e0, ne = UNITS[i]
-            for u in (0,) if i in SHARED else pairs:
+            for u in (0,) if i in SCALAR_GATHERS else pairs:
                 nc.vector.tensor_copy(picked(i)[:, u, :], windows[a, u].bitcast(U32).indirect(slots_of(e0 * C, ne * C)))
 
-        def gather_share(i, half):
+        def gather_singles(i, half):
             a, e0, ne = UNITS[i]
             ns = ne * C // 2
-            words = stage[i][:, 2 * ns * (2 + half) : 2 * ns * (3 + half)].rearrange("p (c i) -> p c i", i=2)
+            pairs = runs[i][:, 2 * ns * (2 + half) : 2 * ns * (3 + half)].rearrange("p (c i) -> p c i", i=2)
             for k in range(2):
-                nc.scalar.activation(words[:, :, k], singles[:, k, :].indirect(slots_of(e0 * C + ns * half, ns)), ACT.Copy)
+                nc.scalar.activation(pairs[:, :, k], singles[:, k, :].indirect(slots_of(e0 * C + ns * half, ns)), ACT.Copy)
+
+        def join_singles(s):
+            nc.gpsimd.tensor_copy(
+                windows[1, 1][:, 2 * TH * s : 2 * TH * (s + 1)].rearrange("p (t i) -> p t i", i=2),
+                singles[:, :, TH * s : TH * (s + 1)].rearrange("p i t -> p t i"),
+            )
+
 
         def weave(i, copy, slots):
             copy(
-                paired[i].bitcast(U32).rearrange("p (c u) -> p c u", u=2)[:, slots, :],
+                woven[i].bitcast(U32).rearrange("p (c u) -> p c u", u=2)[:, slots, :],
                 picked(i).rearrange("p u c -> p c u")[:, slots, :],
             )
 
-        def pair(i):
-            weave(i, nc.gpsimd.tensor_copy, slice(0, WOVEN[i]))
+        def weave_gpsimd(i):
+            weave(i, nc.gpsimd.tensor_copy, slice(0, GPSIMD_WEAVES[i]))
 
-        def pair_rest(i):
-            weave(i, nc.scalar.copy, slice(WOVEN[i], UNITS[i][2] * C))
+        def weave_scalar(i):
+            weave(i, nc.scalar.copy, slice(GPSIMD_WEAVES[i], UNITS[i][2] * C))
 
         def quantize_x(i):
             n = UNITS[i][2] * C
             x_codes[i] = keep.tile([P, n], U32, name="x_codes%d" % i, align_bytes=64)
             x_plane[i] = keep.tile([P, n], U8, name="x_plane%d" % i, align_bytes=64)
-            nc.vector.quantize_mx(x_codes[i][:].bitcast(FP8X4), x_plane[i][:], paired[i])
+            nc.vector.quantize_mx(x_codes[i][:].bitcast(FP8X4), x_plane[i][:], woven[i])
 
         y = [keep.tile([P, S], F32, name="y%d" % h) for h in range(HALVES)]
         unit_of = {(a, e): i for i, (a, e0, ne) in enumerate(UNITS) for e in range(e0, e0 + ne)}
 
-        def one_pass(h, e0, e, a):
-            i = unit_of[a, e]
-            own = slice(C * (e - UNITS[i][1]), C * (e - UNITS[i][1] + 1))
-            word0 = ((e % 2) * PASSES + a) * N + h * P
-            byte0 = (e * PASSES + a) * N + h * P
-            nc.tensor.matmul_mx(
-                banks[BANK_OF[h, e0]][:, C * (e - e0) : C * (e - e0 + 1)],
-                lhsT=w_codes[e // 2][:, 4 * word0 : 4 * (word0 + P)].bitcast(FP8X4),
-                lhsT_scale=w_plane[:, byte0 : byte0 + P],
-                rhs=x_codes[i][:, own].bitcast(FP8X4),
-                rhs_scale=x_plane[i][:, own],
-                start=(a == 0),
-                stop=(a == PASSES - 1),
-            )
-
         def multiply(h, e0, ne):
             for e in range(e0, e0 + ne):
                 for a in range(PASSES):
-                    one_pass(h, e0, e, a)
+                    i = unit_of[a, e]
+                    own = slice(C * (e - UNITS[i][1]), C * (e - UNITS[i][1] + 1))
+                    word0 = ((e % 2) * PASSES + a) * N + h * P
+                    byte0 = (e * PASSES + a) * N + h * P
+                    nc.tensor.matmul_mx(
+                        banks[BANK_OF[h, e0]][:, C * (e - e0) : C * (e - e0 + 1)],
+                        lhsT=w_codes[e // 2][:, 4 * word0 : 4 * (word0 + P)].bitcast(FP8X4),
+                        lhsT_scale=w_plane[:, byte0 : byte0 + P],
+                        rhs=x_codes[i][:, own].bitcast(FP8X4),
+                        rhs_scale=x_plane[i][:, own],
+                        start=(a == 0),
+                        stop=(a == PASSES - 1),
+                    )
 
         def rectify(h, group, e0, ne, positive):
             for e in range(e0, e0 + ne):
@@ -256,114 +258,109 @@ def tile_moe_prv_lin_relu2_kernel(
         def square(h, e0, ne, positive):
             nc.scalar.activation(y[h][:, e0 * C : (e0 + ne) * C], positive, ACT.Square)
 
-        def activate(h, e0, ne, positive):
-            rectify(h, e0, e0, ne, positive)
-            square(h, e0, ne, positive)
-
         gather(0)
         for u in (1, 0):
             cast_wu(1, u, nc.scalar.copy, slice(0, P // 2))
-            cast_wu(
-                1, u, lambda dst, src: nc.gpsimd.tensor_scalar(dst, src, 1.0, 0.0, ALU.mult, ALU.add), slice(P // 2, P)
-            )
-        pair(0)
-        pair_rest(0)
+            cast_wu(1, u, gpsimd_cast, slice(P // 2, P))
+        weave_gpsimd(0)
+        weave_scalar(0)
         quantize_wu(1, 1)
         for s in range(2):
             project(1, 1, TH * s, TH, 6 + s)
             nc.scalar.copy(singles[:, :, TH * s : TH * (s + 1)], banks[6 + s][:].rearrange("p (i t) -> p i t", i=2))
+        join_singles(0)
         gather(1, (0,))
         quantize_wu(1, 0)
         for s in range(2):
             project(1, 0, TH * s, TH, s)
         gather(1, (1,))
         quantize_x(0)
-        pair(1)
-        gather_share(3, 0)
-        gather_share(3, 1)
+        weave_gpsimd(1)
+        gather_singles(3, 0)
+        gather_singles(3, 1)
         for s in range(2):
-            fill(1, 0, TH * s, TH, s, nc.scalar.copy)
+            fill_window(1, 0, TH * s, TH, s, nc.scalar.copy)
+
         gather(2)
         quantize_x(1)
-        pair(2)
-        pair_rest(2)
-        gather_share(4, 0)
-        gather(3)
-        quantize_x(2)
-        pair(3)
-        pair_rest(3)
-        gather_share(4, 1)
-        gather(4)
-        quantize_x(3)
-        pair(4)
-        pair_rest(4)
+        for i in (2, 3):
+            weave_gpsimd(i)
+            weave_scalar(i)
+            gather_singles(4, i - 2)
+            gather(i + 1)
+            quantize_x(i)
+        weave_gpsimd(4)
+        weave_scalar(4)
         gather(5)
-        gather_share(5, 0)
-        gather_share(5, 1)
+        gather_singles(5, 0)
+        gather_singles(5, 1)
         quantize_x(4)
-        weave(5, nc.gpsimd.tensor_copy, slice(0, 2 * C))
-        weave(5, nc.gpsimd.tensor_copy, slice(2 * C, WOVEN[5]))
-        pair_rest(5)
+        weave_gpsimd(5)
+        join_singles(1)
+        weave_scalar(5)
         gather(6)
         quantize_x(5)
-        ahead = [paired[i][:, 4 * WOVEN[i] : 4 * WOVEN[i] + 2 * C].bitcast(F32) for i in (6, 7)]
-        rest = keep.tile([P, 10 * C], F32, name="rest")
+
+        first_relu = [woven[i][:, 4 * GPSIMD_WEAVES[i] : 4 * GPSIMD_WEAVES[i] + 2 * C].bitcast(F32) for i in (6, 7)]
+        relus = keep.tile([P, 10 * C], F32, name="relus")
+
+        def rectify_group(g):
+            e0, others = 4 * g, relus[:, 3 * C * g : 3 * C * (g + 1)]
+            rectify(0, e0, e0, 1, first_relu[g])
+            rectify(0, e0, e0 + 1, 1, others[:, :C])
+            square(0, e0, 1, first_relu[g])
+            rectify(0, e0, e0 + 2, 2, others[:, C:])
+            return others
+
         multiply(0, 0, 4)
-        rectify(0, 0, 0, 1, ahead[0])
-        rectify(0, 0, 1, 1, rest[:, :C])
-        square(0, 0, 1, ahead[0])
-        rectify(0, 0, 2, 2, rest[:, C : 3 * C])
-        fill(1, 1, 0, TH, 6, nc.scalar.copy)
-        square(0, 1, 3, rest[:, : 3 * C])
-        fill(1, 1, TH, TH, 7, nc.scalar.copy)
+        square(0, 1, 3, rectify_group(0))
         multiply(1, 0, 4)
-        multiply(0, 4, 4)
-        multiply(1, 4, 4)
-        multiply(0, 8, 4)
-        multiply(1, 8, 4)
-        pair(6)
-        pair_rest(6)
+        for e0 in (4, 8):
+            for h in range(HALVES):
+                multiply(h, e0, 4)
+        weave_gpsimd(6)
+        weave_scalar(6)
         gather(7)
         quantize_x(6)
-        rectify(0, 4, 4, 1, ahead[1])
-        rectify(0, 4, 5, 1, rest[:, 3 * C : 4 * C])
-        square(0, 4, 1, ahead[1])
-        rectify(0, 4, 6, 2, rest[:, 4 * C : 6 * C])
-        pair(7)
-        pair_rest(7)
-        square(0, 5, 3, rest[:, 3 * C : 6 * C])
+        others = rectify_group(1)
+        weave_gpsimd(7)
+        weave_scalar(7)
+        square(0, 5, 3, others)
         gather(8)
         quantize_x(7)
-        third = rest[:, 6 * C :]
+        third = relus[:, 6 * C :]
         rectify(0, 8, 8, 4, third)
-        pair(8)
+        weave_gpsimd(8)
         gather(9)
         quantize_x(8)
         quantize_x(9)
-        fresh = keep.tile([P, 3 * C], F32, name="fresh")
+        fourth = keep.tile([P, 3 * C], F32, name="fourth")
         multiply(0, 12, 2)
-        rectify(0, 12, 12, 2, fresh[:, : 2 * C])
         square(0, 8, 4, third)
+        rectify(0, 12, 12, 2, fourth[:, : 2 * C])
         multiply(0, 14, 1)
-        rectify(0, 14, 14, 1, fresh[:, 2 * C :])
-        square(0, 12, 2, fresh[:, : 2 * C])
+        rectify(0, 14, 14, 1, fourth[:, 2 * C :])
+        square(0, 12, 2, fourth[:, : 2 * C])
         multiply(0, 15, 1)
         multiply(1, 12, 4)
         spread = late[:].rearrange("p (g c) -> p g c", g=16)[:, :, :8]
         nc.scalar.activation(
             spread, banks[BANK_OF[0, 15]][:, :C].rearrange("p (g c) -> p g c", g=16), ACT.Relu, bias=bias[:, 0, 15:16]
         )
-        square(0, 14, 1, fresh[:, 2 * C :])
+        square(0, 14, 1, fourth[:, 2 * C :])
         nc.scalar.activation(y[0][:, 15 * C :].rearrange("p (g c) -> p g c", g=16), spread, ACT.Square)
-        first = stage[9][:, : 8 * C].bitcast(F32)
+
+        waiting = runs[9][:, : 8 * C].bitcast(F32)
         for e in range(4):
             slots = slice(C * e, C * (e + 1))
             nc.vector.tensor_scalar(
-                first[:, slots], banks[BANK_OF[1, 0]][:, slots], bias[:, 1, e : e + 1], 0.0, ALU.add, ALU.max
+                waiting[:, slots], banks[BANK_OF[1, 0]][:, slots], bias[:, 1, e : e + 1], 0.0, ALU.add, ALU.max
             )
-        nc.vector.tensor_tensor(y[1][:, : 4 * C], first, first, ALU.mult)
+        nc.vector.tensor_tensor(y[1][:, : 4 * C], waiting, waiting, ALU.mult)
         for e0 in (4, 8, 12):
-            activate(1, e0, 4, late[:, C * (e0 - 4) : C * e0])
+            positive = late[:, C * (e0 - 4) : C * e0]
+            rectify(1, e0, e0, 4, positive)
+            square(1, e0, 4, positive)
 
         def fetch(h, r, cols):
             prod = keep.tile([P, cols.stop - cols.start], F32, name="prod%d%d_%d" % (h, r, cols.start))
@@ -372,7 +369,9 @@ def tile_moe_prv_lin_relu2_kernel(
             )
             return prod
 
-        def turn(turned, prod, blk0, start, stop):
+        turned = [banks[4 + blk][:, :P] for blk in range(T // P)]
+
+        def add_turned(prod, blk0, start, stop):
             for i in range(prod.shape[1] // P):
                 nc.tensor.matmul(
                     turned[blk0 + i],
@@ -383,32 +382,32 @@ def tile_moe_prv_lin_relu2_kernel(
                     is_transpose=True,
                 )
 
-        def turn_back(turned, summed, nb):
-            back = banks[nb][:, : len(turned) * P]
-            for i, block in enumerate(turned):
+        def turn_back(blocks, summed, bank):
+            back = banks[bank][:, : len(blocks) * P]
+            for i, block in enumerate(blocks):
                 cols = slice(P * i, P * (i + 1))
                 nc.scalar.copy(summed[:, cols], block)
                 nc.tensor.transpose(back[:, cols], summed[:, cols], ident[:])
             return back
 
         whole = slice(0, T)
-        halves = [slice(0, TH), slice(TH, T)]
-        turned = [banks[4 + blk][:, :P] for blk in range(T // P)]
         for r in range(TOP):
-            turn(turned, fetch(0, r, whole), 0, r == 0, r == TOP - 1)
+            add_turned(fetch(0, r, whole), 0, r == 0, r == TOP - 1)
         back = turn_back(turned, late[:, 8 * C :], 3)
         result = keep.tile([P, T], F32, name="result0")
         nc.scalar.copy(result[:], back)
         nc.sync.dma_start(out[:P, :], result[:])
 
         for r in range(TOP - 2):
-            turn(turned, fetch(1, r, whole), 0, r == 0, False)
+            add_turned(fetch(1, r, whole), 0, r == 0, False)
+        pieces = [slice(0, TH), slice(TH, TH + P), slice(TH + P, T)]
         partial = []
-        for s, cols in enumerate(halves):
-            turn(turned, fetch(1, TOP - 2, cols), 2 * s, False, True)
-            partial.append(turn_back(turned[2 * s : 2 * s + 2], late[:, TH * s : TH * (s + 1)], s))
-        last = [fetch(1, TOP - 1, cols) for cols in halves]
-        for s, cols in ((0, slice(0, TH)), (1, slice(0, P)), (1, slice(P, TH))):
-            result = keep.tile([P, cols.stop - cols.start], F32, name="result1%d_%d" % (s, cols.start))
-            nc.vector.tensor_tensor(result[:], partial[s][:, cols], last[s][:, cols], ALU.add)
-            nc.sync.dma_start(out[P:, TH * s + cols.start : TH * s + cols.stop], result[:])
+        for s, cols in enumerate(pieces):
+            add_turned(fetch(1, TOP - 2, cols), cols.start // P, False, True)
+            partial.append(turn_back(turned[cols.start // P : cols.stop // P], late[:, cols], s))
+        last = [fetch(1, TOP - 1, slice(TH * s, TH * (s + 1))) for s in range(2)]
+        for s, cols in enumerate(pieces):
+            result = keep.tile([P, cols.stop - cols.start], F32, name="result1%d" % s)
+            own = slice(cols.start % TH, cols.start % TH + cols.stop - cols.start)
+            nc.vector.tensor_tensor(result[:], partial[s], last[cols.start // TH][:, own], ALU.add)
+            nc.sync.dma_start(out[P:, cols], result[:])

@@ -23,11 +23,15 @@ RUN = 2 * 4 * C
 WINDOW = 704
 TOKEN_LOADS = [(0, 256), (256, 128), (384, 128)]
 TOKEN_PIECES = [(0, 0), (0, 128), (1, 256), (2, 384)]
-UNITS = [(0, 0, 4), (0, 4, 4), (0, 8, 4), (1, 0, 4), (1, 4, 4), (1, 8, 4), (0, 12, 4), (1, 12, 2), (1, 14, 1), (1, 15, 1)]
-LAST_UNIT = len(UNITS) - 1
-SCALAR_GATHERS = (3, 4, 5)
+UNITS = [(0, 0, 4), (0, 4, 4), (0, 8, 4), (0, 12, 4), (1, 0, 4), (1, 4, 4), (1, 8, 4), (1, 12, 2), (1, 14, 1), (1, 15, 1)]
 SHORT_SHARE = 320
-GPSIMD_WEAVES = [2 * C, 4 * C, SHORT_SHARE, SHORT_SHARE, SHORT_SHARE, 2 * C, SHORT_SHARE, C, C]
+HALF = RUN // 2
+LAP = 32
+RAW, FREE, SECOND = 0, 4 * RUN, 5 * RUN + LAP
+WOVEN1 = SECOND + 2 * RUN - LAP
+TWINS0 = WOVEN1 + 2 * RUN - LAP
+ROOM = TWINS0 + 4 * RUN
+SPARE_SHARE = 224
 BANK_OF = {(0, 0): 2, (1, 0): 3, (0, 4): 4, (1, 4): 0, (0, 8): 5, (1, 8): 1, (0, 12): 6, (0, 14): 7, (0, 15): 4, (1, 12): 2}
 FLOPS = 2 * M * K * T + 2 * K * N * S
 
@@ -44,12 +48,13 @@ def tile_moe_prv_lin_relu2_kernel(
         offs_t = keep.tile([P, S // 16], U16, name="offs_t")
         pos_t = [keep.tile([P, T // 16], U16, name="pos_t%d" % r) for r in range(TOP)]
 
-        spare = [keep.tile([P, 2 * RUN], BF16, name="spare%d" % i, align_bytes=64) for i in range(5)]
-        shifted = keep.tile([P, T + 2 * RUN], BF16, name="shifted", align_bytes=64)
-        windows = {(1, 1): shifted[:, : 2 * T]}
-        for a, u in ((0, 0), (0, 1), (1, 0)):
+        room = keep.tile([P, ROOM], BF16, name="room", align_bytes=64)
+        windows = {}
+        for a, u in ((0, 0), (1, 0), (1, 1)):
             windows[a, u] = keep.tile([P, 2 * WINDOW], BF16, name="win%d%d" % (a, u), align_bytes=64)[:]
             nc.vector.memset(windows[a, u][:, 2 * T :].bitcast(U32), 0)
+        singles = keep.tile([P, 2, WINDOW], BF16, name="singles", align_bytes=64)
+        nc.vector.memset(singles[:, :, T:].bitcast(U32), 0)
         w_plane = keep.tile([P, E * PASSES * N], U8, name="w_plane", align_bytes=64)
         nc.vector.memset(w_plane[:].bitcast(I32), 0)
         ident = keep.tile([P, P], F32, name="ident")
@@ -57,11 +62,11 @@ def tile_moe_prv_lin_relu2_kernel(
 
         wu_rows = wu.rearrange("(p j) k -> p j k", j=4)
         uT_rows = uT.rearrange("(p j) t -> p j t", j=4)
-        wu_room, wu_raw, u_raw = {}, {}, {}
+        first_raw = keep.tile([P, 4, 512], F32, name="first_raw", align_bytes=64)
+        wu_raw = [first_raw[:], room[:, RAW : RAW + 4 * RUN].bitcast(F32).rearrange("p (j x) -> p j x", j=4)]
+        u_raw = {}
 
         def load_wu(a):
-            wu_room[a] = keep.tile([P, 4 + a, 512], F32, name="wu_raw%d" % a, align_bytes=64)
-            wu_raw[a] = wu_room[a][:, :4, :]
             nc.sync.dma_start(wu_raw[a], wu_rows[:, :, 512 * a : 512 * (a + 1)])
 
         load_wu(0)
@@ -92,13 +97,10 @@ def tile_moe_prv_lin_relu2_kernel(
         for r in range(TOP):
             nc.sync.dma_start(gate_t[r][:], gate[r, :P, :])
 
-        odd = wu_room[1][:].rearrange("p j c -> p (j c)").bitcast(BF16)
-        even = keep.tile([P, 3 * RUN], BF16, name="even", align_bytes=64)
-        runs = [even[:, : 2 * RUN], odd[:, 2 * RUN : 4 * RUN], even[:, : 2 * RUN]] + [odd[:, 3 * RUN :], even[:, RUN:]] * 4
-
         wu_codes, wu_plane = {}, {}
-        second_bf = keep.tile([P, 2 * RUN], BF16, name="second_bf", align_bytes=64)
-        wu_bf = {(0, 0): even[:, :RUN], (0, 1): even[:, RUN : 2 * RUN], (1, 0): second_bf[:, :RUN], (1, 1): second_bf[:, RUN:]}
+        first_bf = keep.tile([P, 2 * RUN], BF16, name="first_bf", align_bytes=64)
+        both_bf = [first_bf[:], room[:, SECOND : SECOND + 2 * RUN]]
+        wu_bf = {(a, u): both_bf[a][:, RUN * u : RUN * (u + 1)] for a in range(PASSES) for u in range(2)}
 
         def cast_wu(a, u, copy, words=slice(0, P)):
             copy(
@@ -109,10 +111,14 @@ def tile_moe_prv_lin_relu2_kernel(
         def gpsimd_cast(dst, src):
             nc.gpsimd.tensor_scalar(dst, src, 1.0, 0.0, ALU.mult, ALU.add)
 
-        def quantize_wu(a, u):
-            wu_codes[a, u] = keep.tile([P, 2 * P], U32, name="wu_codes%d%d" % (a, u), align_bytes=64)
-            wu_plane[a, u] = keep.tile([P, 2 * P], U8, name="wu_plane%d%d" % (a, u), align_bytes=64)
-            nc.vector.quantize_mx(wu_codes[a, u][:].bitcast(FP8X4), wu_plane[a, u][:], wu_bf[a, u])
+        def quantize_wu(a, pairs):
+            n = 2 * P * len(pairs)
+            codes = keep.tile([P, n], U32, name="wu_codes%d%d" % (a, pairs[0]), align_bytes=64)
+            plane = keep.tile([P, n], U8, name="wu_plane%d%d" % (a, pairs[0]), align_bytes=64)
+            nc.vector.quantize_mx(codes[:].bitcast(FP8X4), plane[:], both_bf[a][:, RUN * pairs[0] : RUN * (pairs[-1] + 1)])
+            for k, u in enumerate(pairs):
+                wu_codes[a, u] = codes[:, 2 * P * k : 2 * P * (k + 1)]
+                wu_plane[a, u] = plane[:, 2 * P * k : 2 * P * (k + 1)]
 
         u_codes = keep.tile([P, T], U32, name="u_codes", align_bytes=64)
         u_plane = keep.tile([P, T], U8, name="u_plane", align_bytes=64)
@@ -149,7 +155,7 @@ def tile_moe_prv_lin_relu2_kernel(
 
         cast_wu(0, 0, nc.vector.tensor_copy)
         cast_wu(0, 1, nc.scalar.copy)
-        quantize_wu(0, 0)
+        quantize_wu(0, (0,))
         cast_u(0, nc.scalar.copy)
         cast_u(1, nc.vector.tensor_copy)
         quantize_u(0)
@@ -157,76 +163,88 @@ def tile_moe_prv_lin_relu2_kernel(
         quantize_u(1)
         cast_u(3, nc.scalar.copy)
         quantize_u(2)
-        quantize_wu(0, 1)
+        quantize_wu(0, (1,))
         quantize_u(3)
         for s in range(T // P):
             project(0, 0, P * s, P, s)
             fill_window(0, 0, P * s, P, s, nc.scalar.copy if s % 2 else nc.vector.tensor_copy)
         for s in range(2):
             project(0, 1, TH * s, TH, 4 + s)
-            fill_window(0, 1, TH * s, TH, 4 + s, nc.scalar.copy)
+            nc.scalar.copy(singles[:, :, TH * s : TH * (s + 1)], banks[4 + s][:].rearrange("p (i t) -> p i t", i=2))
 
         x_codes, x_plane = {}, {}
-        singles = keep.tile([P, 2, T], BF16, name="singles", align_bytes=64)
+        y = [keep.tile([P, S], F32, name="y%d" % h, align_bytes=64) for h in range(HALVES)]
         late = keep.tile([P, 12 * C], F32, name="late")
+        even = keep.tile([P, 2 * RUN + HALF], BF16, name="even", align_bytes=64)
+        odd = keep.tile([P, 2 * RUN], BF16, name="odd", align_bytes=64)
+        runs = [
+            (even, 0, RUN),
+            (odd, 0, RUN),
+            (room, FREE, SECOND - LAP),
+            (room, RAW, SECOND + RUN - LAP),
+            (even, 0, RUN),
+            (odd, 0, RUN),
+            (even, 0, RUN),
+            (odd, 0, HALF),
+            (even, HALF, RUN + HALF),
+        ]
+        lapped = keep.tile([P, 7 * RUN - 2 * LAP], BF16, name="lapped", align_bytes=64)
+        twins = [room[:, TWINS0:], lapped[:, 2 * RUN - LAP : 6 * RUN - LAP]]
+        spare = keep.tile([P, 2 * RUN - LAP], BF16, name="spare", align_bytes=64)
         woven = [
-            odd[:, : 2 * RUN],
-            spare[2][:],
-            spare[3][:],
-            spare[0][:],
-            shifted[:, T:],
-            spare[3][:],
-            spare[1][:],
-            spare[4][:, :RUN],
-            runs[7][:, 4 * C : 8 * C],
-            runs[9][:, : 4 * C],
+            both_bf[1],
+            room[:, WOVEN1 : WOVEN1 + 2 * RUN],
+            twins[0][:, : 2 * RUN],
+            twins[1][:, : 2 * RUN],
+            lapped[:, : 2 * RUN],
+            twins[0][:, 2 * RUN :],
+            twins[1][:, 2 * RUN :],
+            spare[:, RUN - LAP :],
+            y[0][:, 8 * C : 10 * C].bitcast(BF16),
+            odd[:, :HALF],
         ]
 
         def slots_of(s0, ns):
             return offs_t[:, s0 // 16 : (s0 + ns) // 16]
 
-        def picked(i):
-            words = runs[i][:, : 4 * UNITS[i][2] * C].bitcast(U32)
-            return words.rearrange("p (c u) -> p u c" if i == LAST_UNIT else "p (u c) -> p u c", u=2)
-
         def gather(i, pairs=(0, 1)):
             a, e0, ne = UNITS[i]
-            for u in (0,) if i in SCALAR_GATHERS else pairs:
-                nc.vector.tensor_copy(picked(i)[:, u, :], windows[a, u].bitcast(U32).indirect(slots_of(e0 * C, ne * C)))
+            for u in pairs:
+                at = runs[i][1 + u]
+                nc.vector.tensor_copy(
+                    runs[i][0][:, at : at + 2 * ne * C].bitcast(U32),
+                    windows[a, u].bitcast(U32).indirect(slots_of(e0 * C, ne * C)),
+                )
 
-        def gather_singles(i, half):
+        def gather_woven(i):
             a, e0, ne = UNITS[i]
-            ns = ne * C // 2
-            pairs = runs[i][:, 2 * ns * (2 + half) : 2 * ns * (3 + half)].rearrange("p (c i) -> p c i", i=2)
+            words = woven[i].bitcast(U32).rearrange("p (c u) -> p u c", u=2)
+            for u in range(2):
+                nc.vector.tensor_copy(words[:, u, :], windows[a, u].bitcast(U32).indirect(slots_of(e0 * C, ne * C)))
+
+        def gather_singles(i):
+            a, e0, ne = UNITS[i]
+            at = runs[i][2]
+            pairs = runs[i][0][:, at : at + 2 * ne * C].rearrange("p (c i) -> p c i", i=2)
             for k in range(2):
-                nc.scalar.activation(pairs[:, :, k], singles[:, k, :].indirect(slots_of(e0 * C + ns * half, ns)), ACT.Copy)
+                nc.scalar.activation(pairs[:, :, k], singles[:, k, :].indirect(slots_of(e0 * C, ne * C)), ACT.Copy)
 
-        def join_singles(s):
-            nc.gpsimd.tensor_copy(
-                windows[1, 1][:, 2 * TH * s : 2 * TH * (s + 1)].rearrange("p (t i) -> p t i", i=2),
-                singles[:, :, TH * s : TH * (s + 1)].rearrange("p i t -> p t i"),
-            )
-
-
-        def weave(i, copy, slots):
+        def weave(i, copy, s0, ns):
+            tile, first, second = runs[i]
             copy(
-                woven[i].bitcast(U32).rearrange("p (c u) -> p c u", u=2)[:, slots, :],
-                picked(i).rearrange("p u c -> p c u")[:, slots, :],
+                woven[i][:, 4 * s0 : 4 * (s0 + ns)].bitcast(U32).rearrange("p (c u) -> p c u", u=2),
+                tile[:, first : 2 * second - first].bitcast(U32).rearrange("p (u x) -> p x u", u=2)[:, s0 : s0 + ns, :],
             )
 
-        def weave_gpsimd(i):
-            weave(i, nc.gpsimd.tensor_copy, slice(0, GPSIMD_WEAVES[i]))
+        def quantize_x(units, source):
+            n = sum(UNITS[i][2] for i in units) * C
+            codes = keep.tile([P, n], U32, name="x_codes%d" % units[0], align_bytes=64)
+            plane = keep.tile([P, n], U8, name="x_plane%d" % units[0], align_bytes=64)
+            nc.vector.quantize_mx(codes[:].bitcast(FP8X4), plane[:], source)
+            for k, i in enumerate(units):
+                cols = slice(n // len(units) * k, n // len(units) * (k + 1))
+                x_codes[i], x_plane[i] = codes[:, cols], plane[:, cols]
 
-        def weave_scalar(i):
-            weave(i, nc.scalar.copy, slice(GPSIMD_WEAVES[i], UNITS[i][2] * C))
-
-        def quantize_x(i):
-            n = UNITS[i][2] * C
-            x_codes[i] = keep.tile([P, n], U32, name="x_codes%d" % i, align_bytes=64)
-            x_plane[i] = keep.tile([P, n], U8, name="x_plane%d" % i, align_bytes=64)
-            nc.vector.quantize_mx(x_codes[i][:].bitcast(FP8X4), x_plane[i][:], woven[i])
-
-        y = [keep.tile([P, S], F32, name="y%d" % h) for h in range(HALVES)]
         unit_of = {(a, e): i for i, (a, e0, ne) in enumerate(UNITS) for e in range(e0, e0 + ne)}
 
         def multiply(h, e0, ne):
@@ -258,105 +276,78 @@ def tile_moe_prv_lin_relu2_kernel(
         def square(h, e0, ne, positive):
             nc.scalar.activation(y[h][:, e0 * C : (e0 + ne) * C], positive, ACT.Square)
 
-        gather(0)
-        for u in (1, 0):
-            cast_wu(1, u, nc.scalar.copy, slice(0, P // 2))
-            cast_wu(1, u, gpsimd_cast, slice(P // 2, P))
-        weave_gpsimd(0)
-        weave_scalar(0)
-        quantize_wu(1, 1)
+        gp = nc.gpsimd.tensor_copy
+        W = 4 * C
+        for i in range(3):
+            gather(i, (0,))
+        gather_singles(0)
+        gather_singles(1)
+        for u in range(2):
+            cast_wu(1, u, gpsimd_cast)
+        quantize_wu(1, (0, 1))
+        gather(3, (0,))
         for s in range(2):
-            project(1, 1, TH * s, TH, 6 + s)
-            nc.scalar.copy(singles[:, :, TH * s : TH * (s + 1)], banks[6 + s][:].rearrange("p (i t) -> p i t", i=2))
-        join_singles(0)
-        gather(1, (0,))
-        quantize_wu(1, 0)
+            project(1, 0, TH * s, TH, 6 + s)
+            fill_window(1, 0, TH * s, TH, 6 + s, nc.vector.tensor_copy if s else nc.scalar.copy)
         for s in range(2):
-            project(1, 0, TH * s, TH, s)
-        gather(1, (1,))
-        quantize_x(0)
-        weave_gpsimd(1)
-        gather_singles(3, 0)
-        gather_singles(3, 1)
-        for s in range(2):
-            fill_window(1, 0, TH * s, TH, s, nc.scalar.copy)
-
-        gather(2)
-        quantize_x(1)
-        for i in (2, 3):
-            weave_gpsimd(i)
-            weave_scalar(i)
-            gather_singles(4, i - 2)
-            gather(i + 1)
-            quantize_x(i)
-        weave_gpsimd(4)
-        weave_scalar(4)
+            project(1, 1, TH * s, TH, s)
+            fill_window(1, 1, TH * s, TH, s, nc.scalar.copy)
+        weave(0, gp, 0, W)
+        quantize_x((0,), woven[0])
+        weave(1, gp, 0, W)
+        gather(4)
+        gather_singles(2)
+        quantize_x((1,), woven[1])
+        weave(4, gp, 0, W)
+        weave(2, gp, 0, SPARE_SHARE)
         gather(5)
-        gather_singles(5, 0)
-        gather_singles(5, 1)
-        quantize_x(4)
-        weave_gpsimd(5)
-        join_singles(1)
-        weave_scalar(5)
+        gather_singles(3)
+        quantize_x((4,), woven[4])
+        weave(5, gp, 0, W)
+        weave(3, gp, 0, SPARE_SHARE)
         gather(6)
-        quantize_x(5)
-
-        first_relu = [woven[i][:, 4 * GPSIMD_WEAVES[i] : 4 * GPSIMD_WEAVES[i] + 2 * C].bitcast(F32) for i in (6, 7)]
-        relus = keep.tile([P, 10 * C], F32, name="relus")
-
-        def rectify_group(g):
-            e0, others = 4 * g, relus[:, 3 * C * g : 3 * C * (g + 1)]
-            rectify(0, e0, e0, 1, first_relu[g])
-            rectify(0, e0, e0 + 1, 1, others[:, :C])
-            square(0, e0, 1, first_relu[g])
-            rectify(0, e0, e0 + 2, 2, others[:, C:])
-            return others
-
-        multiply(0, 0, 4)
-        square(0, 1, 3, rectify_group(0))
-        multiply(1, 0, 4)
+        weave(2, nc.scalar.copy, SPARE_SHARE, W - SPARE_SHARE)
+        weave(3, nc.scalar.copy, SPARE_SHARE, W - SPARE_SHARE)
+        quantize_x((2, 5), twins[0])
+        relus = [lapped[:, 6 * RUN - 2 * LAP :].bitcast(F32), spare[:, :RUN].bitcast(F32)]
+        for h in range(HALVES):
+            multiply(h, 0, 4)
+        rectify(0, 0, 0, 4, relus[0])
+        square(0, 0, 4, relus[0])
+        weave(6, gp, 0, SHORT_SHARE)
+        weave(6, nc.scalar.copy, SHORT_SHARE, W - SHORT_SHARE)
+        rectify(1, 0, 0, 4, relus[1])
+        square(1, 0, 4, relus[1])
+        gather(7)
+        quantize_x((3, 6), twins[1])
+        weave(7, gp, C, C)
+        weave(7, nc.scalar.copy, 0, C)
+        gather(8)
+        others = keep.tile([P, 11 * C], F32, name="others")
         for e0 in (4, 8):
             for h in range(HALVES):
                 multiply(h, e0, 4)
-        weave_gpsimd(6)
-        weave_scalar(6)
-        gather(7)
-        quantize_x(6)
-        others = rectify_group(1)
-        weave_gpsimd(7)
-        weave_scalar(7)
-        square(0, 5, 3, others)
-        gather(8)
-        quantize_x(7)
-        third = relus[:, 6 * C :]
-        rectify(0, 8, 8, 4, third)
-        weave_gpsimd(8)
-        gather(9)
-        quantize_x(8)
-        quantize_x(9)
-        fourth = keep.tile([P, 3 * C], F32, name="fourth")
+        rectify(0, 4, 4, 4, others[:, :W])
+        square(0, 4, 4, others[:, :W])
+        rectify(0, 8, 8, 4, others[:, W : 2 * W])
+        quantize_x((7,), woven[7])
+        weave(8, gp, 0, C)
+        gather_woven(9)
+        quantize_x((8,), woven[8])
+        quantize_x((9,), woven[9])
         multiply(0, 12, 2)
-        square(0, 8, 4, third)
-        rectify(0, 12, 12, 2, fourth[:, : 2 * C])
+        rectify(0, 12, 12, 2, others[:, 2 * W : 10 * C])
         multiply(0, 14, 1)
-        rectify(0, 14, 14, 1, fourth[:, 2 * C :])
-        square(0, 12, 2, fourth[:, : 2 * C])
+        rectify(0, 14, 14, 1, others[:, 10 * C :])
         multiply(0, 15, 1)
         multiply(1, 12, 4)
         spread = late[:].rearrange("p (g c) -> p g c", g=16)[:, :, :8]
         nc.scalar.activation(
             spread, banks[BANK_OF[0, 15]][:, :C].rearrange("p (g c) -> p g c", g=16), ACT.Relu, bias=bias[:, 0, 15:16]
         )
-        square(0, 14, 1, fourth[:, 2 * C :])
+        nc.vector.tensor_tensor(y[0][:, 8 * C : 14 * C], others[:, W : 10 * C], others[:, W : 10 * C], ALU.mult)
+        square(0, 14, 1, others[:, 10 * C :])
         nc.scalar.activation(y[0][:, 15 * C :].rearrange("p (g c) -> p g c", g=16), spread, ACT.Square)
-
-        waiting = runs[9][:, : 8 * C].bitcast(F32)
-        for e in range(4):
-            slots = slice(C * e, C * (e + 1))
-            nc.vector.tensor_scalar(
-                waiting[:, slots], banks[BANK_OF[1, 0]][:, slots], bias[:, 1, e : e + 1], 0.0, ALU.add, ALU.max
-            )
-        nc.vector.tensor_tensor(y[1][:, : 4 * C], waiting, waiting, ALU.mult)
         for e0 in (4, 8, 12):
             positive = late[:, C * (e0 - 4) : C * e0]
             rectify(1, e0, e0, 4, positive)

@@ -27,11 +27,11 @@ UNITS = [(0, 0, 4), (0, 4, 4), (0, 8, 4), (0, 12, 4), (1, 0, 4), (1, 4, 4), (1, 
 SHORT_SHARE = 320
 HALF = RUN // 2
 LAP = 32
-RAW, FREE, SECOND = 0, 4 * RUN, 5 * RUN + LAP
+RAW, SECOND = HALF, 2 * RUN + HALF + LAP
 WOVEN1 = SECOND + 2 * RUN - LAP
 TWINS0 = WOVEN1 + 2 * RUN - LAP
 ROOM = TWINS0 + 4 * RUN
-SPARE_SHARE = 224
+SPARE_SHARE = 160
 BANK_OF = {(0, 0): 2, (1, 0): 3, (0, 4): 4, (1, 4): 0, (0, 8): 5, (1, 8): 1, (0, 12): 6, (0, 14): 7, (0, 15): 4, (1, 12): 2}
 FLOPS = 2 * M * K * T + 2 * K * N * S
 
@@ -63,18 +63,16 @@ def tile_moe_prv_lin_relu2_kernel(
         wu_rows = wu.rearrange("(p j) k -> p j k", j=4)
         uT_rows = uT.rearrange("(p j) t -> p j t", j=4)
         first_raw = keep.tile([P, 4, 512], F32, name="first_raw", align_bytes=64)
-        wu_raw = [first_raw[:], room[:, RAW : RAW + 4 * RUN].bitcast(F32).rearrange("p (j x) -> p j x", j=4)]
+        early_raw = keep.tile([P, 4, 256], F32, name="early_raw", align_bytes=64)
+        second_raw = [early_raw[:], room[:, RAW : RAW + 2 * RUN].bitcast(F32).rearrange("p (j x) -> p j x", j=4)]
         u_raw = {}
-
-        def load_wu(a):
-            nc.sync.dma_start(wu_raw[a], wu_rows[:, :, 512 * a : 512 * (a + 1)])
-
-        load_wu(0)
+        nc.sync.dma_start(first_raw[:], wu_rows[:, :, :512])
         for s, (t0, nt) in enumerate(TOKEN_LOADS):
             u_raw[s] = keep.tile([P, 4, nt], F32, name="u_raw%d" % s)
             nc.sync.dma_start(u_raw[s][:], uT_rows[:, :, t0 : t0 + nt])
         nc.sync.dma_start(offs_t[:], offs)
-        load_wu(1)
+        for s in range(2):
+            nc.sync.dma_start(second_raw[s], wu_rows[:, :, 512 + 256 * s : 512 + 256 * (s + 1)])
         scale_rows = w_scales.rearrange("e a q n -> q (e a) n")
         for q in range(4):
             nc.sync.dma_start(
@@ -102,10 +100,10 @@ def tile_moe_prv_lin_relu2_kernel(
         both_bf = [first_bf[:], room[:, SECOND : SECOND + 2 * RUN]]
         wu_bf = {(a, u): both_bf[a][:, RUN * u : RUN * (u + 1)] for a in range(PASSES) for u in range(2)}
 
-        def cast_wu(a, u, copy, words=slice(0, P)):
+        def cast_wu(a, u, copy):
             copy(
-                wu_bf[a, u].rearrange("p (i m j) -> p m i j", i=2, j=4)[:, words],
-                wu_raw[a].rearrange("p j (m t) -> p m t j", t=4)[:, words, 2 * u : 2 * u + 2, :],
+                wu_bf[a, u].rearrange("p (i m j) -> p m i j", i=2, j=4),
+                first_raw[:].rearrange("p j (m t) -> p m t j", t=4)[:, :, 2 * u : 2 * u + 2, :],
             )
 
         def gpsimd_cast(dst, src):
@@ -180,8 +178,8 @@ def tile_moe_prv_lin_relu2_kernel(
         runs = [
             (even, 0, RUN),
             (odd, 0, RUN),
-            (room, FREE, SECOND - LAP),
-            (room, RAW, SECOND + RUN - LAP),
+            (room, 0, SECOND - LAP),
+            (room, RUN, SECOND + RUN - LAP),
             (even, 0, RUN),
             (odd, 0, RUN),
             (even, 0, RUN),
@@ -207,13 +205,14 @@ def tile_moe_prv_lin_relu2_kernel(
         def slots_of(s0, ns):
             return offs_t[:, s0 // 16 : (s0 + ns) // 16]
 
-        def gather(i, pairs=(0, 1)):
+        def gather(i, pairs=(0, 1), s0=0, ns=None):
             a, e0, ne = UNITS[i]
+            ns = ns or ne * C
             for u in pairs:
-                at = runs[i][1 + u]
+                at = runs[i][1 + u] + 2 * s0
                 nc.vector.tensor_copy(
-                    runs[i][0][:, at : at + 2 * ne * C].bitcast(U32),
-                    windows[a, u].bitcast(U32).indirect(slots_of(e0 * C, ne * C)),
+                    runs[i][0][:, at : at + 2 * ns].bitcast(U32),
+                    windows[a, u].bitcast(U32).indirect(slots_of(e0 * C + s0, ns)),
                 )
 
         def gather_woven(i):
@@ -278,17 +277,22 @@ def tile_moe_prv_lin_relu2_kernel(
 
         gp = nc.gpsimd.tensor_copy
         W = 4 * C
-        for i in range(3):
-            gather(i, (0,))
+        gather(0, (0,))
+        gather(1, (0,))
+        gather(2, (0,), 0, W // 2)
         gather_singles(0)
         gather_singles(1)
-        for u in range(2):
-            cast_wu(1, u, gpsimd_cast)
+        for s in range(2):
+            gpsimd_cast(
+                both_bf[1].rearrange("p (t m j) -> p m t j", t=4, j=4)[:, P // 2 * s : P // 2 * (s + 1)],
+                second_raw[s].rearrange("p j (m t) -> p m t j", t=4),
+            )
         quantize_wu(1, (0, 1))
+        gather(2, (0,), W // 2, W // 2)
         gather(3, (0,))
         for s in range(2):
             project(1, 0, TH * s, TH, 6 + s)
-            fill_window(1, 0, TH * s, TH, 6 + s, nc.vector.tensor_copy if s else nc.scalar.copy)
+            fill_window(1, 0, TH * s, TH, 6 + s, nc.scalar.copy if s else nc.vector.tensor_copy)
         for s in range(2):
             project(1, 1, TH * s, TH, s)
             fill_window(1, 1, TH * s, TH, s, nc.scalar.copy)
@@ -324,9 +328,9 @@ def tile_moe_prv_lin_relu2_kernel(
         weave(7, nc.scalar.copy, 0, C)
         gather(8)
         others = keep.tile([P, 11 * C], F32, name="others")
-        for e0 in (4, 8):
-            for h in range(HALVES):
-                multiply(h, e0, 4)
+        multiply(0, 4, 4)
+        multiply(1, 4, 4)
+        multiply(0, 8, 4)
         rectify(0, 4, 4, 4, others[:, :W])
         square(0, 4, 4, others[:, :W])
         rectify(0, 8, 8, 4, others[:, W : 2 * W])
@@ -340,13 +344,15 @@ def tile_moe_prv_lin_relu2_kernel(
         multiply(0, 14, 1)
         rectify(0, 14, 14, 1, others[:, 10 * C :])
         multiply(0, 15, 1)
+        multiply(1, 8, 4)
         multiply(1, 12, 4)
         spread = late[:].rearrange("p (g c) -> p g c", g=16)[:, :, :8]
         nc.scalar.activation(
             spread, banks[BANK_OF[0, 15]][:, :C].rearrange("p (g c) -> p g c", g=16), ACT.Relu, bias=bias[:, 0, 15:16]
         )
-        nc.vector.tensor_tensor(y[0][:, 8 * C : 14 * C], others[:, W : 10 * C], others[:, W : 10 * C], ALU.mult)
-        square(0, 14, 1, others[:, 10 * C :])
+        for e0, e1 in ((8, 12), (12, 15)):
+            positive = others[:, (e0 - 4) * C : (e1 - 4) * C]
+            nc.vector.tensor_tensor(y[0][:, e0 * C : e1 * C], positive, positive, ALU.mult)
         nc.scalar.activation(y[0][:, 15 * C :].rearrange("p (g c) -> p g c", g=16), spread, ACT.Square)
         for e0 in (4, 8, 12):
             positive = late[:, C * (e0 - 4) : C * e0]

@@ -24,14 +24,14 @@ WINDOW = 704
 TOKEN_LOADS = [(0, 256), (256, 128), (384, 128)]
 TOKEN_PIECES = [(0, 0), (0, 128), (1, 256), (2, 384)]
 UNITS = [(0, 0, 4), (0, 4, 4), (0, 8, 4), (0, 12, 4), (1, 0, 4), (1, 4, 4), (1, 8, 4), (1, 12, 2), (1, 14, 1), (1, 15, 1)]
-SHORT_SHARE = 320
+SHORT_SHARE = 288
 HALF = RUN // 2
 LAP = 32
 RAW, SECOND = HALF, 2 * RUN + HALF + LAP
 WOVEN1 = SECOND + 2 * RUN - LAP
 TWINS0 = WOVEN1 + 2 * RUN - LAP
 ROOM = TWINS0 + 4 * RUN
-SPARE_SHARE = 160
+SPARE_SHARE = 64
 BANK_OF = {(0, 0): 2, (1, 0): 3, (0, 4): 4, (1, 4): 0, (0, 8): 5, (1, 8): 1, (0, 12): 6, (0, 14): 7, (0, 15): 4, (1, 12): 2}
 FLOPS = 2 * M * K * T + 2 * K * N * S
 
@@ -172,7 +172,7 @@ def tile_moe_prv_lin_relu2_kernel(
 
         x_codes, x_plane = {}, {}
         y = [keep.tile([P, S], F32, name="y%d" % h, align_bytes=64) for h in range(HALVES)]
-        late = keep.tile([P, 12 * C], F32, name="late")
+        late = keep.tile([P, 14 * C], F32, name="late")
         even = keep.tile([P, 2 * RUN + HALF], BF16, name="even", align_bytes=64)
         odd = keep.tile([P, 2 * RUN], BF16, name="odd", align_bytes=64)
         runs = [
@@ -188,7 +188,7 @@ def tile_moe_prv_lin_relu2_kernel(
         ]
         lapped = keep.tile([P, 7 * RUN - 2 * LAP], BF16, name="lapped", align_bytes=64)
         twins = [room[:, TWINS0:], lapped[:, 2 * RUN - LAP : 6 * RUN - LAP]]
-        spare = keep.tile([P, 2 * RUN - LAP], BF16, name="spare", align_bytes=64)
+        spare = keep.tile([P, RUN + HALF - LAP], BF16, name="spare", align_bytes=64)
         woven = [
             both_bf[1],
             room[:, WOVEN1 : WOVEN1 + 2 * RUN],
@@ -197,7 +197,7 @@ def tile_moe_prv_lin_relu2_kernel(
             lapped[:, : 2 * RUN],
             twins[0][:, 2 * RUN :],
             twins[1][:, 2 * RUN :],
-            spare[:, RUN - LAP :],
+            spare[:, HALF - LAP :],
             y[0][:, 8 * C : 10 * C].bitcast(BF16),
             odd[:, :HALF],
         ]
@@ -313,15 +313,15 @@ def tile_moe_prv_lin_relu2_kernel(
         weave(2, nc.scalar.copy, SPARE_SHARE, W - SPARE_SHARE)
         weave(3, nc.scalar.copy, SPARE_SHARE, W - SPARE_SHARE)
         quantize_x((2, 5), twins[0])
-        relus = [lapped[:, 6 * RUN - 2 * LAP :].bitcast(F32), spare[:, :RUN].bitcast(F32)]
+        relus = [lapped[:, 6 * RUN - 2 * LAP :].bitcast(F32), spare[:, :HALF].bitcast(F32)]
         for h in range(HALVES):
             multiply(h, 0, 4)
         rectify(0, 0, 0, 4, relus[0])
         square(0, 0, 4, relus[0])
         weave(6, gp, 0, SHORT_SHARE)
         weave(6, nc.scalar.copy, SHORT_SHARE, W - SHORT_SHARE)
-        rectify(1, 0, 0, 4, relus[1])
-        square(1, 0, 4, relus[1])
+        rectify(1, 0, 0, 2, relus[1])
+        square(1, 0, 2, relus[1])
         gather(7)
         quantize_x((3, 6), twins[1])
         weave(7, gp, C, C)
@@ -354,8 +354,11 @@ def tile_moe_prv_lin_relu2_kernel(
             positive = others[:, (e0 - 4) * C : (e1 - 4) * C]
             nc.vector.tensor_tensor(y[0][:, e0 * C : e1 * C], positive, positive, ALU.mult)
         nc.scalar.activation(y[0][:, 15 * C :].rearrange("p (g c) -> p g c", g=16), spread, ACT.Square)
-        for e0 in (4, 8, 12):
-            positive = late[:, C * (e0 - 4) : C * e0]
+        rectify(1, 0, 2, 2, late[:, : 2 * C])
+        rectify(1, 4, 4, 4, late[:, 2 * C : 6 * C])
+        square(1, 2, 6, late[:, : 6 * C])
+        for e0 in (8, 12):
+            positive = late[:, C * (e0 - 2) : C * (e0 + 2)]
             rectify(1, e0, e0, 4, positive)
             square(1, e0, 4, positive)
 
@@ -390,7 +393,7 @@ def tile_moe_prv_lin_relu2_kernel(
         whole = slice(0, T)
         for r in range(TOP):
             add_turned(fetch(0, r, whole), 0, r == 0, r == TOP - 1)
-        back = turn_back(turned, late[:, 8 * C :], 3)
+        back = turn_back(turned, late[:, 10 * C :], 3)
         result = keep.tile([P, T], F32, name="result0")
         nc.scalar.copy(result[:], back)
         nc.sync.dma_start(out[:P, :], result[:])

@@ -94,6 +94,9 @@ def tile_moe_prv_lin_relu2_kernel(
         gate_t = [keep.tile([P, T], F32, name="gate%d" % r) for r in range(TOP)]
         for r in range(TOP):
             nc.sync.dma_start(gate_t[r][:], gate[r, :P, :])
+        gate_col = keep.tile([P, T // P], F32, name="gate_col")
+        with nc.allow_non_contiguous_dma(reason="one weight a partition and block of tokens"):
+            nc.sync.dma_start(gate_col[:], gate[TOP - 1, 0, :].rearrange("(g p) -> p g", p=P))
 
         wu_codes, wu_plane = {}, {}
         first_bf = keep.tile([P, 2 * RUN], BF16, name="first_bf", align_bytes=64)
@@ -172,7 +175,7 @@ def tile_moe_prv_lin_relu2_kernel(
 
         x_codes, x_plane = {}, {}
         y = [keep.tile([P, S], F32, name="y%d" % h, align_bytes=64) for h in range(HALVES)]
-        late = keep.tile([P, 14 * C], F32, name="late")
+        late = keep.tile([P, 12 * C], F32, name="late")
         even = keep.tile([P, 2 * RUN + HALF], BF16, name="even", align_bytes=64)
         odd = keep.tile([P, 2 * RUN], BF16, name="odd", align_bytes=64)
         runs = [
@@ -188,7 +191,7 @@ def tile_moe_prv_lin_relu2_kernel(
         ]
         lapped = keep.tile([P, 7 * RUN - 2 * LAP], BF16, name="lapped", align_bytes=64)
         twins = [room[:, TWINS0:], lapped[:, 2 * RUN - LAP : 6 * RUN - LAP]]
-        spare = keep.tile([P, RUN + HALF - LAP], BF16, name="spare", align_bytes=64)
+        spare = keep.tile([P, 2 * RUN - LAP], BF16, name="spare", align_bytes=64)
         woven = [
             both_bf[1],
             room[:, WOVEN1 : WOVEN1 + 2 * RUN],
@@ -197,7 +200,7 @@ def tile_moe_prv_lin_relu2_kernel(
             lapped[:, : 2 * RUN],
             twins[0][:, 2 * RUN :],
             twins[1][:, 2 * RUN :],
-            spare[:, HALF - LAP :],
+            spare[:, RUN - LAP :],
             y[0][:, 8 * C : 10 * C].bitcast(BF16),
             odd[:, :HALF],
         ]
@@ -313,15 +316,15 @@ def tile_moe_prv_lin_relu2_kernel(
         weave(2, nc.scalar.copy, SPARE_SHARE, W - SPARE_SHARE)
         weave(3, nc.scalar.copy, SPARE_SHARE, W - SPARE_SHARE)
         quantize_x((2, 5), twins[0])
-        relus = [lapped[:, 6 * RUN - 2 * LAP :].bitcast(F32), spare[:, :HALF].bitcast(F32)]
+        relus = [lapped[:, 6 * RUN - 2 * LAP :].bitcast(F32), spare[:, :RUN].bitcast(F32)]
         for h in range(HALVES):
             multiply(h, 0, 4)
         rectify(0, 0, 0, 4, relus[0])
         square(0, 0, 4, relus[0])
         weave(6, gp, 0, SHORT_SHARE)
         weave(6, nc.scalar.copy, SHORT_SHARE, W - SHORT_SHARE)
-        rectify(1, 0, 0, 2, relus[1])
-        square(1, 0, 2, relus[1])
+        rectify(1, 0, 0, 4, relus[1])
+        square(1, 0, 4, relus[1])
         gather(7)
         quantize_x((3, 6), twins[1])
         weave(7, gp, C, C)
@@ -354,11 +357,8 @@ def tile_moe_prv_lin_relu2_kernel(
             positive = others[:, (e0 - 4) * C : (e1 - 4) * C]
             nc.vector.tensor_tensor(y[0][:, e0 * C : e1 * C], positive, positive, ALU.mult)
         nc.scalar.activation(y[0][:, 15 * C :].rearrange("p (g c) -> p g c", g=16), spread, ACT.Square)
-        rectify(1, 0, 2, 2, late[:, : 2 * C])
-        rectify(1, 4, 4, 4, late[:, 2 * C : 6 * C])
-        square(1, 2, 6, late[:, : 6 * C])
-        for e0 in (8, 12):
-            positive = late[:, C * (e0 - 2) : C * (e0 + 2)]
+        for e0 in (4, 8, 12):
+            positive = late[:, C * (e0 - 4) : C * e0]
             rectify(1, e0, e0, 4, positive)
             square(1, e0, 4, positive)
 
@@ -382,30 +382,43 @@ def tile_moe_prv_lin_relu2_kernel(
                     is_transpose=True,
                 )
 
-        def turn_back(blocks, summed, bank):
+        def turn_back(blocks, summed, bank, beside=None):
             back = banks[bank][:, : len(blocks) * P]
             for i, block in enumerate(blocks):
                 cols = slice(P * i, P * (i + 1))
                 nc.scalar.copy(summed[:, cols], block)
-                nc.tensor.transpose(back[:, cols], summed[:, cols], ident[:])
+                if beside is not None:
+                    nc.tensor.matmul(back[:, cols], lhsT=beside[:, cols], rhs=ident[:], start=True, stop=False, is_transpose=True)
+                nc.tensor.matmul(
+                    back[:, cols], lhsT=summed[:, cols], rhs=ident[:], start=beside is None, stop=True, is_transpose=True
+                )
             return back
 
         whole = slice(0, T)
         for r in range(TOP):
             add_turned(fetch(0, r, whole), 0, r == 0, r == TOP - 1)
-        back = turn_back(turned, late[:, 10 * C :], 3)
+        plain = keep.tile([P, T], F32, name="plain")
+        weighted = keep.tile([P, T], F32, name="weighted")
+        nc.scalar.activation(plain[:], y[1][:].indirect(pos_t[TOP - 1][:]), ACT.Copy)
+        for blk in range(T // P):
+            cols = slice(P * blk, P * (blk + 1))
+            nc.tensor.transpose(banks[2][:, cols], plain[:, cols], ident[:])
+        back = turn_back(turned, late[:, 8 * C :], 3)
+        for blk in range(T // P):
+            cols = slice(P * blk, P * (blk + 1))
+            nc.scalar.activation(weighted[:, cols], banks[2][:, cols], ACT.Copy, scale=gate_col[:, blk : blk + 1])
         result = keep.tile([P, T], F32, name="result0")
         nc.scalar.copy(result[:], back)
         nc.sync.dma_start(out[:P, :], result[:])
 
-        for r in range(TOP - 2):
-            add_turned(fetch(1, r, whole), 0, r == 0, False)
+        add_turned(fetch(1, 0, whole), 0, True, False)
         pieces = [slice(0, TH), slice(TH, TH + P), slice(TH + P, T)]
         partial = []
         for s, cols in enumerate(pieces):
-            add_turned(fetch(1, TOP - 2, cols), cols.start // P, False, True)
-            partial.append(turn_back(turned[cols.start // P : cols.stop // P], late[:, cols], s))
-        last = [fetch(1, TOP - 1, slice(TH * s, TH * (s + 1))) for s in range(2)]
+            add_turned(fetch(1, 1, cols), cols.start // P, False, True)
+        for s, cols in enumerate(pieces):
+            partial.append(turn_back(turned[cols.start // P : cols.stop // P], late[:, cols], s, weighted[:, cols]))
+        last = [fetch(1, 2, slice(TH * s, TH * (s + 1))) for s in range(2)]
         for s, cols in enumerate(pieces):
             result = keep.tile([P, cols.stop - cols.start], F32, name="result1%d" % s)
             own = slice(cols.start % TH, cols.start % TH + cols.stop - cols.start)

from contextlib import ExitStack

import concourse.mybir as mybir
from concourse.masks import make_identity

F32 = mybir.dt.float32
BF16 = mybir.dt.bfloat16
I32 = mybir.dt.int32
U32 = mybir.dt.uint32
U16 = mybir.dt.uint16
U8 = mybir.dt.uint8
FP8X4 = mybir.dt.float8_e4m3fn_x4
ACT = mybir.ActivationFunctionType
ALU = mybir.AluOpType

P = 128
K, T, E, C, N, M, TOP = 1024, 512, 16, 128, 256, 512, 4
S = E * C
PASSES = K // 512
HALVES = N // P
TH = T // 2
RUN = 2 * 4 * C
WINDOW = 704
TOKEN_LOADS = [(0, 256), (256, 128), (384, 128)]
TOKEN_PIECES = [(0, 0), (0, 128), (1, 256), (2, 384)]
UNITS = [(0, 0, 4), (0, 4, 4), (0, 8, 4), (0, 12, 4), (1, 0, 4), (1, 4, 4), (1, 8, 4), (1, 12, 2), (1, 14, 1), (1, 15, 1)]
SHORT_SHARE = 288
HALF = RUN // 2
LAP = 32
RAW, SECOND = HALF, 2 * RUN + HALF + LAP
WOVEN1 = SECOND + 2 * RUN - LAP
TWINS0 = WOVEN1 + 2 * RUN - LAP
ROOM = TWINS0 + 4 * RUN
SPARE_SHARE = 64
BANK_OF = {(0, 0): 2, (1, 0): 3, (0, 4): 4, (1, 4): 0, (0, 8): 5, (1, 8): 1, (0, 12): 6, (0, 14): 7, (0, 15): 4, (1, 12): 2}
FLOPS = 2 * M * K * T + 2 * K * N * S


def tile_moe_prv_lin_relu2_kernel(
    tc, uT, wu, w_words, w_scales, b, gate, offs, pos1, pos2, pos3, pos4, out
):
    nc = tc.nc
    with ExitStack() as ctx:
        keep = ctx.enter_context(tc.tile_pool(name="keep", bufs=1))
        psum = ctx.enter_context(tc.psum_pool(name="psum", bufs=1))
        banks = [psum.tile([P, 512], F32, name="bank%d" % i) for i in range(8)]

        offs_t = keep.tile([P, S // 16], U16, name="offs_t")
        pos_t = [keep.tile([P, T // 16], U16, name="pos_t%d" % r) for r in range(TOP)]

        room = keep.tile([P, ROOM], BF16, name="room", align_bytes=64)
        windows = {}
        for a, u in ((0, 0), (1, 0), (1, 1)):
            windows[a, u] = keep.tile([P, 2 * WINDOW], BF16, name="win%d%d" % (a, u), align_bytes=64)[:]
            nc.vector.memset(windows[a, u][:, 2 * T :].bitcast(U32), 0)
        singles = keep.tile([P, 2, WINDOW], BF16, name="singles", align_bytes=64)
        nc.vector.memset(singles[:, :, T:].bitcast(U32), 0)
        w_plane = keep.tile([P, E * PASSES * N], U8, name="w_plane", align_bytes=64)
        nc.vector.memset(w_plane[:].bitcast(I32), 0)
        ident = keep.tile([P, P], F32, name="ident")
        make_identity(nc, ident[:])

        wu_rows = wu.rearrange("(p j) k -> p j k", j=4)
        uT_rows = uT.rearrange("(p j) t -> p j t", j=4)
        first_raw = keep.tile([P, 4, 512], F32, name="first_raw", align_bytes=64)
        early_raw = keep.tile([P, 4, 256], F32, name="early_raw", align_bytes=64)
        second_raw = [early_raw[:], room[:, RAW : RAW + 2 * RUN].bitcast(F32).rearrange("p (j x) -> p j x", j=4)]
        u_raw = {}
        nc.sync.dma_start(first_raw[:], wu_rows[:, :, :512])
        for s, (t0, nt) in enumerate(TOKEN_LOADS):
            u_raw[s] = keep.tile([P, 4, nt], F32, name="u_raw%d" % s)
            nc.sync.dma_start(u_raw[s][:], uT_rows[:, :, t0 : t0 + nt])
        nc.sync.dma_start(offs_t[:], offs)
        for s in range(2):
            nc.sync.dma_start(second_raw[s], wu_rows[:, :, 512 + 256 * s : 512 + 256 * (s + 1)])
        scale_rows = w_scales.rearrange("e a q n -> q (e a) n")
        for q in range(4):
            nc.sync.dma_start(
                w_plane[32 * q : 32 * q + 4, :].bitcast(I32).rearrange("p (g n) -> p g n", g=E * PASSES),
                scale_rows[4 * q : 4 * q + 4].bitcast(I32),
            )
        bias = keep.tile([P, HALVES, E], F32, name="bias")
        nc.sync.dma_start(bias[:], b.rearrange("(h p) e -> p h e", p=P))
        w_codes = []
        for g in range(E // 2):
            two_experts = keep.tile([P, 2 * PASSES * N * 4], U8, name="w_codes%d" % g, align_bytes=64)
            nc.sync.dma_start(
                two_experts[:].bitcast(I32).rearrange("p (g n) -> p g n", g=2 * PASSES),
                w_words[2 * g : 2 * g + 2].rearrange("e a p n r -> p (e a) (n r)").bitcast(I32),
            )
            w_codes.append(two_experts)
        for r, pos in enumerate((pos1, pos2, pos3, pos4)):
            nc.sync.dma_start(pos_t[r][:], pos)
        gate_t = [keep.tile([P, T], F32, name="gate%d" % r) for r in range(TOP)]
        for r in range(TOP):
            nc.sync.dma_start(gate_t[r][:], gate[r, :P, :])
        gate_col = keep.tile([P, T // P], F32, name="gate_col")
        with nc.allow_non_contiguous_dma(reason="one weight a partition and block of tokens"):
            nc.sync.dma_start(gate_col[:], gate[TOP - 1, 0, :].rearrange("(g p) -> p g", p=P))

        wu_codes, wu_plane = {}, {}
        first_bf = keep.tile([P, 2 * RUN], BF16, name="first_bf", align_bytes=64)
        both_bf = [first_bf[:], room[:, SECOND : SECOND + 2 * RUN]]
        wu_bf = {(a, u): both_bf[a][:, RUN * u : RUN * (u + 1)] for a in range(PASSES) for u in range(2)}

        def cast_wu(a, u, copy):
            copy(
                wu_bf[a, u].rearrange("p (i m j) -> p m i j", i=2, j=4),
                first_raw[:].rearrange("p j (m t) -> p m t j", t=4)[:, :, 2 * u : 2 * u + 2, :],
            )

        def gpsimd_cast(dst, src):
            nc.gpsimd.tensor_scalar(dst, src, 1.0, 0.0, ALU.mult, ALU.add)

        def quantize_wu(a, pairs):
            n = 2 * P * len(pairs)
            codes = keep.tile([P, n], U32, name="wu_codes%d%d" % (a, pairs[0]), align_bytes=64)
            plane = keep.tile([P, n], U8, name="wu_plane%d%d" % (a, pairs[0]), align_bytes=64)
            nc.vector.quantize_mx(codes[:].bitcast(FP8X4), plane[:], both_bf[a][:, RUN * pairs[0] : RUN * (pairs[-1] + 1)])
            for k, u in enumerate(pairs):
                wu_codes[a, u] = codes[:, 2 * P * k : 2 * P * (k + 1)]
                wu_plane[a, u] = plane[:, 2 * P * k : 2 * P * (k + 1)]

        u_codes = keep.tile([P, T], U32, name="u_codes", align_bytes=64)
        u_plane = keep.tile([P, T], U8, name="u_plane", align_bytes=64)
        u_bf = [keep.tile([P, 4 * P], BF16, name="u_bf%d" % t0, align_bytes=64) for load, t0 in TOKEN_PIECES]

        def cast_u(s, copy):
            load, t0 = TOKEN_PIECES[s]
            c0 = t0 - TOKEN_LOADS[load][0]
            copy(u_bf[s][:].rearrange("p (c j) -> p c j", j=4), u_raw[load][:, :, c0 : c0 + P].rearrange("p j c -> p c j"))

        def quantize_u(s):
            t0 = TOKEN_PIECES[s][1]
            nc.vector.quantize_mx(u_codes[:, t0 : t0 + P].bitcast(FP8X4), u_plane[:, t0 : t0 + P], u_bf[s][:])

        def project(a, u, t0, nt, bank):
            both = banks[bank][:, : 2 * nt].rearrange("p (i t) -> p i t", i=2)
            for i in range(2):
                cols = slice(P * i, P * (i + 1))
                nc.tensor.matmul_mx(
                    both[:, i, :],
                    lhsT=wu_codes[a, u][:, cols].bitcast(FP8X4),
                    lhsT_scale=wu_plane[a, u][:, cols],
                    rhs=u_codes[:, t0 : t0 + nt].bitcast(FP8X4),
                    rhs_scale=u_plane[:, t0 : t0 + nt],
                    start=True,
                    stop=True,
                )

        def fill_window(a, u, t0, nt, bank, copy):
            copy(
                windows[a, u][:, 2 * t0 : 2 * (t0 + nt)].rearrange("p (t i) -> p t i", i=2),
                banks[bank][:, : 2 * nt].rearrange("p (i t) -> p t i", i=2),
            )

        cast_wu(0, 0, nc.vector.tensor_copy)
        cast_wu(0, 1, nc.scalar.copy)
        quantize_wu(0, (0,))
        cast_u(0, nc.scalar.copy)
        cast_u(1, nc.vector.tensor_copy)
        quantize_u(0)
        cast_u(2, nc.scalar.copy)
        quantize_u(1)
        cast_u(3, nc.scalar.copy)
        quantize_u(2)
        quantize_wu(0, (1,))
        quantize_u(3)
        for s in range(T // P):
            project(0, 0, P * s, P, s)
            fill_window(0, 0, P * s, P, s, nc.scalar.copy if s % 2 else nc.vector.tensor_copy)
        for s in range(2):
            project(0, 1, TH * s, TH, 4 + s)
            nc.scalar.copy(singles[:, :, TH * s : TH * (s + 1)], banks[4 + s][:].rearrange("p (i t) -> p i t", i=2))

        x_codes, x_plane = {}, {}
        y = [keep.tile([P, S], F32, name="y%d" % h, align_bytes=64) for h in range(HALVES)]
        late = keep.tile([P, 12 * C], F32, name="late")
        even = keep.tile([P, 2 * RUN + HALF], BF16, name="even", align_bytes=64)
        odd = keep.tile([P, 2 * RUN], BF16, name="odd", align_bytes=64)
        runs = [
            (even, 0, RUN),
            (odd, 0, RUN),
            (room, 0, SECOND - LAP),
            (room, RUN, SECOND + RUN - LAP),
            (even, 0, RUN),
            (odd, 0, RUN),
            (even, 0, RUN),
            (odd, 0, HALF),
            (even, HALF, RUN + HALF),
        ]
        lapped = keep.tile([P, 7 * RUN - 2 * LAP], BF16, name="lapped", align_bytes=64)
        twins = [room[:, TWINS0:], lapped[:, 2 * RUN - LAP : 6 * RUN - LAP]]
        spare = keep.tile([P, 2 * RUN - LAP], BF16, name="spare", align_bytes=64)
        woven = [
            both_bf[1],
            room[:, WOVEN1 : WOVEN1 + 2 * RUN],
            twins[0][:, : 2 * RUN],
            twins[1][:, : 2 * RUN],
            lapped[:, : 2 * RUN],
            twins[0][:, 2 * RUN :],
            twins[1][:, 2 * RUN :],
            spare[:, RUN - LAP :],
            y[0][:, 8 * C : 10 * C].bitcast(BF16),
            odd[:, :HALF],
        ]

        def slots_of(s0, ns):
            return offs_t[:, s0 // 16 : (s0 + ns) // 16]

        def gather(i, pairs=(0, 1), s0=0, ns=None):
            a, e0, ne = UNITS[i]
            ns = ns or ne * C
            for u in pairs:
                at = runs[i][1 + u] + 2 * s0
                nc.vector.tensor_copy(
                    runs[i][0][:, at : at + 2 * ns].bitcast(U32),
                    windows[a, u].bitcast(U32).indirect(slots_of(e0 * C + s0, ns)),
                )

        def gather_woven(i):
            a, e0, ne = UNITS[i]
            words = woven[i].bitcast(U32).rearrange("p (c u) -> p u c", u=2)
            for u in range(2):
                nc.vector.tensor_copy(words[:, u, :], windows[a, u].bitcast(U32).indirect(slots_of(e0 * C, ne * C)))

        def gather_singles(i):
            a, e0, ne = UNITS[i]
            at = runs[i][2]
            pairs = runs[i][0][:, at : at + 2 * ne * C].rearrange("p (c i) -> p c i", i=2)
            for k in range(2):
                nc.scalar.activation(pairs[:, :, k], singles[:, k, :].indirect(slots_of(e0 * C, ne * C)), ACT.Copy)

        def weave(i, copy, s0, ns):
            tile, first, second = runs[i]
            copy(
                woven[i][:, 4 * s0 : 4 * (s0 + ns)].bitcast(U32).rearrange("p (c u) -> p c u", u=2),
                tile[:, first : 2 * second - first].bitcast(U32).rearrange("p (u x) -> p x u", u=2)[:, s0 : s0 + ns, :],
            )

        def quantize_x(units, source):
            n = sum(UNITS[i][2] for i in units) * C
            codes = keep.tile([P, n], U32, name="x_codes%d" % units[0], align_bytes=64)
            plane = keep.tile([P, n], U8, name="x_plane%d" % units[0], align_bytes=64)
            nc.vector.quantize_mx(codes[:].bitcast(FP8X4), plane[:], source)
            for k, i in enumerate(units):
                cols = slice(n // len(units) * k, n // len(units) * (k + 1))
                x_codes[i], x_plane[i] = codes[:, cols], plane[:, cols]

        unit_of = {(a, e): i for i, (a, e0, ne) in enumerate(UNITS) for e in range(e0, e0 + ne)}

        def multiply(h, e0, ne):
            for e in range(e0, e0 + ne):
                for a in range(PASSES):
                    i = unit_of[a, e]
                    own = slice(C * (e - UNITS[i][1]), C * (e - UNITS[i][1] + 1))
                    word0 = ((e % 2) * PASSES + a) * N + h * P
                    byte0 = (e * PASSES + a) * N + h * P
                    nc.tensor.matmul_mx(
                        banks[BANK_OF[h, e0]][:, C * (e - e0) : C * (e - e0 + 1)],
                        lhsT=w_codes[e // 2][:, 4 * word0 : 4 * (word0 + P)].bitcast(FP8X4),
                        lhsT_scale=w_plane[:, byte0 : byte0 + P],
                        rhs=x_codes[i][:, own].bitcast(FP8X4),
                        rhs_scale=x_plane[i][:, own],
                        start=(a == 0),
                        stop=(a == PASSES - 1),
                    )

        def rectify(h, group, e0, ne, positive):
            for e in range(e0, e0 + ne):
                nc.scalar.activation(
                    positive[:, C * (e - e0) : C * (e - e0 + 1)],
                    banks[BANK_OF[h, group]][:, C * (e - group) : C * (e - group + 1)],
                    ACT.Relu,
                    bias=bias[:, h, e : e + 1],
                )

        def square(h, e0, ne, positive):
            nc.scalar.activation(y[h][:, e0 * C : (e0 + ne) * C], positive, ACT.Square)

        gp = nc.gpsimd.tensor_copy
        W = 4 * C
        gather(0, (0,))
        gather(1, (0,))
        gather(2, (0,), 0, W // 2)
        gather_singles(0)
        gather_singles(1)
        for s in range(2):
            gpsimd_cast(
                both_bf[1].rearrange("p (t m j) -> p m t j", t=4, j=4)[:, P // 2 * s : P // 2 * (s + 1)],
                second_raw[s].rearrange("p j (m t) -> p m t j", t=4),
            )
        quantize_wu(1, (0, 1))
        gather(2, (0,), W // 2, W // 2)
        gather(3, (0,))
        for s in range(2):
            project(1, 0, TH * s, TH, 6 + s)
            fill_window(1, 0, TH * s, TH, 6 + s, nc.scalar.copy if s else nc.vector.tensor_copy)
        for s in range(2):
            project(1, 1, TH * s, TH, s)
            fill_window(1, 1, TH * s, TH, s, nc.scalar.copy)
        weave(0, gp, 0, W)
        quantize_x((0,), woven[0])
        weave(1, gp, 0, W)
        gather(4)
        gather_singles(2)
        quantize_x((1,), woven[1])
        weave(4, gp, 0, W)
        weave(2, gp, 0, SPARE_SHARE)
        gather(5)
        gather_singles(3)
        quantize_x((4,), woven[4])
        weave(5, gp, 0, W)
        weave(3, gp, 0, SPARE_SHARE)
        gather(6)
        weave(2, nc.scalar.copy, SPARE_SHARE, W - SPARE_SHARE)
        weave(3, nc.scalar.copy, SPARE_SHARE, W - SPARE_SHARE)
        quantize_x((2, 5), twins[0])
        relus = [lapped[:, 6 * RUN - 2 * LAP :].bitcast(F32), spare[:, :RUN].bitcast(F32)]
        for h in range(HALVES):
            multiply(h, 0, 4)
        rectify(0, 0, 0, 4, relus[0])
        square(0, 0, 4, relus[0])
        weave(6, gp, 0, SHORT_SHARE)
        weave(6, nc.scalar.copy, SHORT_SHARE, W - SHORT_SHARE)
        rectify(1, 0, 0, 4, relus[1])
        square(1, 0, 4, relus[1])
        gather(7)
        quantize_x((3, 6), twins[1])
        weave(7, gp, C, C)
        weave(7, nc.scalar.copy, 0, C)
        gather(8)
        others = keep.tile([P, 11 * C], F32, name="others")
        multiply(0, 4, 4)
        multiply(1, 4, 4)
        multiply(0, 8, 4)
        rectify(0, 4, 4, 4, others[:, :W])
        square(0, 4, 4, others[:, :W])
        rectify(0, 8, 8, 4, others[:, W : 2 * W])
        quantize_x((7,), woven[7])
        weave(8, gp, 0, C)
        gather_woven(9)
        quantize_x((8,), woven[8])
        quantize_x((9,), woven[9])
        multiply(0, 12, 2)
        rectify(0, 12, 12, 2, others[:, 2 * W : 10 * C])
        multiply(0, 14, 1)
        rectify(0, 14, 14, 1, others[:, 10 * C :])
        multiply(0, 15, 1)
        multiply(1, 8, 4)
        multiply(1, 12, 4)
        spread = late[:].rearrange("p (g c) -> p g c", g=16)[:, :, :8]
        nc.scalar.activation(
            spread, banks[BANK_OF[0, 15]][:, :C].rearrange("p (g c) -> p g c", g=16), ACT.Relu, bias=bias[:, 0, 15:16]
        )
        for e0, e1 in ((8, 12), (12, 15)):
            positive = others[:, (e0 - 4) * C : (e1 - 4) * C]
            nc.vector.tensor_tensor(y[0][:, e0 * C : e1 * C], positive, positive, ALU.mult)
        nc.scalar.activation(y[0][:, 15 * C :].rearrange("p (g c) -> p g c", g=16), spread, ACT.Square)
        for e0 in (4, 8, 12):
            positive = late[:, C * (e0 - 4) : C * e0]
            rectify(1, e0, e0, 4, positive)
            square(1, e0, 4, positive)

        def fetch(h, r, cols):
            prod = keep.tile([P, cols.stop - cols.start], F32, name="prod%d%d_%d" % (h, r, cols.start))
            nc.vector.tensor_tensor(
                prod[:], y[h][:].indirect(pos_t[r][:, cols.start // 16 : cols.stop // 16]), gate_t[r][:, cols], ALU.mult
            )
            return prod

        turned = [banks[4 + blk][:, :P] for blk in range(T // P)]

        def add_turned(prod, blk0, start, stop):
            for i in range(prod.shape[1] // P):
                nc.tensor.matmul(
                    turned[blk0 + i],
                    lhsT=prod[:, P * i : P * (i + 1)],
                    rhs=ident[:],
                    start=start,
                    stop=stop,
                    is_transpose=True,
                )

        def turn_back(blocks, summed, bank, beside=None):
            back = banks[bank][:, : len(blocks) * P]
            for i, block in enumerate(blocks):
                cols = slice(P * i, P * (i + 1))
                nc.scalar.copy(summed[:, cols], block)
                if beside is not None:
                    nc.tensor.matmul(back[:, cols], lhsT=beside[:, cols], rhs=ident[:], start=True, stop=False, is_transpose=True)
                nc.tensor.matmul(
                    back[:, cols], lhsT=summed[:, cols], rhs=ident[:], start=beside is None, stop=True, is_transpose=True
                )
            return back

        whole = slice(0, T)
        for r in range(TOP):
            add_turned(fetch(0, r, whole), 0, r == 0, r == TOP - 1)
        plain = keep.tile([P, T], F32, name="plain")
        weighted = keep.tile([P, T], F32, name="weighted")
        nc.scalar.activation(plain[:], y[1][:].indirect(pos_t[TOP - 1][:]), ACT.Copy)
        for blk in range(T // P):
            cols = slice(P * blk, P * (blk + 1))
            nc.tensor.transpose(banks[2][:, cols], plain[:, cols], ident[:])
        back = turn_back(turned, late[:, 8 * C :], 3)
        for blk in range(T // P):
            cols = slice(P * blk, P * (blk + 1))
            nc.scalar.activation(weighted[:, cols], banks[2][:, cols], ACT.Copy, scale=gate_col[:, blk : blk + 1])
        result = keep.tile([P, T], F32, name="result0")
        nc.scalar.copy(result[:], back)
        nc.sync.dma_start(out[:P, :], result[:])

        add_turned(fetch(1, 0, whole), 0, True, False)
        pieces = [slice(0, TH), slice(TH, TH + P), slice(TH + P, T)]
        partial = []
        for s, cols in enumerate(pieces):
            add_turned(fetch(1, 1, cols), cols.start // P, False, True)
        for s, cols in enumerate(pieces):
            partial.append(turn_back(turned[cols.start // P : cols.stop // P], late[:, cols], s, weighted[:, cols]))
        last = [fetch(1, 2, slice(TH * s, TH * (s + 1))) for s in range(2)]
        for s, cols in enumerate(pieces):
            result = keep.tile([P, cols.stop - cols.start], F32, name="result1%d" % s)
            own = slice(cols.start % TH, cols.start % TH + cols.stop - cols.start)
            nc.vector.tensor_tensor(result[:], partial[s], last[cols.start // TH][:, own], ALU.add)
            nc.sync.dma_start(out[P:, cols], result[:])
